import numpy as np
import ml_dtypes


def mxq(x, axis, fmt="e4m3"):
    dtype, down = {"e4m3": (ml_dtypes.float8_e4m3fn, 7), "e5m2": (ml_dtypes.float8_e5m2, 14)}[fmt]
    v = np.moveaxis(np.asarray(x, np.float32).astype(ml_dtypes.bfloat16).astype(np.float64), axis, -1)
    blocks = v.reshape(v.shape[:-1] + (-1, 32))
    amax = np.abs(blocks).max(-1, keepdims=True)
    byte = np.maximum(np.where(amax > 0, np.frexp(amax)[1] - 1 + 127, 0) - down, 1)
    scale = np.exp2(byte - 127.0)
    codes = (blocks / scale).astype(np.float32).astype(dtype).astype(np.float64)
    return np.moveaxis((codes * scale).reshape(v.shape), -1, axis)


WIDE = False


def mx_kscale(k):
    if not WIDE:
        return np.ones(k)
    levels = np.array([24, -24, 12, -12, 0])
    if k % 512:
        return np.exp2(np.random.permutation(np.resize(levels, k // 32))).repeat(32)
    a = np.empty((k // 512, 16))
    for p in range(k // 512):
        a[p, :8] = np.random.permutation(np.resize(levels, 8))
        for g in range(8):
            far = levels[np.abs(levels - a[p, g]) >= 10]
            a[p, g + 8] = far[np.random.randint(len(far))]
    return np.exp2(a.ravel()).repeat(32)


def f64(x):
    return np.asarray(x).astype(np.float64)


def striped(idx):
    return np.tile(idx.reshape(-1, 16).T, (8, 1)).astype(np.uint16)


def unstriped(offs):
    return offs[:16].T.reshape(-1).astype(np.int64)


E2M1 = np.array([0.0, 0.5, 1.0, 1.5, 2.0, 3.0, 4.0, 6.0, -0.0, -0.5, -1.0, -1.5, -2.0, -3.0, -4.0, -6.0])


def pack_weight(w, fmt):
    k, n = w.shape
    w = f64(np.asarray(w, np.float32).astype(ml_dtypes.bfloat16)).reshape(k // 32, 32, n)
    amax = np.abs(w).max(1)
    if fmt == "e4m3":
        byte = np.frexp(amax)[1] - 1 + 127 - 7
    else:
        mant, ex = np.frexp(amax / 6.0)
        byte = np.where(mant > 0.5, ex, ex - 1) + 127
    byte = np.clip(np.where(amax > 0, byte, 1), 1, 254)
    scaled = (w * np.exp2(127.0 - byte)[:, None, :]).reshape(k, n).astype(np.float32)
    by_word = np.ascontiguousarray(scaled.reshape(k // 512, 128, 4, n).transpose(0, 1, 3, 2))
    if fmt == "e4m3":
        words = by_word.astype(ml_dtypes.float8_e4m3fn).view(np.uint8)
    else:
        c = by_word.astype(ml_dtypes.float4_e2m1fn).view(np.uint8) & 0xF
        words = (c[..., 0::2] | (c[..., 1::2] << 4)).reshape(k // 512, 128, 2 * n)
    return np.ascontiguousarray(words), np.ascontiguousarray(byte.astype(np.uint8).reshape(k // 512, 16, n))


def unpack_weight(words, scales, fmt):
    g, _, n = scales.shape
    words = np.ascontiguousarray(words).reshape(g, 128, n, -1)
    if fmt == "e4m3":
        vals = words.view(ml_dtypes.float8_e4m3fn).astype(np.float64)
    else:
        nib = np.empty((g, 128, n, 4), np.uint8)
        nib[..., 0::2] = words & 0xF
        nib[..., 1::2] = words >> 4
        vals = E2M1[nib]
    vals = vals * np.repeat(np.exp2(scales.astype(np.float64) - 127.0), 8, axis=1)[..., None]
    return vals.transpose(0, 1, 3, 2).reshape(g * 512, n)


def pack_table4(v):
    words, scales = pack_weight(v, "e2m1")
    g, t = words.shape[0] // 2, v.shape[1]
    return np.ascontiguousarray(words.reshape(g, 2, 128, t, 2).transpose(0, 2, 3, 1, 4).reshape(g, 128, t, 4)), scales


def unpack_table4(words, scales):
    g, _, t, _ = words.shape
    return unpack_weight(words.reshape(g, 128, t, 2, 2).transpose(0, 3, 1, 2, 4).reshape(2 * g, 128, 2 * t), scales, "e2m1")


def sigm(f):
    return 1.0 / (1.0 + np.exp(-np.maximum(f, -700.0)))


K, L, R, N, T, J = 512, 1024, 1024, 256, 2048, 1024


def setup_inputs():
    n = np.random.standard_normal
    s = mx_kscale(K)[:, None]
    s2 = mx_kscale(L)[:, None]
    u = mx_kscale(R)[:, None]
    p_tab = pack_weight(n((K, T)) * s, "e4m3")
    p_tab2 = pack_table4(n((L, T)) * s2)
    p_wa = pack_weight(n((K, R)) / np.sqrt(K) / s * u.T, "e4m3")
    return {
        "tab_words": p_tab[0],
        "tab_scales": p_tab[1],
        "tab2_words": p_tab2[0],
        "tab2_scales": p_tab2[1],
        "wa_words": p_wa[0],
        "wa_scales": p_wa[1],
        "wb": (n((L, R)) / np.sqrt(L) / s2 * u.T).astype(np.float32),
        "en": (n((R, N)) / np.sqrt(R) / u).astype(np.float32),
        "offs": striped(np.random.permutation(T)[:J]),
        "offs2": striped(np.random.permutation(T)[:J]),
    }


def reference(tab_words, tab_scales, tab2_words, tab2_scales, wa_words, wa_scales, wb, en, offs, offs2):
    idx = unstriped(offs)
    idx2 = unstriped(offs2)
    tab_ = unpack_weight(tab_words, tab_scales, "e4m3")[:, idx]
    tab2_ = unpack_table4(tab2_words, tab2_scales)[:, idx2]
    wa_ = unpack_weight(wa_words, wa_scales, "e4m3")
    wb_ = mxq(f64(wb), 0, "e4m3")
    ha = wa_.T @ tab_
    hb = wb_.T @ tab2_
    h = np.maximum(ha, hb)
    h_ = mxq(h, 0, "e4m3")
    en_ = mxq(f64(en), 0, "e4m3")
    y = en_.T @ h_
    return sigm(y)

@@ -1,0 +1,267 @@
+from contextlib import ExitStack
+
+import concourse.mybir as mybir
+
+K, L, R, N, T, J = 512, 1024, 1024, 256, 2048, 1024
+FLOPS = 2 * (K * R * J + L * R * J + R * N * J)
+
+F32 = mybir.dt.float32
+BF16 = mybir.dt.bfloat16
+I32 = mybir.dt.int32
+U32 = mybir.dt.uint32
+U16 = mybir.dt.uint16
+U8 = mybir.dt.uint8
+FP8X4 = mybir.dt.float8_e4m3fn_x4
+FP4X4 = mybir.dt.float4_e2m1fn_x4
+MULT, ADD, MAX = mybir.AluOpType.mult, mybir.AluOpType.add, mybir.AluOpType.max
+
+P = 128
+PACK = 4
+K_PASS = P * PACK
+HALF = J // 2
+CHUNK = 128
+CHUNKS = J // CHUNK
+SECOND_RUNS = (2, 2, 2, 1, 1)
+
+
+def tile_list_kg_max_sig_kernel(
+    tc, tab_words, tab_scales, tab2_words, tab2_scales, wa_words, wa_scales, wb, en, offs, offs2, out
+):
+    nc = tc.nc
+    with ExitStack() as ctx:
+        keep = ctx.enter_context(tc.tile_pool(name="keep", bufs=1))
+        stage = ctx.enter_context(tc.tile_pool(name="stage", bufs=4))
+        ring = ctx.enter_context(tc.tile_pool(name="ring", bufs=3))
+        psum_a = ctx.enter_context(tc.psum_pool(name="psum_a", bufs=3))
+        psum_b = ctx.enter_context(tc.psum_pool(name="psum_b", bufs=3))
+        psum_y = ctx.enter_context(tc.psum_pool(name="psum_y", bufs=2))
+
+        list1 = keep.tile([P, J // 16], U16, name="list1")
+        list2 = keep.tile([P, J // 16], U16, name="list2")
+        tab_s = keep.tile([P, T], U8, name="tab_s")
+        tab2_s = keep.tile([P, T], U8, name="tab2_s")
+        wa_s_raw = keep.tile([P, R], U8, name="wa_s_raw")
+        tab_w = keep.tile([P, T], I32, name="tab_w")
+        tab2_w = keep.tile([P, T], I32, name="tab2_w")
+        wa_w_raw = keep.tile([P, R], I32, name="wa_w_raw")
+        g_s = keep.tile([P, J], U8, name="g_s", align_bytes=64)
+        g2_s = keep.tile([P, J], U8, name="g2_s", align_bytes=64)
+        g2_s1 = keep.tile([P, J], U8, name="g2_s1", align_bytes=64)
+        wa_w = keep.tile([P, R], I32, name="wa_w", align_bytes=64)
+        wa_s = keep.tile([P, R], U8, name="wa_s", align_bytes=64)
+
+        nc.vector.memset(tab_s[:].bitcast(I32), 0)
+        nc.vector.memset(tab2_s[:].bitcast(I32), 0)
+        nc.gpsimd.memset(wa_s_raw[:].bitcast(I32), 0)
+        nc.gpsimd.memset(g2_s1[:].bitcast(I32), 0)
+
+        def load_scale_rows(plane, scales):
+            rows = 4 * scales.shape[0]
+            for q in range(4):
+                nc.sync.dma_start(
+                    out=plane[32 * q : 32 * q + rows, :].bitcast(I32),
+                    in_=scales[:, 4 * q : 4 * q + 4, :].bitcast(I32),
+                )
+
+        def load_words(words, packed):
+            nc.sync.dma_start(out=words[:], in_=packed[0].rearrange("p c i -> p (c i)").bitcast(I32))
+
+        wb_raw = {}
+
+        def load_wb(a, b):
+            wb_raw[a, b] = stage.tile([P, PACK, K_PASS], F32, name="wb_raw", tag="raw")
+            rows = wb[a * K_PASS : (a + 1) * K_PASS, b * K_PASS : (b + 1) * K_PASS]
+            nc.sync.dma_start(out=wb_raw[a, b][:], in_=rows.rearrange("(p i) r -> p i r", i=PACK))
+
+        nc.sync.dma_start(list1[:], offs)
+        nc.sync.dma_start(list2[:], offs2)
+        load_words(wa_w_raw, wa_words)
+        load_scale_rows(tab_s, tab_scales)
+        load_words(tab_w, tab_words)
+        load_scale_rows(wa_s_raw, wa_scales)
+        load_wb(0, 0)
+        load_scale_rows(tab2_s, tab2_scales)
+        load_words(tab2_w, tab2_words)
+        load_wb(1, 0)
+        load_wb(0, 1)
+        load_wb(1, 1)
+        en_raw = stage.tile([P, 2, PACK, N], F32, name="en_raw", tag="raw")
+        en_rows = en.rearrange("(b g t e) n -> b t g e n", b=2, t=PACK, e=8)
+        for b in range(2):
+            for t in range(PACK):
+                nc.sync.dma_start(out=en_raw[:, b, t, :], in_=en_rows[b, t])
+
+        nc.gpsimd.tensor_copy(
+            out=wa_w[:].rearrange("p (t g e) -> p t g e", t=PACK, e=8),
+            in_=wa_w_raw[:].rearrange("p (g t e) -> p t g e", t=PACK, e=8),
+        )
+        nc.gpsimd.tensor_copy(
+            out=wa_s[:].bitcast(I32).rearrange("p (t g e) -> p t g e", t=PACK, e=2),
+            in_=wa_s_raw[:].bitcast(I32).rearrange("p (g t e) -> p t g e", t=PACK, e=2),
+        )
+
+        def half_of(entries, h):
+            return entries[:, h * HALF // 16 : (h + 1) * HALF // 16]
+
+        nc.vector.tensor_copy(g_s[:], tab_s[:].indirect(list1[:]))
+        g_w = []
+        for h in range(2):
+            picked = keep.tile([P, HALF], U32, name="g_w%d" % h, align_bytes=64)
+            nc.vector.tensor_copy(picked[:], tab_w[:].bitcast(U32).indirect(half_of(list1, h)))
+            g_w.append(picked)
+        nc.vector.tensor_copy(g2_s[:], tab2_s[:].indirect(list2[:]))
+        g2_planes = (g2_s, g2_s1)
+
+        wb_bf, wb_w, wb_s = {}, {}, {}
+
+        def round_wb(a, b, on_scalar):
+            wb_bf[a, b] = ring.tile([P, PACK * K_PASS], BF16, name="wb_bf", tag="wb_bf", align_bytes=64)
+            src = wb_raw[a, b][:].rearrange("p i (g t c e) -> p t g c i e", t=PACK, c=2, e=4)
+            dst = wb_bf[a, b][:].rearrange("p (t g c e i) -> p t g c i e", t=PACK, c=2, e=4, i=PACK)
+            for t in range(on_scalar):
+                nc.scalar.copy(out=dst[:, t], in_=src[:, t])
+            src = wb_raw[a, b][:].rearrange("p i (g t e) -> p t g e i", t=PACK, e=8)
+            dst = wb_bf[a, b][:].rearrange("p (t g e i) -> p t g e i", t=PACK, e=8, i=PACK)
+            for t in range(on_scalar, PACK):
+                nc.gpsimd.tensor_scalar(
+                    out=dst[:, t], in0=src[:, t], scalar1=1.0, scalar2=0.0, op0=MULT, op1=ADD
+                )
+
+        def quantize_wb(a, b):
+            wb_w[a, b] = keep.tile([P, K_PASS], U32, name="wb_w%d%d" % (a, b), align_bytes=64)
+            wb_s[a, b] = keep.tile([P, K_PASS], U8, name="wb_s%d%d" % (a, b), align_bytes=64)
+            nc.vector.quantize_mx(out=wb_w[a, b][:].bitcast(FP8X4), scales=wb_s[a, b][:], in_=wb_bf[a, b][:])
+
+        ha = {}
+
+        def make_ha(b, c):
+            h, j0 = divmod(c * CHUNK, HALF)
+            bank = psum_a.tile([P, PACK, CHUNK], F32, name="bank_a")
+            for t in range(PACK):
+                cols = slice(t * 2 * P + b * P, t * 2 * P + (b + 1) * P)
+                nc.tensor.matmul_mx(
+                    out=bank[:, t, :],
+                    lhsT=wa_w[:, cols].bitcast(FP8X4),
+                    lhsT_scale=wa_s[:, cols],
+                    rhs=g_w[h][:, j0 : j0 + CHUNK].bitcast(FP8X4),
+                    rhs_scale=g_s[:, c * CHUNK : (c + 1) * CHUNK],
+                    start=True,
+                    stop=True,
+                )
+            ha[b, c] = keep.tile([P, CHUNK, PACK], F32, name="ha%d_%d" % (b, c))
+            nc.scalar.copy(out=ha[b, c][:], in_=bank[:].rearrange("p t j -> p j t"))
+
+        round_wb(0, 0, 0)
+        for c in range(CHUNKS):
+            make_ha(0, c)
+        for q in range(4):
+            nc.scalar.dma_start(
+                out=g2_s1[32 * q : 32 * q + 4, :].bitcast(I32),
+                in_=g2_s[32 * q + 4 : 32 * q + 8, :].bitcast(I32),
+            )
+
+        g2_w = []
+        for h in range(2):
+            picked = keep.tile([P, HALF], U32, name="g2_pair%d" % h)
+            nc.vector.tensor_copy(picked[:], tab2_w[:].bitcast(U32).indirect(half_of(list2, h)))
+            if h == 0:
+                quantize_wb(0, 0)
+            parted = keep.tile([P, 2, 2 * HALF], U8, name="g2_w%d" % h, align_bytes=64)
+            nc.vector.tensor_copy(
+                out=parted[:].bitcast(U16),
+                in_=picked[:].bitcast(U16).rearrange("p (j d) -> p d j", d=2),
+            )
+            g2_w.append(parted)
+
+        round_wb(1, 0, 2)
+        quantize_wb(1, 0)
+
+        h_w = [keep.tile([P, J], U32, name="h_w%d" % b, align_bytes=64) for b in range(2)]
+        h_s = [keep.tile([P, J], U8, name="h_s%d" % b, align_bytes=64) for b in range(2)]
+
+        def make_h(b, c0, count):
+            h_bf = ring.tile([P, count * CHUNK * PACK], BF16, name="h_bf", tag="h_bf", align_bytes=64)
+            for s in range(count):
+                c = c0 + s
+                h, j0 = divmod(c * CHUNK, HALF)
+                bank = psum_b.tile([P, PACK, CHUNK], F32, name="bank_b")
+                for t in range(PACK):
+                    cols = slice(t * P, (t + 1) * P)
+                    for a in range(2):
+                        nc.tensor.matmul_mx(
+                            out=bank[:, t, :],
+                            lhsT=wb_w[a, b][:, cols].bitcast(FP8X4),
+                            lhsT_scale=wb_s[a, b][:, cols],
+                            rhs=g2_w[h][:, a, 2 * j0 : 2 * (j0 + CHUNK)].bitcast(FP4X4),
+                            rhs_scale=g2_planes[a][:, c * CHUNK : (c + 1) * CHUNK],
+                            start=(a == 0),
+                            stop=(a == 1),
+                        )
+                nc.vector.tensor_tensor(
+                    out=h_bf[:, s * CHUNK * PACK : (s + 1) * CHUNK * PACK].rearrange("p (j t) -> p j t", t=PACK),
+                    in0=bank[:].rearrange("p t j -> p j t"),
+                    in1=ha[b, c][:],
+                    op=MAX,
+                )
+            return h_bf
+
+        def quantize_h(b, c0, count, h_bf):
+            cols = slice(c0 * CHUNK, (c0 + count) * CHUNK)
+            nc.vector.quantize_mx(out=h_w[b][:, cols].bitcast(FP8X4), scales=h_s[b][:, cols], in_=h_bf[:])
+
+        en_bf = keep.tile([P, 2 * N * PACK], BF16, name="en_bf", align_bytes=64)
+        en_w = keep.tile([P, 2 * N], U32, name="en_w", align_bytes=64)
+        en_s = keep.tile([P, 2 * N], U8, name="en_s", align_bytes=64)
+
+        def score(c0, count):
+            queries = slice(c0 * CHUNK, (c0 + count) * CHUNK)
+            bank = psum_y.tile([P, N // P, count * CHUNK], F32, name="bank_y")
+            for m in range(N // P):
+                for b in range(2):
+                    cols = slice(b * N + m * P, b * N + (m + 1) * P)
+                    nc.tensor.matmul_mx(
+                        out=bank[:, m, :],
+                        lhsT=en_w[:, cols].bitcast(FP8X4),
+                        lhsT_scale=en_s[:, cols],
+                        rhs=h_w[b][:, queries].bitcast(FP8X4),
+                        rhs_scale=h_s[b][:, queries],
+                        start=(b == 0),
+                        stop=(b == 1),
+                    )
+            result = ring.tile([P, N // P, count * CHUNK], F32, name="result", tag="result")
+            nc.scalar.activation(out=result[:], in_=bank[:], func=mybir.ActivationFunctionType.Sigmoid)
+            nc.sync.dma_start(out=out[:, queries].rearrange("(m p) j -> p m j", p=P), in_=result[:])
+
+        first = make_h(0, 0, 4)
+        make_ha(1, 0)
+        round_wb(0, 1, PACK)
+        make_ha(1, 1)
+        round_wb(1, 1, PACK)
+        second = make_h(0, 4, 4)
+        quantize_wb(0, 1)
+        quantize_wb(1, 1)
+        quantize_h(0, 0, 4, first)
+        quantize_h(0, 4, 4, second)
+        for c in range(2, 5):
+            make_ha(1, c)
+        for b in range(2):
+            nc.scalar.copy(
+                out=en_bf[:, b * N * PACK : (b + 1) * N * PACK].rearrange("p (c e t) -> p c t e", e=4, t=PACK),
+                in_=en_raw[:, b].rearrange("p t (c e) -> p c t e", e=4),
+            )
+        for c in range(5, CHUNKS):
+            make_ha(1, c)
+
+        waiting = None
+        c0 = 0
+        for count in SECOND_RUNS:
+            h_bf = make_h(1, c0, count)
+            if waiting is None:
+                nc.vector.quantize_mx(out=en_w[:].bitcast(FP8X4), scales=en_s[:], in_=en_bf[:])
+            else:
+                quantize_h(1, *waiting)
+                score(waiting[0], waiting[1])
+            waiting = (c0, count, h_bf)
+            c0 += count
+        quantize_h(1, *waiting)
+        score(waiting[0], waiting[1])

@@ -30,37 +30,31 @@ def tile_list_kg_max_sig_kernel(
     nc = tc.nc
     with ExitStack() as ctx:
         keep = ctx.enter_context(tc.tile_pool(name="keep", bufs=1))
-        stage = ctx.enter_context(tc.tile_pool(name="stage", bufs=4))
         ring = ctx.enter_context(tc.tile_pool(name="ring", bufs=3))
         psum_a = ctx.enter_context(tc.psum_pool(name="psum_a", bufs=3))
-        psum_b = ctx.enter_context(tc.psum_pool(name="psum_b", bufs=3))
-        psum_y = ctx.enter_context(tc.psum_pool(name="psum_y", bufs=2))
+        psum_b = ctx.enter_context(tc.psum_pool(name="psum_b", bufs=5))
 
         list1 = keep.tile([P, J // 16], U16, name="list1")
         list2 = keep.tile([P, J // 16], U16, name="list2")
         tab_s = keep.tile([P, T], U8, name="tab_s")
-        tab2_s = keep.tile([P, T], U8, name="tab2_s")
+        tab2_s = keep.tile([P, 2 * T], U8, name="tab2_s")
         wa_s_raw = keep.tile([P, R], U8, name="wa_s_raw")
         tab_w = keep.tile([P, T], I32, name="tab_w")
         tab2_w = keep.tile([P, T], I32, name="tab2_w")
-        wa_w_raw = keep.tile([P, R], I32, name="wa_w_raw")
         g_s = keep.tile([P, J], U8, name="g_s", align_bytes=64)
-        g2_s = keep.tile([P, J], U8, name="g2_s", align_bytes=64)
-        g2_s1 = keep.tile([P, J], U8, name="g2_s1", align_bytes=64)
-        wa_w = keep.tile([P, R], I32, name="wa_w", align_bytes=64)
+        g2_s = [keep.tile([P, J], U8, name="g2_s%d" % a, align_bytes=64) for a in range(2)]
         wa_s = keep.tile([P, R], U8, name="wa_s", align_bytes=64)
 
         nc.vector.memset(tab_s[:].bitcast(I32), 0)
         nc.vector.memset(tab2_s[:].bitcast(I32), 0)
         nc.gpsimd.memset(wa_s_raw[:].bitcast(I32), 0)
-        nc.gpsimd.memset(g2_s1[:].bitcast(I32), 0)
 
-        def load_scale_rows(plane, scales):
-            rows = 4 * scales.shape[0]
+        def load_scale_rows(planes, scales):
+            passes = scales.shape[0]
             for q in range(4):
                 nc.sync.dma_start(
-                    out=plane[32 * q : 32 * q + rows, :].bitcast(I32),
-                    in_=scales[:, 4 * q : 4 * q + 4, :].bitcast(I32),
+                    out=planes[32 * q : 32 * q + 4, :].bitcast(I32).rearrange("r (a c) -> r a c", a=passes),
+                    in_=scales[:, 4 * q : 4 * q + 4, :].bitcast(I32).rearrange("a r c -> r a c"),
                 )
 
         def load_words(words, packed):
@@ -69,13 +63,23 @@ def tile_list_kg_max_sig_kernel(
         wb_raw = {}
 
         def load_wb(a, b):
-            wb_raw[a, b] = stage.tile([P, PACK, K_PASS], F32, name="wb_raw", tag="raw")
+            wb_raw[a, b] = keep.tile([P, PACK, K_PASS], F32, name="wb_raw%d%d" % (a, b))
             rows = wb[a * K_PASS : (a + 1) * K_PASS, b * K_PASS : (b + 1) * K_PASS]
             nc.sync.dma_start(out=wb_raw[a, b][:], in_=rows.rearrange("(p i) r -> p i r", i=PACK))
 
+        wa_rows = wa_words[0].rearrange("p c i -> p (c i)").bitcast(I32)
+        wa_w_raw = [keep.tile([P, K_PASS], I32, name="wa_w_raw%d" % b) for b in range(2)]
+        wa_w = [keep.tile([P, K_PASS], I32, name="wa_w%d" % b, align_bytes=64) for b in range(2)]
+
+        def order_wa(b):
+            nc.vector.tensor_copy(
+                out=wa_w[b][:].rearrange("p (t g e) -> p t g e", t=PACK, e=8),
+                in_=wa_w_raw[b][:].rearrange("p (g t e) -> p t g e", t=PACK, e=8),
+            )
+
         nc.sync.dma_start(list1[:], offs)
         nc.sync.dma_start(list2[:], offs2)
-        load_words(wa_w_raw, wa_words)
+        nc.sync.dma_start(out=wa_w_raw[0][:], in_=wa_rows[:, :K_PASS])
         load_scale_rows(tab_s, tab_scales)
         load_words(tab_w, tab_words)
         load_scale_rows(wa_s_raw, wa_scales)
@@ -83,49 +87,48 @@ def tile_list_kg_max_sig_kernel(
         load_scale_rows(tab2_s, tab2_scales)
         load_words(tab2_w, tab2_words)
         load_wb(1, 0)
+        nc.sync.dma_start(out=wa_w_raw[1][:], in_=wa_rows[:, K_PASS:])
         load_wb(0, 1)
         load_wb(1, 1)
-        en_raw = stage.tile([P, 2, PACK, N], F32, name="en_raw", tag="raw")
+        en_raw = keep.tile([P, 2, PACK, N], F32, name="en_raw")
         en_rows = en.rearrange("(b g t e) n -> b t g e n", b=2, t=PACK, e=8)
         for b in range(2):
             for t in range(PACK):
                 nc.sync.dma_start(out=en_raw[:, b, t, :], in_=en_rows[b, t])
 
-        nc.gpsimd.tensor_copy(
-            out=wa_w[:].rearrange("p (t g e) -> p t g e", t=PACK, e=8),
-            in_=wa_w_raw[:].rearrange("p (g t e) -> p t g e", t=PACK, e=8),
-        )
-        nc.gpsimd.tensor_copy(
-            out=wa_s[:].bitcast(I32).rearrange("p (t g e) -> p t g e", t=PACK, e=2),
-            in_=wa_s_raw[:].bitcast(I32).rearrange("p (g t e) -> p t g e", t=PACK, e=2),
-        )
+        order_wa(0)
 
         def half_of(entries, h):
             return entries[:, h * HALF // 16 : (h + 1) * HALF // 16]
 
         nc.vector.tensor_copy(g_s[:], tab_s[:].indirect(list1[:]))
+        nc.gpsimd.tensor_copy(
+            out=wa_s[:].bitcast(I32).rearrange("p (t g e) -> p t g e", t=PACK, e=2),
+            in_=wa_s_raw[:].bitcast(I32).rearrange("p (g t e) -> p t g e", t=PACK, e=2),
+        )
         g_w = []
         for h in range(2):
             picked = keep.tile([P, HALF], U32, name="g_w%d" % h, align_bytes=64)
             nc.vector.tensor_copy(picked[:], tab_w[:].bitcast(U32).indirect(half_of(list1, h)))
             g_w.append(picked)
-        nc.vector.tensor_copy(g2_s[:], tab2_s[:].indirect(list2[:]))
-        g2_planes = (g2_s, g2_s1)
+        for a in range(2):
+            nc.vector.tensor_copy(g2_s[a][:], tab2_s[:, a * T : (a + 1) * T].indirect(list2[:]))
 
         wb_bf, wb_w, wb_s = {}, {}, {}
 
-        def round_wb(a, b, on_scalar):
-            wb_bf[a, b] = ring.tile([P, PACK * K_PASS], BF16, name="wb_bf", tag="wb_bf", align_bytes=64)
-            src = wb_raw[a, b][:].rearrange("p i (g t c e) -> p t g c i e", t=PACK, c=2, e=4)
+        def round_wb_on_scalar(a, b):
+            wb_bf[a, b] = keep.tile([P, PACK * K_PASS], BF16, name="wb_bf%d%d" % (a, b), align_bytes=64)
             dst = wb_bf[a, b][:].rearrange("p (t g c e i) -> p t g c i e", t=PACK, c=2, e=4, i=PACK)
-            for t in range(on_scalar):
+            src = wb_raw[a, b][:].rearrange("p i (g t c e) -> p t g c i e", t=PACK, c=2, e=4)
+            for t in range(PACK):
                 nc.scalar.copy(out=dst[:, t], in_=src[:, t])
-            src = wb_raw[a, b][:].rearrange("p i (g t e) -> p t g e i", t=PACK, e=8)
+
+        def round_wb_on_gpsimd(a, b):
+            wb_bf[a, b] = keep.tile([P, PACK * K_PASS], BF16, name="wb_bf%d%d" % (a, b), align_bytes=64)
             dst = wb_bf[a, b][:].rearrange("p (t g e i) -> p t g e i", t=PACK, e=8, i=PACK)
-            for t in range(on_scalar, PACK):
-                nc.gpsimd.tensor_scalar(
-                    out=dst[:, t], in0=src[:, t], scalar1=1.0, scalar2=0.0, op0=MULT, op1=ADD
-                )
+            src = wb_raw[a, b][:].rearrange("p i (g t e) -> p t g e i", t=PACK, e=8)
+            for t in range(PACK):
+                nc.gpsimd.tensor_scalar(out=dst[:, t], in0=src[:, t], scalar1=1.0, scalar2=0.0, op0=MULT, op1=ADD)
 
         def quantize_wb(a, b):
             wb_w[a, b] = keep.tile([P, K_PASS], U32, name="wb_w%d%d" % (a, b), align_bytes=64)
@@ -136,12 +139,12 @@ def tile_list_kg_max_sig_kernel(
 
         def make_ha(b, c):
             h, j0 = divmod(c * CHUNK, HALF)
-            bank = psum_a.tile([P, PACK, CHUNK], F32, name="bank_a")
+            bank = psum_a.tile([P, PACK, CHUNK], F32, name="bank_a", tag="for_scalar")
             for t in range(PACK):
                 cols = slice(t * 2 * P + b * P, t * 2 * P + (b + 1) * P)
                 nc.tensor.matmul_mx(
                     out=bank[:, t, :],
-                    lhsT=wa_w[:, cols].bitcast(FP8X4),
+                    lhsT=wa_w[b][:, t * P : (t + 1) * P].bitcast(FP8X4),
                     lhsT_scale=wa_s[:, cols],
                     rhs=g_w[h][:, j0 : j0 + CHUNK].bitcast(FP8X4),
                     rhs_scale=g_s[:, c * CHUNK : (c + 1) * CHUNK],
@@ -151,30 +154,23 @@ def tile_list_kg_max_sig_kernel(
             ha[b, c] = keep.tile([P, CHUNK, PACK], F32, name="ha%d_%d" % (b, c))
             nc.scalar.copy(out=ha[b, c][:], in_=bank[:].rearrange("p t j -> p j t"))
 
-        round_wb(0, 0, 0)
+        round_wb_on_scalar(0, 0)
+        round_wb_on_scalar(1, 0)
         for c in range(CHUNKS):
             make_ha(0, c)
-        for q in range(4):
-            nc.scalar.dma_start(
-                out=g2_s1[32 * q : 32 * q + 4, :].bitcast(I32),
-                in_=g2_s[32 * q + 4 : 32 * q + 8, :].bitcast(I32),
-            )
 
         g2_w = []
         for h in range(2):
             picked = keep.tile([P, HALF], U32, name="g2_pair%d" % h)
             nc.vector.tensor_copy(picked[:], tab2_w[:].bitcast(U32).indirect(half_of(list2, h)))
-            if h == 0:
-                quantize_wb(0, 0)
+            quantize_wb(h, 0)
             parted = keep.tile([P, 2, 2 * HALF], U8, name="g2_w%d" % h, align_bytes=64)
             nc.vector.tensor_copy(
                 out=parted[:].bitcast(U16),
                 in_=picked[:].bitcast(U16).rearrange("p (j d) -> p d j", d=2),
             )
             g2_w.append(parted)
-
-        round_wb(1, 0, 2)
-        quantize_wb(1, 0)
+        order_wa(1)
 
         h_w = [keep.tile([P, J], U32, name="h_w%d" % b, align_bytes=64) for b in range(2)]
         h_s = [keep.tile([P, J], U8, name="h_s%d" % b, align_bytes=64) for b in range(2)]
@@ -193,7 +189,7 @@ def tile_list_kg_max_sig_kernel(
                             lhsT=wb_w[a, b][:, cols].bitcast(FP8X4),
                             lhsT_scale=wb_s[a, b][:, cols],
                             rhs=g2_w[h][:, a, 2 * j0 : 2 * (j0 + CHUNK)].bitcast(FP4X4),
-                            rhs_scale=g2_planes[a][:, c * CHUNK : (c + 1) * CHUNK],
+                            rhs_scale=g2_s[a][:, c * CHUNK : (c + 1) * CHUNK],
                             start=(a == 0),
                             stop=(a == 1),
                         )
@@ -215,7 +211,7 @@ def tile_list_kg_max_sig_kernel(
 
         def score(c0, count):
             queries = slice(c0 * CHUNK, (c0 + count) * CHUNK)
-            bank = psum_y.tile([P, N // P, count * CHUNK], F32, name="bank_y")
+            bank = psum_a.tile([P, N // P, count * CHUNK], F32, name="bank_y", tag="for_scalar")
             for m in range(N // P):
                 for b in range(2):
                     cols = slice(b * N + m * P, b * N + (m + 1) * P)
@@ -228,28 +224,26 @@ def tile_list_kg_max_sig_kernel(
                         start=(b == 0),
                         stop=(b == 1),
                     )
-            result = ring.tile([P, N // P, count * CHUNK], F32, name="result", tag="result")
+            result = keep.tile([P, N // P, count * CHUNK], F32, name="result%d" % c0)
             nc.scalar.activation(out=result[:], in_=bank[:], func=mybir.ActivationFunctionType.Sigmoid)
             nc.sync.dma_start(out=out[:, queries].rearrange("(m p) j -> p m j", p=P), in_=result[:])
 
+        round_wb_on_scalar(0, 1)
+        round_wb_on_gpsimd(1, 1)
         first = make_h(0, 0, 4)
-        make_ha(1, 0)
-        round_wb(0, 1, PACK)
-        make_ha(1, 1)
-        round_wb(1, 1, PACK)
         second = make_h(0, 4, 4)
         quantize_wb(0, 1)
         quantize_wb(1, 1)
         quantize_h(0, 0, 4, first)
         quantize_h(0, 4, 4, second)
-        for c in range(2, 5):
+        for c in range(CHUNKS // 2):
             make_ha(1, c)
         for b in range(2):
             nc.scalar.copy(
                 out=en_bf[:, b * N * PACK : (b + 1) * N * PACK].rearrange("p (c e t) -> p c t e", e=4, t=PACK),
                 in_=en_raw[:, b].rearrange("p t (c e) -> p c t e", e=4),
             )
-        for c in range(5, CHUNKS):
+        for c in range(CHUNKS // 2, CHUNKS):
             make_ha(1, c)
 
         waiting = None

@@ -21,6 +21,7 @@ K_PASS = P * PACK
 HALF = J // 2
 CHUNK = 128
 CHUNKS = J // CHUNK
+PARKED = 8
 SECOND_RUNS = (2, 2, 2, 1, 1)
 
 
@@ -31,30 +32,27 @@ def tile_list_kg_max_sig_kernel(
     with ExitStack() as ctx:
         keep = ctx.enter_context(tc.tile_pool(name="keep", bufs=1))
         ring = ctx.enter_context(tc.tile_pool(name="ring", bufs=3))
-        psum_a = ctx.enter_context(tc.psum_pool(name="psum_a", bufs=3))
-        psum_b = ctx.enter_context(tc.psum_pool(name="psum_b", bufs=5))
+        psum = ctx.enter_context(tc.psum_pool(name="psum", bufs=8))
 
         list1 = keep.tile([P, J // 16], U16, name="list1")
         list2 = keep.tile([P, J // 16], U16, name="list2")
         tab_s = keep.tile([P, T], U8, name="tab_s")
-        tab2_s = keep.tile([P, 2 * T], U8, name="tab2_s")
+        tab2_s = keep.tile([P, T], U8, name="tab2_s")
         wa_s_raw = keep.tile([P, R], U8, name="wa_s_raw")
         tab_w = keep.tile([P, T], I32, name="tab_w")
         tab2_w = keep.tile([P, T], I32, name="tab2_w")
         g_s = keep.tile([P, J], U8, name="g_s", align_bytes=64)
-        g2_s = [keep.tile([P, J], U8, name="g2_s%d" % a, align_bytes=64) for a in range(2)]
+        g2_s = [keep.tile([P, J], U8, name="g2_s0", align_bytes=64)]
         wa_s = keep.tile([P, R], U8, name="wa_s", align_bytes=64)
 
         nc.vector.memset(tab_s[:].bitcast(I32), 0)
         nc.vector.memset(tab2_s[:].bitcast(I32), 0)
         nc.gpsimd.memset(wa_s_raw[:].bitcast(I32), 0)
 
-        def load_scale_rows(planes, scales):
-            passes = scales.shape[0]
+        def load_scale_rows(plane, rows):
             for q in range(4):
                 nc.sync.dma_start(
-                    out=planes[32 * q : 32 * q + 4, :].bitcast(I32).rearrange("r (a c) -> r a c", a=passes),
-                    in_=scales[:, 4 * q : 4 * q + 4, :].bitcast(I32).rearrange("a r c -> r a c"),
+                    out=plane[32 * q : 32 * q + 4, :].bitcast(I32), in_=rows[4 * q : 4 * q + 4, :].bitcast(I32)
                 )
 
         def load_words(words, packed):
@@ -62,10 +60,15 @@ def tile_list_kg_max_sig_kernel(
 
         wb_raw = {}
 
-        def load_wb(a, b):
-            wb_raw[a, b] = keep.tile([P, PACK, K_PASS], F32, name="wb_raw%d%d" % (a, b))
-            rows = wb[a * K_PASS : (a + 1) * K_PASS, b * K_PASS : (b + 1) * K_PASS]
-            nc.sync.dma_start(out=wb_raw[a, b][:], in_=rows.rearrange("(p i) r -> p i r", i=PACK))
+        def load_wb(a, b, buffers):
+            width = K_PASS // len(buffers)
+            wb_raw[a, b] = []
+            for piece, tag in enumerate(buffers):
+                raw = keep.tile([P, PACK, width], F32, name="wb_raw", tag=tag, align_bytes=64)
+                c0 = b * K_PASS + piece * width
+                rows = wb[a * K_PASS : (a + 1) * K_PASS, c0 : c0 + width]
+                nc.sync.dma_start(out=raw[:], in_=rows.rearrange("(p i) r -> p i r", i=PACK))
+                wb_raw[a, b].append(raw)
 
         wa_rows = wa_words[0].rearrange("p c i -> p (c i)").bitcast(I32)
         wa_w_raw = [keep.tile([P, K_PASS], I32, name="wa_w_raw%d" % b) for b in range(2)]
@@ -80,21 +83,16 @@ def tile_list_kg_max_sig_kernel(
         nc.sync.dma_start(list1[:], offs)
         nc.sync.dma_start(list2[:], offs2)
         nc.sync.dma_start(out=wa_w_raw[0][:], in_=wa_rows[:, :K_PASS])
-        load_scale_rows(tab_s, tab_scales)
+        load_scale_rows(tab_s, tab_scales[0])
         load_words(tab_w, tab_words)
-        load_scale_rows(wa_s_raw, wa_scales)
-        load_wb(0, 0)
-        load_scale_rows(tab2_s, tab2_scales)
+        load_scale_rows(tab2_s, tab2_scales[0])
+        nc.sync.dma_start(out=tab2_s[PARKED : PARKED + 16, :].bitcast(I32), in_=tab2_scales[1].bitcast(I32))
+        load_wb(0, 0, ["raw0"])
+        load_scale_rows(wa_s_raw, wa_scales[0])
         load_words(tab2_w, tab2_words)
-        load_wb(1, 0)
+        load_wb(1, 0, ["raw1", "raw2"])
         nc.sync.dma_start(out=wa_w_raw[1][:], in_=wa_rows[:, K_PASS:])
-        load_wb(0, 1)
-        load_wb(1, 1)
-        en_raw = keep.tile([P, 2, PACK, N], F32, name="en_raw")
-        en_rows = en.rearrange("(b g t e) n -> b t g e n", b=2, t=PACK, e=8)
-        for b in range(2):
-            for t in range(PACK):
-                nc.sync.dma_start(out=en_raw[:, b, t, :], in_=en_rows[b, t])
+        load_wb(0, 1, ["raw3"])
 
         order_wa(0)
 
@@ -111,22 +109,23 @@ def tile_list_kg_max_sig_kernel(
             picked = keep.tile([P, HALF], U32, name="g_w%d" % h, align_bytes=64)
             nc.vector.tensor_copy(picked[:], tab_w[:].bitcast(U32).indirect(half_of(list1, h)))
             g_w.append(picked)
-        for a in range(2):
-            nc.vector.tensor_copy(g2_s[a][:], tab2_s[:, a * T : (a + 1) * T].indirect(list2[:]))
+        nc.vector.tensor_copy(g2_s[0][:], tab2_s[:].indirect(list2[:]))
 
         wb_bf, wb_w, wb_s = {}, {}, {}
 
         def round_wb_on_scalar(a, b):
-            wb_bf[a, b] = keep.tile([P, PACK * K_PASS], BF16, name="wb_bf%d%d" % (a, b), align_bytes=64)
-            dst = wb_bf[a, b][:].rearrange("p (t g c e i) -> p t g c i e", t=PACK, c=2, e=4, i=PACK)
-            src = wb_raw[a, b][:].rearrange("p i (g t c e) -> p t g c i e", t=PACK, c=2, e=4)
-            for t in range(PACK):
-                nc.scalar.copy(out=dst[:, t], in_=src[:, t])
+            wb_bf[a, b] = keep.tile([P, PACK * K_PASS], BF16, name="wb_bf", tag="wb_bf%d%d" % (a, b), align_bytes=64)
+            pieces = len(wb_raw[a, b])
+            dst = wb_bf[a, b][:].rearrange("p (t s g c e i) -> p s t g c i e", t=PACK, s=pieces, c=2, e=4, i=PACK)
+            for piece, raw in enumerate(wb_raw[a, b]):
+                src = raw[:].rearrange("p i (g t c e) -> p t g c i e", t=PACK, c=2, e=4)
+                for t in range(PACK):
+                    nc.scalar.copy(out=dst[:, piece, t], in_=src[:, t])
 
         def round_wb_on_gpsimd(a, b):
-            wb_bf[a, b] = keep.tile([P, PACK * K_PASS], BF16, name="wb_bf%d%d" % (a, b), align_bytes=64)
+            wb_bf[a, b] = keep.tile([P, PACK * K_PASS], BF16, name="wb_bf", tag="wb_bf%d%d" % (a, b), align_bytes=64)
             dst = wb_bf[a, b][:].rearrange("p (t g e i) -> p t g e i", t=PACK, e=8, i=PACK)
-            src = wb_raw[a, b][:].rearrange("p i (g t e) -> p t g e i", t=PACK, e=8)
+            src = wb_raw[a, b][0][:].rearrange("p i (g t e) -> p t g e i", t=PACK, e=8)
             for t in range(PACK):
                 nc.gpsimd.tensor_scalar(out=dst[:, t], in0=src[:, t], scalar1=1.0, scalar2=0.0, op0=MULT, op1=ADD)
 
@@ -139,7 +138,7 @@ def tile_list_kg_max_sig_kernel(
 
         def make_ha(b, c):
             h, j0 = divmod(c * CHUNK, HALF)
-            bank = psum_a.tile([P, PACK, CHUNK], F32, name="bank_a", tag="for_scalar")
+            bank = psum.tile([P, PACK, CHUNK], F32, name="bank_a", tag="bank")
             for t in range(PACK):
                 cols = slice(t * 2 * P + b * P, t * 2 * P + (b + 1) * P)
                 nc.tensor.matmul_mx(
@@ -155,7 +154,20 @@ def tile_list_kg_max_sig_kernel(
             nc.scalar.copy(out=ha[b, c][:], in_=bank[:].rearrange("p t j -> p j t"))
 
         round_wb_on_scalar(0, 0)
+        g2_s.append(keep.tile([P, J], U8, name="g2_s1", tag="raw0", align_bytes=64))
+        nc.gpsimd.memset(g2_s[1][:].bitcast(I32), 0)
+        for q in range(4):
+            nc.scalar.dma_start(
+                out=g2_s[1][32 * q : 32 * q + 4, :].bitcast(I32),
+                in_=g2_s[0][PARKED + 4 * q : PARKED + 4 * q + 4, :].bitcast(I32),
+            )
         round_wb_on_scalar(1, 0)
+        load_wb(1, 1, ["raw1"])
+        en_raw = keep.tile([P, 2, PACK, N], F32, name="en_raw", tag="raw2", align_bytes=64)
+        en_rows = en.rearrange("(b g t e) n -> b t g e n", b=2, t=PACK, e=8)
+        for b in range(2):
+            for t in range(PACK):
+                nc.sync.dma_start(out=en_raw[:, b, t, :], in_=en_rows[b, t])
         for c in range(CHUNKS):
             make_ha(0, c)
 
@@ -164,7 +176,7 @@ def tile_list_kg_max_sig_kernel(
             picked = keep.tile([P, HALF], U32, name="g2_pair%d" % h)
             nc.vector.tensor_copy(picked[:], tab2_w[:].bitcast(U32).indirect(half_of(list2, h)))
             quantize_wb(h, 0)
-            parted = keep.tile([P, 2, 2 * HALF], U8, name="g2_w%d" % h, align_bytes=64)
+            parted = keep.tile([P, 2, 2 * HALF], U8, name="g2_w%d" % h, tag="wb_bf%d0" % h, align_bytes=64)
             nc.vector.tensor_copy(
                 out=parted[:].bitcast(U16),
                 in_=picked[:].bitcast(U16).rearrange("p (j d) -> p d j", d=2),
@@ -180,7 +192,7 @@ def tile_list_kg_max_sig_kernel(
             for s in range(count):
                 c = c0 + s
                 h, j0 = divmod(c * CHUNK, HALF)
-                bank = psum_b.tile([P, PACK, CHUNK], F32, name="bank_b")
+                bank = psum.tile([P, PACK, CHUNK], F32, name="bank_b", tag="bank")
                 for t in range(PACK):
                     cols = slice(t * P, (t + 1) * P)
                     for a in range(2):
@@ -211,7 +223,7 @@ def tile_list_kg_max_sig_kernel(
 
         def score(c0, count):
             queries = slice(c0 * CHUNK, (c0 + count) * CHUNK)
-            bank = psum_a.tile([P, N // P, count * CHUNK], F32, name="bank_y", tag="for_scalar")
+            bank = psum.tile([P, N // P, count * CHUNK], F32, name="bank_y", tag="bank")
             for m in range(N // P):
                 for b in range(2):
                     cols = slice(b * N + m * P, b * N + (m + 1) * P)
@@ -231,13 +243,14 @@ def tile_list_kg_max_sig_kernel(
         round_wb_on_scalar(0, 1)
         round_wb_on_gpsimd(1, 1)
         first = make_h(0, 0, 4)
+        for c in range(3):
+            make_ha(1, c)
         second = make_h(0, 4, 4)
         quantize_wb(0, 1)
         quantize_wb(1, 1)
         quantize_h(0, 0, 4, first)
         quantize_h(0, 4, 4, second)
-        for c in range(CHUNKS // 2):
-            make_ha(1, c)
+        make_ha(1, 3)
         for b in range(2):
             nc.scalar.copy(
                 out=en_bf[:, b * N * PACK : (b + 1) * N * PACK].rearrange("p (c e t) -> p c t e", e=4, t=PACK),

@@ -116,11 +116,9 @@ def tile_list_kg_max_sig_kernel(
         def round_wb_on_scalar(a, b):
             wb_bf[a, b] = keep.tile([P, PACK * K_PASS], BF16, name="wb_bf", tag="wb_bf%d%d" % (a, b), align_bytes=64)
             pieces = len(wb_raw[a, b])
-            dst = wb_bf[a, b][:].rearrange("p (t s g c e i) -> p s t g c i e", t=PACK, s=pieces, c=2, e=4, i=PACK)
+            dst = wb_bf[a, b][:].rearrange("p (t s g e i) -> p s t g e i", t=PACK, s=pieces, e=8, i=PACK)
             for piece, raw in enumerate(wb_raw[a, b]):
-                src = raw[:].rearrange("p i (g t c e) -> p t g c i e", t=PACK, c=2, e=4)
-                for t in range(PACK):
-                    nc.scalar.copy(out=dst[:, piece, t], in_=src[:, t])
+                nc.scalar.copy(out=dst[:, piece], in_=raw[:].rearrange("p i (g t e) -> p t g e i", t=PACK, e=8))
 
         def round_wb_on_gpsimd(a, b):
             wb_bf[a, b] = keep.tile([P, PACK * K_PASS], BF16, name="wb_bf", tag="wb_bf%d%d" % (a, b), align_bytes=64)
@@ -253,8 +251,8 @@ def tile_list_kg_max_sig_kernel(
         make_ha(1, 3)
         for b in range(2):
             nc.scalar.copy(
-                out=en_bf[:, b * N * PACK : (b + 1) * N * PACK].rearrange("p (c e t) -> p c t e", e=4, t=PACK),
-                in_=en_raw[:, b].rearrange("p t (c e) -> p c t e", e=4),
+                out=en_bf[:, b * N * PACK : (b + 1) * N * PACK].rearrange("p (n t) -> p n t", t=PACK),
+                in_=en_raw[:, b].rearrange("p t n -> p n t"),
             )
         for c in range(CHUNKS // 2, CHUNKS):
             make_ha(1, c)

@@ -21,8 +21,9 @@ K_PASS = P * PACK
 HALF = J // 2
 CHUNK = 128
 CHUNKS = J // CHUNK
-PARKED = 8
+PARKED = 16
 SECOND_RUNS = (2, 2, 2, 1, 1)
+SIGMOID = mybir.ActivationFunctionType.Sigmoid
 
 
 def tile_list_kg_max_sig_kernel(
@@ -31,8 +32,7 @@ def tile_list_kg_max_sig_kernel(
     nc = tc.nc
     with ExitStack() as ctx:
         keep = ctx.enter_context(tc.tile_pool(name="keep", bufs=1))
-        ring = ctx.enter_context(tc.tile_pool(name="ring", bufs=3))
-        psum = ctx.enter_context(tc.psum_pool(name="psum", bufs=8))
+        psum = ctx.enter_context(tc.psum_pool(name="psum", bufs=1))
 
         list1 = keep.tile([P, J // 16], U16, name="list1")
         list2 = keep.tile([P, J // 16], U16, name="list2")
@@ -42,101 +42,119 @@ def tile_list_kg_max_sig_kernel(
         tab_w = keep.tile([P, T], I32, name="tab_w")
         tab2_w = keep.tile([P, T], I32, name="tab2_w")
         g_s = keep.tile([P, J], U8, name="g_s", align_bytes=64)
-        g2_s = [keep.tile([P, J], U8, name="g2_s0", align_bytes=64)]
+        g2_s = [keep.tile([P, J], U8, name="g2_s%d" % a, align_bytes=64) for a in range(2)]
         wa_s = keep.tile([P, R], U8, name="wa_s", align_bytes=64)
+        warm = keep.tile([P, 2], F32, name="warm")
+        wa_rows = wa_words[0].rearrange("p c i -> p (c i)").bitcast(I32)
+        wa_w_raw = [keep.tile([P, K_PASS], I32, name="wa_w_raw%d" % b) for b in range(2)]
+        wa_w = [keep.tile([P, K_PASS], I32, name="wa_w%d" % b, align_bytes=64) for b in range(2)]
+        pieces = [(a, b) for b in range(2) for a in range(2)]
+        wb_raw = {ab: keep.tile([P, PACK, K_PASS], F32, name="wb_raw%d%d" % ab, align_bytes=64) for ab in pieces}
+        wb_bf = {ab: keep.tile([P, PACK * K_PASS], BF16, name="wb_bf%d%d" % ab, align_bytes=64) for ab in pieces}
+        wb_w = {ab: keep.tile([P, K_PASS], U32, name="wb_w%d%d" % ab, align_bytes=64) for ab in pieces}
+        wb_s = {ab: keep.tile([P, K_PASS], U8, name="wb_s%d%d" % ab, align_bytes=64) for ab in pieces}
+        en_raw = [keep.tile([P, PACK, N], F32, name="en_raw%d" % b, align_bytes=64) for b in range(2)]
+        en_w = keep.tile([P, 2 * N], U32, name="en_w", align_bytes=64)
+        en_s = keep.tile([P, 2 * N], U8, name="en_s", align_bytes=64)
+        g_w = {}
+        g2_pair = [keep.tile([P, HALF], U32, name="g2_pair%d" % h, align_bytes=64) for h in range(2)]
+        g2_w = {}
+        h_w = [keep.tile([P, J], U32, name="h_w%d" % b, align_bytes=64) for b in range(2)]
+        ha = {}
+        h_s = [keep.tile([P, J], U8, name="h_s%d" % b, align_bytes=64) for b in range(2)]
 
-        nc.vector.memset(tab_s[:].bitcast(I32), 0)
-        nc.vector.memset(tab2_s[:].bitcast(I32), 0)
-        nc.gpsimd.memset(wa_s_raw[:].bitcast(I32), 0)
-
-        def load_scale_rows(plane, rows):
+        def load_scale_rows(queue, plane, rows):
             for q in range(4):
-                nc.sync.dma_start(
+                queue.dma_start(
                     out=plane[32 * q : 32 * q + 4, :].bitcast(I32), in_=rows[4 * q : 4 * q + 4, :].bitcast(I32)
                 )
+
+        def load_tab2_scales():
+            rows = tab2_scales.bitcast(I32).rearrange("a (q r) c -> r q a c", r=4)
+            for r in range(4):
+                nc.sync.dma_start(out=tab2_s[r:P:PARKED, :].bitcast(I32), in_=rows[r])
 
         def load_words(words, packed):
             nc.sync.dma_start(out=words[:], in_=packed[0].rearrange("p c i -> p (c i)").bitcast(I32))
 
-        wb_raw = {}
+        def load_wa(b):
+            nc.sync.dma_start(out=wa_w_raw[b][:], in_=wa_rows[:, b * K_PASS : (b + 1) * K_PASS])
 
-        def load_wb(a, b, buffers):
-            width = K_PASS // len(buffers)
-            wb_raw[a, b] = []
-            for piece, tag in enumerate(buffers):
-                raw = keep.tile([P, PACK, width], F32, name="wb_raw", tag=tag, align_bytes=64)
-                c0 = b * K_PASS + piece * width
-                rows = wb[a * K_PASS : (a + 1) * K_PASS, c0 : c0 + width]
-                nc.sync.dma_start(out=raw[:], in_=rows.rearrange("(p i) r -> p i r", i=PACK))
-                wb_raw[a, b].append(raw)
+        def load_wb(a, b):
+            rows = wb[a * K_PASS : (a + 1) * K_PASS, b * K_PASS : (b + 1) * K_PASS]
+            nc.sync.dma_start(out=wb_raw[a, b][:], in_=rows.rearrange("(p i) r -> p i r", i=PACK))
 
-        wa_rows = wa_words[0].rearrange("p c i -> p (c i)").bitcast(I32)
-        wa_w_raw = [keep.tile([P, K_PASS], I32, name="wa_w_raw%d" % b) for b in range(2)]
-        wa_w = [keep.tile([P, K_PASS], I32, name="wa_w%d" % b, align_bytes=64) for b in range(2)]
+        def load_en(b):
+            en_rows = en.rearrange("(b g t e) n -> b t g e n", b=2, t=PACK, e=8)
+            for t in range(PACK):
+                nc.sync.dma_start(out=en_raw[b][:, t, :], in_=en_rows[b, t])
 
-        def order_wa(b):
-            nc.vector.tensor_copy(
+        def order_wa(b, engine):
+            engine.tensor_copy(
                 out=wa_w[b][:].rearrange("p (t g e) -> p t g e", t=PACK, e=8),
                 in_=wa_w_raw[b][:].rearrange("p (g t e) -> p t g e", t=PACK, e=8),
             )
 
-        nc.sync.dma_start(list1[:], offs)
-        nc.sync.dma_start(list2[:], offs2)
-        nc.sync.dma_start(out=wa_w_raw[0][:], in_=wa_rows[:, :K_PASS])
-        load_scale_rows(tab_s, tab_scales[0])
-        load_words(tab_w, tab_words)
-        load_scale_rows(tab2_s, tab2_scales[0])
-        nc.sync.dma_start(out=tab2_s[PARKED : PARKED + 16, :].bitcast(I32), in_=tab2_scales[1].bitcast(I32))
-        load_wb(0, 0, ["raw0"])
-        load_scale_rows(wa_s_raw, wa_scales[0])
-        load_words(tab2_w, tab2_words)
-        load_wb(1, 0, ["raw1", "raw2"])
-        nc.sync.dma_start(out=wa_w_raw[1][:], in_=wa_rows[:, K_PASS:])
-        load_wb(0, 1, ["raw3"])
-
-        order_wa(0)
+        def order_wa_scales(engine):
+            engine.tensor_copy(
+                out=wa_s[:].bitcast(I32).rearrange("p (t g e) -> p t g e", t=PACK, e=2),
+                in_=wa_s_raw[:].bitcast(I32).rearrange("p (g t e) -> p t g e", t=PACK, e=2),
+            )
 
         def half_of(entries, h):
             return entries[:, h * HALF // 16 : (h + 1) * HALF // 16]
 
-        nc.vector.tensor_copy(g_s[:], tab_s[:].indirect(list1[:]))
-        nc.gpsimd.tensor_copy(
-            out=wa_s[:].bitcast(I32).rearrange("p (t g e) -> p t g e", t=PACK, e=2),
-            in_=wa_s_raw[:].bitcast(I32).rearrange("p (g t e) -> p t g e", t=PACK, e=2),
-        )
-        g_w = []
-        for h in range(2):
-            picked = keep.tile([P, HALF], U32, name="g_w%d" % h, align_bytes=64)
-            nc.vector.tensor_copy(picked[:], tab_w[:].bitcast(U32).indirect(half_of(list1, h)))
-            g_w.append(picked)
-        nc.vector.tensor_copy(g2_s[0][:], tab2_s[:].indirect(list2[:]))
+        def gather_tab(h, tag):
+            g_w[h] = keep.tile([P, HALF], U32, name="g_w", tag=tag, align_bytes=64)
+            nc.vector.tensor_copy(g_w[h][:], tab_w[:].bitcast(U32).indirect(half_of(list1, h)))
 
-        wb_bf, wb_w, wb_s = {}, {}, {}
+        def gather_tab2(h):
+            nc.vector.tensor_copy(g2_pair[h][:], tab2_w[:].bitcast(U32).indirect(half_of(list2, h)))
 
-        def round_wb_on_scalar(a, b):
-            wb_bf[a, b] = keep.tile([P, PACK * K_PASS], BF16, name="wb_bf", tag="wb_bf%d%d" % (a, b), align_bytes=64)
-            pieces = len(wb_raw[a, b])
-            dst = wb_bf[a, b][:].rearrange("p (t s g e i) -> p s t g e i", t=PACK, s=pieces, e=8, i=PACK)
-            for piece, raw in enumerate(wb_raw[a, b]):
-                nc.scalar.copy(out=dst[:, piece], in_=raw[:].rearrange("p i (g t e) -> p t g e i", t=PACK, e=8))
+        def part(h, tag):
+            g2_w[h] = keep.tile([P, 2, 2 * HALF], U8, name="g2_w", tag=tag, align_bytes=64)
+            nc.vector.tensor_copy(
+                out=g2_w[h][:].bitcast(U16),
+                in_=g2_pair[h][:].bitcast(U16).rearrange("p (j d) -> p d j", d=2),
+            )
 
-        def round_wb_on_gpsimd(a, b):
-            wb_bf[a, b] = keep.tile([P, PACK * K_PASS], BF16, name="wb_bf", tag="wb_bf%d%d" % (a, b), align_bytes=64)
+        def wb_views(a, b):
             dst = wb_bf[a, b][:].rearrange("p (t g e i) -> p t g e i", t=PACK, e=8, i=PACK)
-            src = wb_raw[a, b][0][:].rearrange("p i (g t e) -> p t g e i", t=PACK, e=8)
-            for t in range(PACK):
+            src = wb_raw[a, b][:].rearrange("p i (g t e) -> p t g e i", t=PACK, e=8)
+            return dst, src
+
+        def round_wb_on_scalar(a, b, t0, t1):
+            dst, src = wb_views(a, b)
+            nc.scalar.copy(out=dst[:, t0:t1], in_=src[:, t0:t1])
+
+        def round_wb_on_gpsimd(a, b, t0, t1):
+            dst, src = wb_views(a, b)
+            for t in range(t0, t1):
                 nc.gpsimd.tensor_scalar(out=dst[:, t], in0=src[:, t], scalar1=1.0, scalar2=0.0, op0=MULT, op1=ADD)
 
         def quantize_wb(a, b):
-            wb_w[a, b] = keep.tile([P, K_PASS], U32, name="wb_w%d%d" % (a, b), align_bytes=64)
-            wb_s[a, b] = keep.tile([P, K_PASS], U8, name="wb_s%d%d" % (a, b), align_bytes=64)
             nc.vector.quantize_mx(out=wb_w[a, b][:].bitcast(FP8X4), scales=wb_s[a, b][:], in_=wb_bf[a, b][:])
 
-        ha = {}
+        def en_views(b):
+            dst = en_bf[:, b * N * PACK : (b + 1) * N * PACK].rearrange("p (n t) -> p n t", t=PACK)
+            return dst, en_raw[b][:].rearrange("p t n -> p n t")
 
-        def make_ha(b, c):
+        def round_en_on_scalar(b):
+            dst, src = en_views(b)
+            nc.scalar.copy(out=dst, in_=src)
+
+        def round_en_on_gpsimd(b):
+            dst, src = en_views(b)
+            for m in range(PACK):
+                cols = slice(m * N // PACK, (m + 1) * N // PACK)
+                nc.gpsimd.tensor_scalar(out=dst[:, cols], in0=src[:, cols], scalar1=1.0, scalar2=0.0, op0=MULT, op1=ADD)
+
+        def quantize_en():
+            nc.vector.quantize_mx(out=en_w[:].bitcast(FP8X4), scales=en_s[:], in_=en_bf[:])
+
+        def product_a(b, c):
             h, j0 = divmod(c * CHUNK, HALF)
-            bank = psum.tile([P, PACK, CHUNK], F32, name="bank_a", tag="bank")
+            bank = psum.tile([P, PACK, CHUNK], F32, name="bank_a", tag="bank%d" % c)
             for t in range(PACK):
                 cols = slice(t * 2 * P + b * P, t * 2 * P + (b + 1) * P)
                 nc.tensor.matmul_mx(
@@ -148,80 +166,48 @@ def tile_list_kg_max_sig_kernel(
                     start=True,
                     stop=True,
                 )
-            ha[b, c] = keep.tile([P, CHUNK, PACK], F32, name="ha%d_%d" % (b, c))
-            nc.scalar.copy(out=ha[b, c][:], in_=bank[:].rearrange("p t j -> p j t"))
+            return bank
 
-        round_wb_on_scalar(0, 0)
-        g2_s.append(keep.tile([P, J], U8, name="g2_s1", tag="raw0", align_bytes=64))
-        nc.gpsimd.memset(g2_s[1][:].bitcast(I32), 0)
-        for q in range(4):
-            nc.scalar.dma_start(
-                out=g2_s[1][32 * q : 32 * q + 4, :].bitcast(I32),
-                in_=g2_s[0][PARKED + 4 * q : PARKED + 4 * q + 4, :].bitcast(I32),
-            )
-        round_wb_on_scalar(1, 0)
-        load_wb(1, 1, ["raw1"])
-        en_raw = keep.tile([P, 2, PACK, N], F32, name="en_raw", tag="raw2", align_bytes=64)
-        en_rows = en.rearrange("(b g t e) n -> b t g e n", b=2, t=PACK, e=8)
-        for b in range(2):
+        def product_b(b, c):
+            h, j0 = divmod(c * CHUNK, HALF)
+            bank = psum.tile([P, PACK, CHUNK], F32, name="bank_b", tag="bank%d" % c)
             for t in range(PACK):
-                nc.sync.dma_start(out=en_raw[:, b, t, :], in_=en_rows[b, t])
-        for c in range(CHUNKS):
-            make_ha(0, c)
+                cols = slice(t * P, (t + 1) * P)
+                for a in range(2):
+                    nc.tensor.matmul_mx(
+                        out=bank[:, t, :],
+                        lhsT=wb_w[a, b][:, cols].bitcast(FP8X4),
+                        lhsT_scale=wb_s[a, b][:, cols],
+                        rhs=g2_w[h][:, a, 2 * j0 : 2 * (j0 + CHUNK)].bitcast(FP4X4),
+                        rhs_scale=g2_s[a][:, c * CHUNK : (c + 1) * CHUNK],
+                        start=(a == 0),
+                        stop=(a == 1),
+                    )
+            return bank
 
-        g2_w = []
-        for h in range(2):
-            picked = keep.tile([P, HALF], U32, name="g2_pair%d" % h)
-            nc.vector.tensor_copy(picked[:], tab2_w[:].bitcast(U32).indirect(half_of(list2, h)))
-            quantize_wb(h, 0)
-            parted = keep.tile([P, 2, 2 * HALF], U8, name="g2_w%d" % h, tag="wb_bf%d0" % h, align_bytes=64)
-            nc.vector.tensor_copy(
-                out=parted[:].bitcast(U16),
-                in_=picked[:].bitcast(U16).rearrange("p (j d) -> p d j", d=2),
+        def room_for(banks, tag):
+            return keep.tile([P, banks * CHUNK * PACK], F32, name="room", tag=tag, align_bytes=64)
+
+        def copy_ha(b, c0, c1, room):
+            for c in range(c0, c1):
+                ha[b, c] = room[:, (c - c0) * CHUNK * PACK : (c - c0 + 1) * CHUNK * PACK].rearrange("p (j t) -> p j t", t=PACK)
+                nc.scalar.copy(out=ha[b, c], in_=product_a(b, c)[:].rearrange("p t j -> p j t"))
+
+        def maximum(bank, copied, h_bf, s):
+            nc.vector.tensor_tensor(
+                out=h_bf[:, s * CHUNK * PACK : (s + 1) * CHUNK * PACK].rearrange("p (j t) -> p j t", t=PACK),
+                in0=bank[:].rearrange("p t j -> p j t"),
+                in1=copied,
+                op=MAX,
             )
-            g2_w.append(parted)
-        order_wa(1)
-
-        h_w = [keep.tile([P, J], U32, name="h_w%d" % b, align_bytes=64) for b in range(2)]
-        h_s = [keep.tile([P, J], U8, name="h_s%d" % b, align_bytes=64) for b in range(2)]
-
-        def make_h(b, c0, count):
-            h_bf = ring.tile([P, count * CHUNK * PACK], BF16, name="h_bf", tag="h_bf", align_bytes=64)
-            for s in range(count):
-                c = c0 + s
-                h, j0 = divmod(c * CHUNK, HALF)
-                bank = psum.tile([P, PACK, CHUNK], F32, name="bank_b", tag="bank")
-                for t in range(PACK):
-                    cols = slice(t * P, (t + 1) * P)
-                    for a in range(2):
-                        nc.tensor.matmul_mx(
-                            out=bank[:, t, :],
-                            lhsT=wb_w[a, b][:, cols].bitcast(FP8X4),
-                            lhsT_scale=wb_s[a, b][:, cols],
-                            rhs=g2_w[h][:, a, 2 * j0 : 2 * (j0 + CHUNK)].bitcast(FP4X4),
-                            rhs_scale=g2_s[a][:, c * CHUNK : (c + 1) * CHUNK],
-                            start=(a == 0),
-                            stop=(a == 1),
-                        )
-                nc.vector.tensor_tensor(
-                    out=h_bf[:, s * CHUNK * PACK : (s + 1) * CHUNK * PACK].rearrange("p (j t) -> p j t", t=PACK),
-                    in0=bank[:].rearrange("p t j -> p j t"),
-                    in1=ha[b, c][:],
-                    op=MAX,
-                )
-            return h_bf
 
         def quantize_h(b, c0, count, h_bf):
             cols = slice(c0 * CHUNK, (c0 + count) * CHUNK)
-            nc.vector.quantize_mx(out=h_w[b][:, cols].bitcast(FP8X4), scales=h_s[b][:, cols], in_=h_bf[:])
-
-        en_bf = keep.tile([P, 2 * N * PACK], BF16, name="en_bf", align_bytes=64)
-        en_w = keep.tile([P, 2 * N], U32, name="en_w", align_bytes=64)
-        en_s = keep.tile([P, 2 * N], U8, name="en_s", align_bytes=64)
+            nc.vector.quantize_mx(out=h_w[b][:, cols].bitcast(FP8X4), scales=h_s[b][:, cols], in_=h_bf)
 
         def score(c0, count):
             queries = slice(c0 * CHUNK, (c0 + count) * CHUNK)
-            bank = psum.tile([P, N // P, count * CHUNK], F32, name="bank_y", tag="bank")
+            bank = psum.tile([P, N // P, count * CHUNK], F32, name="bank_y", tag="bank%d" % c0)
             for m in range(N // P):
                 for b in range(2):
                     cols = slice(b * N + m * P, b * N + (m + 1) * P)
@@ -235,38 +221,95 @@ def tile_list_kg_max_sig_kernel(
                         stop=(b == 1),
                     )
             result = keep.tile([P, N // P, count * CHUNK], F32, name="result%d" % c0)
-            nc.scalar.activation(out=result[:], in_=bank[:], func=mybir.ActivationFunctionType.Sigmoid)
+            nc.scalar.activation(out=result[:], in_=bank[:], func=SIGMOID)
             nc.sync.dma_start(out=out[:, queries].rearrange("(m p) j -> p m j", p=P), in_=result[:])
 
-        round_wb_on_scalar(0, 1)
-        round_wb_on_gpsimd(1, 1)
-        first = make_h(0, 0, 4)
-        for c in range(3):
-            make_ha(1, c)
-        second = make_h(0, 4, 4)
-        quantize_wb(0, 1)
-        quantize_wb(1, 1)
-        quantize_h(0, 0, 4, first)
-        quantize_h(0, 4, 4, second)
-        make_ha(1, 3)
-        for b in range(2):
-            nc.scalar.copy(
-                out=en_bf[:, b * N * PACK : (b + 1) * N * PACK].rearrange("p (n t) -> p n t", t=PACK),
-                in_=en_raw[:, b].rearrange("p t n -> p n t"),
-            )
-        for c in range(CHUNKS // 2, CHUNKS):
-            make_ha(1, c)
+        nc.vector.memset(tab_s[:, : T // 2].bitcast(I32), 0)
+        nc.gpsimd.memset(tab_s[:, T // 2 :].bitcast(I32), 0)
+        nc.vector.memset(warm[:, 0:1], 0.0)
+        nc.vector.memset(tab2_s[:].bitcast(I32), 0)
+        nc.gpsimd.memset(wa_s_raw[:].bitcast(I32), 0)
+        nc.gpsimd.memset(g2_s[1][:].bitcast(I32), 0)
+        nc.scalar.activation(out=warm[:, 1:2], in_=warm[:, 0:1], func=SIGMOID)
 
-        waiting = None
+        nc.sync.dma_start(list1[:], offs)
+        nc.sync.dma_start(list2[:], offs2)
+        load_scale_rows(nc.sync, tab_s, tab_scales[0])
+        load_wa(0)
+        load_words(tab_w, tab_words)
+        load_tab2_scales()
+        load_wb(0, 0)
+        load_scale_rows(nc.sync, wa_s_raw, wa_scales[0])
+        load_words(tab2_w, tab2_words)
+        load_wb(1, 0)
+        nc.vector.tensor_copy(g_s[:], tab_s[:].indirect(list1[:]))
+        gather_tab(0, "g_w0")
+        gather_tab(1, "g_w1")
+        nc.vector.tensor_copy(g2_s[0][:], tab2_s[:].indirect(list2[:]))
+        nc.sync.dma_start(out=g2_s[1][: P - PARKED, :].bitcast(I32), in_=g2_s[0][PARKED:, :].bitcast(I32))
+        load_wa(1)
+        load_wb(0, 1)
+        load_wb(1, 1)
+        load_en(0)
+        load_en(1)
+
+        order_wa(0, nc.gpsimd)
+        order_wa_scales(nc.gpsimd)
+        gather_tab2(0)
+        gather_tab2(1)
+        part(0, "g2_w0")
+        round_wb_on_scalar(0, 0, 0, 3)
+        round_wb_on_gpsimd(0, 0, 3, 4)
+        quantize_wb(0, 0)
+        round_wb_on_scalar(1, 0, 0, 2)
+        round_wb_on_gpsimd(1, 0, 2, 4)
+        quantize_wb(1, 0)
+        part(1, "wb_bf10")
+        copy_ha(0, 0, 3, room_for(3, "ha0"))
+        copy_ha(0, 3, CHUNKS, room_for(5, "wb_raw10"))
+        order_wa(1, nc.gpsimd)
+        round_wb_on_scalar(0, 1, 0, 1)
+        round_wb_on_gpsimd(0, 1, 1, 4)
+        round_wb_on_scalar(1, 1, 0, 2)
+        round_wb_on_gpsimd(1, 1, 2, 4)
+
+        def maxima(b, c0, count, h_bf):
+            for s in range(count):
+                maximum(product_b(b, c0 + s), ha[b, c0 + s], h_bf, s)
+            return c0, count, h_bf
+
+        h_bf_a = keep.tile([P, 4 * CHUNK * PACK], BF16, name="h_bf_a", align_bytes=64)
+        h_bf_b = keep.tile([P, 2 * CHUNK * PACK], BF16, name="h_bf_b", align_bytes=64)
+        run_a = maxima(0, 0, 4, h_bf_a[:])
+        quantize_wb(0, 1)
+        copy_ha(1, 0, 2, room_for(2, "wb_raw01"))
+        run_b = maxima(0, 4, 2, h_bf_b[:])
+        quantize_h(0, *run_a)
+        quantize_h(0, *run_b)
+        quantize_wb(1, 1)
+        late = room_for(7, "wb_raw11")
+        copy_ha(1, 2, 4, late[:, : 2 * CHUNK * PACK])
+        run_c = maxima(0, 6, 2, late[:, 6 * CHUNK * PACK :].bitcast(BF16))
+        copy_ha(1, 4, CHUNKS, late[:, 2 * CHUNK * PACK : 6 * CHUNK * PACK])
+        en_bf = keep.tile([P, 2 * N * PACK], BF16, name="en_bf", tag="wb_bf11", align_bytes=64)
+        round_en_on_gpsimd(0)
+        round_en_on_scalar(1)
+
+        waiting = []
         c0 = 0
-        for count in SECOND_RUNS:
-            h_bf = make_h(1, c0, count)
-            if waiting is None:
-                nc.vector.quantize_mx(out=en_w[:].bitcast(FP8X4), scales=en_s[:], in_=en_bf[:])
+        for run, count in enumerate(SECOND_RUNS):
+            tag = "wb_bf11" if run == 2 else "h_bf%d" % run
+            h_bf = keep.tile([P, count * CHUNK * PACK], BF16, name="h_bf", tag=tag, align_bytes=64)
+            done = maxima(1, c0, count, h_bf[:])
+            if run == 0:
+                quantize_h(0, *run_c)
             else:
-                quantize_h(1, *waiting)
-                score(waiting[0], waiting[1])
-            waiting = (c0, count, h_bf)
+                quantize_h(1, *waiting[-1])
+            if run == 1:
+                quantize_en()
+            if run >= 1:
+                score(*waiting[-1][:2])
+            waiting.append(done)
             c0 += count
-        quantize_h(1, *waiting)
-        score(waiting[0], waiting[1])
+        quantize_h(1, *waiting[-1])
+        score(*waiting[-1][:2])

@@ -22,7 +22,7 @@ HALF = J // 2
 CHUNK = 128
 CHUNKS = J // CHUNK
 PARKED = 16
-SECOND_RUNS = (2, 2, 2, 1, 1)
+SECOND_RUNS = (4, 1, 1, 1, 1)
 SIGMOID = mybir.ActivationFunctionType.Sigmoid
 
 
@@ -50,16 +50,19 @@ def tile_list_kg_max_sig_kernel(
         wa_w = [keep.tile([P, K_PASS], I32, name="wa_w%d" % b, align_bytes=64) for b in range(2)]
         pieces = [(a, b) for b in range(2) for a in range(2)]
         wb_raw = {ab: keep.tile([P, PACK, K_PASS], F32, name="wb_raw%d%d" % ab, align_bytes=64) for ab in pieces}
-        wb_bf = {ab: keep.tile([P, PACK * K_PASS], BF16, name="wb_bf%d%d" % ab, align_bytes=64) for ab in pieces}
-        wb_w = {ab: keep.tile([P, K_PASS], U32, name="wb_w%d%d" % ab, align_bytes=64) for ab in pieces}
-        wb_s = {ab: keep.tile([P, K_PASS], U8, name="wb_s%d%d" % ab, align_bytes=64) for ab in pieces}
+        wb_bf = {(a, 0): keep.tile([P, PACK * K_PASS], BF16, name="wb_bf%d0" % a, align_bytes=64)[:] for a in range(2)}
+        wb_bf1 = keep.tile([P, 2 * PACK * K_PASS], BF16, name="wb_bf1", align_bytes=64)
+        wb_w = [keep.tile([P, 2 * K_PASS], U32, name="wb_w%d" % b, align_bytes=64) for b in range(2)]
+        wb_s = [keep.tile([P, 2 * K_PASS], U8, name="wb_s%d" % b, align_bytes=64) for b in range(2)]
+        for a in range(2):
+            wb_bf[a, 1] = wb_bf1[:, a * PACK * K_PASS : (a + 1) * PACK * K_PASS]
         en_raw = [keep.tile([P, PACK, N], F32, name="en_raw%d" % b, align_bytes=64) for b in range(2)]
         en_w = keep.tile([P, 2 * N], U32, name="en_w", align_bytes=64)
         en_s = keep.tile([P, 2 * N], U8, name="en_s", align_bytes=64)
-        g_w = {}
+        g_w = keep.tile([P, J], U32, name="g_w", align_bytes=64)
         g2_pair = [keep.tile([P, HALF], U32, name="g2_pair%d" % h, align_bytes=64) for h in range(2)]
         g2_w = {}
-        h_w = [keep.tile([P, J], U32, name="h_w%d" % b, align_bytes=64) for b in range(2)]
+        h_w = {1: keep.tile([P, J], U32, name="h_w1", align_bytes=64)}
         ha = {}
         h_s = [keep.tile([P, J], U8, name="h_s%d" % b, align_bytes=64) for b in range(2)]
 
@@ -104,10 +107,6 @@ def tile_list_kg_max_sig_kernel(
         def half_of(entries, h):
             return entries[:, h * HALF // 16 : (h + 1) * HALF // 16]
 
-        def gather_tab(h, tag):
-            g_w[h] = keep.tile([P, HALF], U32, name="g_w", tag=tag, align_bytes=64)
-            nc.vector.tensor_copy(g_w[h][:], tab_w[:].bitcast(U32).indirect(half_of(list1, h)))
-
         def gather_tab2(h):
             nc.vector.tensor_copy(g2_pair[h][:], tab2_w[:].bitcast(U32).indirect(half_of(list2, h)))
 
@@ -119,7 +118,7 @@ def tile_list_kg_max_sig_kernel(
             )
 
         def wb_views(a, b):
-            dst = wb_bf[a, b][:].rearrange("p (t g e i) -> p t g e i", t=PACK, e=8, i=PACK)
+            dst = wb_bf[a, b].rearrange("p (t g e i) -> p t g e i", t=PACK, e=8, i=PACK)
             src = wb_raw[a, b][:].rearrange("p i (g t e) -> p t g e i", t=PACK, e=8)
             return dst, src
 
@@ -132,8 +131,16 @@ def tile_list_kg_max_sig_kernel(
             for t in range(t0, t1):
                 nc.gpsimd.tensor_scalar(out=dst[:, t], in0=src[:, t], scalar1=1.0, scalar2=0.0, op0=MULT, op1=ADD)
 
-        def quantize_wb(a, b):
-            nc.vector.quantize_mx(out=wb_w[a, b][:].bitcast(FP8X4), scales=wb_s[a, b][:], in_=wb_bf[a, b][:])
+        def round_wb_on_vector(a, b, t0, t1):
+            dst, src = wb_views(a, b)
+            nc.vector.tensor_copy(out=dst[:, t0:t1], in_=src[:, t0:t1])
+
+        def quantize_wb0(a):
+            cols = slice(a * K_PASS, (a + 1) * K_PASS)
+            nc.vector.quantize_mx(out=wb_w[0][:, cols].bitcast(FP8X4), scales=wb_s[0][:, cols], in_=wb_bf[a, 0])
+
+        def quantize_wb1():
+            nc.vector.quantize_mx(out=wb_w[1][:].bitcast(FP8X4), scales=wb_s[1][:], in_=wb_bf1[:])
 
         def en_views(b):
             dst = en_bf[:, b * N * PACK : (b + 1) * N * PACK].rearrange("p (n t) -> p n t", t=PACK)
@@ -153,7 +160,6 @@ def tile_list_kg_max_sig_kernel(
             nc.vector.quantize_mx(out=en_w[:].bitcast(FP8X4), scales=en_s[:], in_=en_bf[:])
 
         def product_a(b, c):
-            h, j0 = divmod(c * CHUNK, HALF)
             bank = psum.tile([P, PACK, CHUNK], F32, name="bank_a", tag="bank%d" % c)
             for t in range(PACK):
                 cols = slice(t * 2 * P + b * P, t * 2 * P + (b + 1) * P)
@@ -161,7 +167,7 @@ def tile_list_kg_max_sig_kernel(
                     out=bank[:, t, :],
                     lhsT=wa_w[b][:, t * P : (t + 1) * P].bitcast(FP8X4),
                     lhsT_scale=wa_s[:, cols],
-                    rhs=g_w[h][:, j0 : j0 + CHUNK].bitcast(FP8X4),
+                    rhs=g_w[:, c * CHUNK : (c + 1) * CHUNK].bitcast(FP8X4),
                     rhs_scale=g_s[:, c * CHUNK : (c + 1) * CHUNK],
                     start=True,
                     stop=True,
@@ -172,12 +178,12 @@ def tile_list_kg_max_sig_kernel(
             h, j0 = divmod(c * CHUNK, HALF)
             bank = psum.tile([P, PACK, CHUNK], F32, name="bank_b", tag="bank%d" % c)
             for t in range(PACK):
-                cols = slice(t * P, (t + 1) * P)
                 for a in range(2):
+                    cols = slice(a * K_PASS + t * P, a * K_PASS + (t + 1) * P)
                     nc.tensor.matmul_mx(
                         out=bank[:, t, :],
-                        lhsT=wb_w[a, b][:, cols].bitcast(FP8X4),
-                        lhsT_scale=wb_s[a, b][:, cols],
+                        lhsT=wb_w[b][:, cols].bitcast(FP8X4),
+                        lhsT_scale=wb_s[b][:, cols],
                         rhs=g2_w[h][:, a, 2 * j0 : 2 * (j0 + CHUNK)].bitcast(FP4X4),
                         rhs_scale=g2_s[a][:, c * CHUNK : (c + 1) * CHUNK],
                         start=(a == 0),
@@ -243,11 +249,10 @@ def tile_list_kg_max_sig_kernel(
         load_words(tab2_w, tab2_words)
         load_wb(1, 0)
         nc.vector.tensor_copy(g_s[:], tab_s[:].indirect(list1[:]))
-        gather_tab(0, "g_w0")
-        gather_tab(1, "g_w1")
+        nc.vector.tensor_copy(g_w[:], tab_w[:].bitcast(U32).indirect(list1[:]))
         nc.vector.tensor_copy(g2_s[0][:], tab2_s[:].indirect(list2[:]))
-        nc.sync.dma_start(out=g2_s[1][: P - PARKED, :].bitcast(I32), in_=g2_s[0][PARKED:, :].bitcast(I32))
         load_wa(1)
+        nc.sync.dma_start(out=g2_s[1][: P - PARKED, :].bitcast(I32), in_=g2_s[0][PARKED:, :].bitcast(I32))
         load_wb(0, 1)
         load_wb(1, 1)
         load_en(0)
@@ -258,58 +263,48 @@ def tile_list_kg_max_sig_kernel(
         gather_tab2(0)
         gather_tab2(1)
         part(0, "g2_w0")
-        round_wb_on_scalar(0, 0, 0, 3)
-        round_wb_on_gpsimd(0, 0, 3, 4)
-        quantize_wb(0, 0)
+        round_wb_on_scalar(0, 0, 0, 4)
+        quantize_wb0(0)
         round_wb_on_scalar(1, 0, 0, 2)
-        round_wb_on_gpsimd(1, 0, 2, 4)
-        quantize_wb(1, 0)
+        round_wb_on_vector(1, 0, 2, 4)
+        order_wa(1, nc.vector)
+        quantize_wb0(1)
         part(1, "wb_bf10")
         copy_ha(0, 0, 3, room_for(3, "ha0"))
         copy_ha(0, 3, CHUNKS, room_for(5, "wb_raw10"))
-        order_wa(1, nc.gpsimd)
-        round_wb_on_scalar(0, 1, 0, 1)
-        round_wb_on_gpsimd(0, 1, 1, 4)
-        round_wb_on_scalar(1, 1, 0, 2)
-        round_wb_on_gpsimd(1, 1, 2, 4)
+        round_wb_on_gpsimd(0, 1, 0, 4)
+        round_wb_on_scalar(1, 1, 0, 4)
 
         def maxima(b, c0, count, h_bf):
             for s in range(count):
                 maximum(product_b(b, c0 + s), ha[b, c0 + s], h_bf, s)
             return c0, count, h_bf
 
-        h_bf_a = keep.tile([P, 4 * CHUNK * PACK], BF16, name="h_bf_a", align_bytes=64)
-        h_bf_b = keep.tile([P, 2 * CHUNK * PACK], BF16, name="h_bf_b", align_bytes=64)
-        run_a = maxima(0, 0, 4, h_bf_a[:])
-        quantize_wb(0, 1)
-        copy_ha(1, 0, 2, room_for(2, "wb_raw01"))
-        run_b = maxima(0, 4, 2, h_bf_b[:])
-        quantize_h(0, *run_a)
-        quantize_h(0, *run_b)
-        quantize_wb(1, 1)
-        late = room_for(7, "wb_raw11")
-        copy_ha(1, 2, 4, late[:, : 2 * CHUNK * PACK])
-        run_c = maxima(0, 6, 2, late[:, 6 * CHUNK * PACK :].bitcast(BF16))
-        copy_ha(1, 4, CHUNKS, late[:, 2 * CHUNK * PACK : 6 * CHUNK * PACK])
-        en_bf = keep.tile([P, 2 * N * PACK], BF16, name="en_bf", tag="wb_bf11", align_bytes=64)
+        first = keep.tile([P, J * PACK], BF16, name="first", align_bytes=64)
+        run_first = maxima(0, 0, CHUNKS, first[:])
+        quantize_wb1()
+        h_w[0] = keep.tile([P, J], U32, name="h_w0", tag="wb_bf1", align_bytes=64)
+        quantize_h(0, *run_first)
+        copy_ha(1, 0, 5, room_for(5, "wb_raw11"))
+        en_bf = keep.tile([P, 2 * N * PACK], BF16, name="en_bf", tag="first", align_bytes=64)
         round_en_on_gpsimd(0)
         round_en_on_scalar(1)
+        copy_ha(1, 5, CHUNKS, room_for(3, "en_raw1"))
 
-        waiting = []
+        waiting = None
         c0 = 0
         for run, count in enumerate(SECOND_RUNS):
-            tag = "wb_bf11" if run == 2 else "h_bf%d" % run
+            tag = "first" if run == 2 else "h_bf%d" % run
             h_bf = keep.tile([P, count * CHUNK * PACK], BF16, name="h_bf", tag=tag, align_bytes=64)
             done = maxima(1, c0, count, h_bf[:])
-            if run == 0:
-                quantize_h(0, *run_c)
-            else:
-                quantize_h(1, *waiting[-1])
+            if run > 0:
+                quantize_h(1, *waiting)
             if run == 1:
                 quantize_en()
-            if run >= 1:
-                score(*waiting[-1][:2])
-            waiting.append(done)
+            if run > 0:
+                for c in range(waiting[0], waiting[0] + waiting[1], 2):
+                    score(c, min(2, waiting[1]))
+            waiting = done
             c0 += count
-        quantize_h(1, *waiting[-1])
-        score(*waiting[-1][:2])
+        quantize_h(1, *waiting)
+        score(*waiting[:2])

@@ -22,7 +22,6 @@ HALF = J // 2
 CHUNK = 128
 CHUNKS = J // CHUNK
 PARKED = 16
-SECOND_RUNS = (4, 1, 1, 1, 1)
 SIGMOID = mybir.ActivationFunctionType.Sigmoid
 
 
@@ -47,7 +46,7 @@ def tile_list_kg_max_sig_kernel(
         warm = keep.tile([P, 2], F32, name="warm")
         wa_rows = wa_words[0].rearrange("p c i -> p (c i)").bitcast(I32)
         wa_w_raw = [keep.tile([P, K_PASS], I32, name="wa_w_raw%d" % b) for b in range(2)]
-        wa_w = [keep.tile([P, K_PASS], I32, name="wa_w%d" % b, align_bytes=64) for b in range(2)]
+        wa_w = {0: keep.tile([P, K_PASS], I32, name="wa_w0", align_bytes=64)}
         pieces = [(a, b) for b in range(2) for a in range(2)]
         wb_raw = {ab: keep.tile([P, PACK, K_PASS], F32, name="wb_raw%d%d" % ab, align_bytes=64) for ab in pieces}
         wb_bf = {(a, 0): keep.tile([P, PACK * K_PASS], BF16, name="wb_bf%d0" % a, align_bytes=64)[:] for a in range(2)}
@@ -143,7 +142,7 @@ def tile_list_kg_max_sig_kernel(
             nc.vector.quantize_mx(out=wb_w[1][:].bitcast(FP8X4), scales=wb_s[1][:], in_=wb_bf1[:])
 
         def en_views(b):
-            dst = en_bf[:, b * N * PACK : (b + 1) * N * PACK].rearrange("p (n t) -> p n t", t=PACK)
+            dst = en_bf[b][:].rearrange("p (n t) -> p n t", t=PACK)
             return dst, en_raw[b][:].rearrange("p t n -> p n t")
 
         def round_en_on_scalar(b):
@@ -156,8 +155,9 @@ def tile_list_kg_max_sig_kernel(
                 cols = slice(m * N // PACK, (m + 1) * N // PACK)
                 nc.gpsimd.tensor_scalar(out=dst[:, cols], in0=src[:, cols], scalar1=1.0, scalar2=0.0, op0=MULT, op1=ADD)
 
-        def quantize_en():
-            nc.vector.quantize_mx(out=en_w[:].bitcast(FP8X4), scales=en_s[:], in_=en_bf[:])
+        def quantize_en(b):
+            cols = slice(b * N, (b + 1) * N)
+            nc.vector.quantize_mx(out=en_w[:, cols].bitcast(FP8X4), scales=en_s[:, cols], in_=en_bf[b][:])
 
         def product_a(b, c):
             bank = psum.tile([P, PACK, CHUNK], F32, name="bank_a", tag="bank%d" % c)
@@ -190,6 +190,12 @@ def tile_list_kg_max_sig_kernel(
                         stop=(a == 1),
                     )
             return bank
+
+        def copy_rounded(bank, room, s):
+            nc.scalar.copy(
+                out=room[:, s * CHUNK * PACK : (s + 1) * CHUNK * PACK].rearrange("p (j t) -> p j t", t=PACK),
+                in_=bank[:].rearrange("p t j -> p j t"),
+            )
 
         def room_for(banks, tag):
             return keep.tile([P, banks * CHUNK * PACK], F32, name="room", tag=tag, align_bytes=64)
@@ -241,18 +247,18 @@ def tile_list_kg_max_sig_kernel(
         nc.sync.dma_start(list1[:], offs)
         nc.sync.dma_start(list2[:], offs2)
         load_scale_rows(nc.sync, tab_s, tab_scales[0])
-        load_wa(0)
-        load_words(tab_w, tab_words)
         load_tab2_scales()
-        load_wb(0, 0)
-        load_scale_rows(nc.sync, wa_s_raw, wa_scales[0])
+        load_words(tab_w, tab_words)
+        load_wa(0)
         load_words(tab2_w, tab2_words)
+        load_scale_rows(nc.sync, wa_s_raw, wa_scales[0])
+        load_wb(0, 0)
         load_wb(1, 0)
         nc.vector.tensor_copy(g_s[:], tab_s[:].indirect(list1[:]))
-        nc.vector.tensor_copy(g_w[:], tab_w[:].bitcast(U32).indirect(list1[:]))
         nc.vector.tensor_copy(g2_s[0][:], tab2_s[:].indirect(list2[:]))
-        load_wa(1)
+        nc.vector.tensor_copy(g_w[:], tab_w[:].bitcast(U32).indirect(list1[:]))
         nc.sync.dma_start(out=g2_s[1][: P - PARKED, :].bitcast(I32), in_=g2_s[0][PARKED:, :].bitcast(I32))
+        load_wa(1)
         load_wb(0, 1)
         load_wb(1, 1)
         load_en(0)
@@ -267,11 +273,12 @@ def tile_list_kg_max_sig_kernel(
         quantize_wb0(0)
         round_wb_on_scalar(1, 0, 0, 2)
         round_wb_on_vector(1, 0, 2, 4)
-        order_wa(1, nc.vector)
         quantize_wb0(1)
         part(1, "wb_bf10")
-        copy_ha(0, 0, 3, room_for(3, "ha0"))
-        copy_ha(0, 3, CHUNKS, room_for(5, "wb_raw10"))
+        wa_w[1] = keep.tile([P, K_PASS], I32, name="wa_w1", tag="wb_bf00", align_bytes=64)
+        order_wa(1, nc.vector)
+        copy_ha(0, 0, 2, room_for(2, "ha0"))
+        copy_ha(0, 2, CHUNKS, room_for(6, "wb_raw10"))
         round_wb_on_gpsimd(0, 1, 0, 4)
         round_wb_on_scalar(1, 1, 0, 4)
 
@@ -280,31 +287,38 @@ def tile_list_kg_max_sig_kernel(
                 maximum(product_b(b, c0 + s), ha[b, c0 + s], h_bf, s)
             return c0, count, h_bf
 
-        first = keep.tile([P, J * PACK], BF16, name="first", align_bytes=64)
-        run_first = maxima(0, 0, CHUNKS, first[:])
+        first = keep.tile([P, 6 * CHUNK * PACK], BF16, name="first", align_bytes=64)
+        maxima(0, 0, 6, first[:])
         quantize_wb1()
+        late = room_for(5, "wb_raw11")
+        run_last = maxima(0, 6, 2, late[:, 4 * CHUNK * PACK :].bitcast(BF16))
         h_w[0] = keep.tile([P, J], U32, name="h_w0", tag="wb_bf1", align_bytes=64)
-        quantize_h(0, *run_first)
-        copy_ha(1, 0, 5, room_for(5, "wb_raw11"))
-        en_bf = keep.tile([P, 2 * N * PACK], BF16, name="en_bf", tag="first", align_bytes=64)
+        quantize_h(0, 0, 4, first[:, : 4 * CHUNK * PACK])
+        quantize_h(0, 4, 2, first[:, 4 * CHUNK * PACK :])
+        quantize_h(0, *run_last)
+        copy_ha(1, 0, 4, late[:, : 4 * CHUNK * PACK])
+        en_bf = [keep.tile([P, N * PACK], BF16, name="en_bf", tag=tag, align_bytes=64) for tag in ("en_bf0", "first")]
         round_en_on_gpsimd(0)
-        round_en_on_scalar(1)
-        copy_ha(1, 5, CHUNKS, room_for(3, "en_raw1"))
-
-        waiting = None
-        c0 = 0
-        for run, count in enumerate(SECOND_RUNS):
-            tag = "first" if run == 2 else "h_bf%d" % run
-            h_bf = keep.tile([P, count * CHUNK * PACK], BF16, name="h_bf", tag=tag, align_bytes=64)
-            done = maxima(1, c0, count, h_bf[:])
-            if run > 0:
-                quantize_h(1, *waiting)
-            if run == 1:
-                quantize_en()
-            if run > 0:
-                for c in range(waiting[0], waiting[0] + waiting[1], 2):
-                    score(c, min(2, waiting[1]))
-            waiting = done
-            c0 += count
-        quantize_h(1, *waiting)
-        score(*waiting[:2])
+        round_en_on_gpsimd(1)
+        ha_late = keep.tile([P, HALF * PACK], BF16, name="ha_late", align_bytes=64)
+        hb_late = keep.tile([P, HALF * PACK], BF16, name="hb_late", align_bytes=64)
+        for s in range(4):
+            copy_rounded(product_a(1, 4 + s), ha_late, s)
+        h_early = keep.tile([P, HALF * PACK], BF16, name="h_early", align_bytes=64)
+        run_early = maxima(1, 0, 4, h_early[:])
+        for s in range(4):
+            copy_rounded(product_b(1, 4 + s), hb_late, s)
+        quantize_en(0)
+        quantize_h(1, *run_early)
+        quantize_en(1)
+        score(0, 2)
+        score(2, 2)
+        h_late = keep.tile([P, HALF * PACK], BF16, name="h_late", tag="first", align_bytes=64)
+        pairs = [slice(s * 2 * CHUNK * PACK, (s + 1) * 2 * CHUNK * PACK) for s in range(2)]
+        for pair in pairs:
+            nc.vector.tensor_tensor(out=h_late[:, pair], in0=ha_late[:, pair], in1=hb_late[:, pair], op=MAX)
+        quantize_h(1, 4, 2, h_late[:, pairs[0]])
+        score(4, 2)
+        for c in range(6, CHUNKS):
+            quantize_h(1, c, 1, h_late[:, (c - 4) * CHUNK * PACK : (c - 3) * CHUNK * PACK])
+            score(c, 1)

@@ -1,3 +1,4 @@
+import math
 from contextlib import ExitStack
 
 import concourse.mybir as mybir
@@ -21,7 +22,9 @@ K_PASS = P * PACK
 HALF = J // 2
 CHUNK = 128
 CHUNKS = J // CHUNK
+BANK = CHUNK * PACK
 PARKED = 16
+WIDTH = {F32: 4, I32: 4, U32: 4, BF16: 2, U8: 1}
 SIGMOID = mybir.ActivationFunctionType.Sigmoid
 
 
@@ -33,41 +36,46 @@ def tile_list_kg_max_sig_kernel(
         keep = ctx.enter_context(tc.tile_pool(name="keep", bufs=1))
         psum = ctx.enter_context(tc.psum_pool(name="psum", bufs=1))
 
-        list1 = keep.tile([P, J // 16], U16, name="list1")
-        list2 = keep.tile([P, J // 16], U16, name="list2")
-        tab_s = keep.tile([P, T], U8, name="tab_s")
-        tab2_s = keep.tile([P, T], U8, name="tab2_s")
-        wa_s_raw = keep.tile([P, R], U8, name="wa_s_raw")
-        tab_w = keep.tile([P, T], I32, name="tab_w")
-        tab2_w = keep.tile([P, T], I32, name="tab2_w")
-        g_s = keep.tile([P, J], U8, name="g_s", align_bytes=64)
-        g2_s = [keep.tile([P, J], U8, name="g2_s%d" % a, align_bytes=64) for a in range(2)]
-        wa_s = keep.tile([P, R], U8, name="wa_s", align_bytes=64)
-        warm = keep.tile([P, 2], F32, name="warm")
-        wa_rows = wa_words[0].rearrange("p c i -> p (c i)").bitcast(I32)
-        wa_w_raw = [keep.tile([P, K_PASS], I32, name="wa_w_raw%d" % b) for b in range(2)]
-        wa_w = {0: keep.tile([P, K_PASS], I32, name="wa_w0", align_bytes=64)}
-        pieces = [(a, b) for b in range(2) for a in range(2)]
-        wb_raw = {ab: keep.tile([P, PACK, K_PASS], F32, name="wb_raw%d%d" % ab, align_bytes=64) for ab in pieces}
-        wb_bf = {(a, 0): keep.tile([P, PACK * K_PASS], BF16, name="wb_bf%d0" % a, align_bytes=64)[:] for a in range(2)}
-        wb_bf1 = keep.tile([P, 2 * PACK * K_PASS], BF16, name="wb_bf1", align_bytes=64)
-        wb_w = [keep.tile([P, 2 * K_PASS], U32, name="wb_w%d" % b, align_bytes=64) for b in range(2)]
-        wb_s = [keep.tile([P, 2 * K_PASS], U8, name="wb_s%d" % b, align_bytes=64) for b in range(2)]
-        for a in range(2):
-            wb_bf[a, 1] = wb_bf1[:, a * PACK * K_PASS : (a + 1) * PACK * K_PASS]
-        en_raw = [keep.tile([P, PACK, N], F32, name="en_raw%d" % b, align_bytes=64) for b in range(2)]
-        en_w = keep.tile([P, 2 * N], U32, name="en_w", align_bytes=64)
-        en_s = keep.tile([P, 2 * N], U8, name="en_s", align_bytes=64)
-        g_w = keep.tile([P, J], U32, name="g_w", align_bytes=64)
-        g2_pair = [keep.tile([P, HALF], U32, name="g2_pair%d" % h, align_bytes=64) for h in range(2)]
-        g2_w = {}
-        h_w = {1: keep.tile([P, J], U32, name="h_w1", align_bytes=64)}
-        ha = {}
-        h_s = [keep.tile([P, J], U8, name="h_s%d" % b, align_bytes=64) for b in range(2)]
+        lists = ctx.enter_context(tc.tile_pool(name="lists", bufs=1))
+        place = {"end": 0}
 
-        def load_scale_rows(queue, plane, rows):
+        def buf(name, shape, dtype, after=None, shift=0, room=0):
+            if after is None:
+                place[name] = place["end"] + room
+                place["end"] = place[name] + math.prod(shape[1:]) * WIDTH[dtype] + room
+            else:
+                place[name] = place[after] + shift
+            return keep.tile(shape, dtype, name=name, align_bytes=64, offset=place[name])
+
+        list1 = lists.tile([P, J // 16], U16, name="list1")
+        list2 = lists.tile([P, J // 16], U16, name="list2")
+        tab_s = buf("tab_s", [P, T], U8)
+        tab2_s = buf("tab2_s", [P, T], U8, room=T // 2)
+        wa_s_raw = buf("wa_s_raw", [P, R], U8)
+        tab_w = buf("tab_w", [P, T], I32)
+        tab2_w = buf("tab2_w", [P, T], I32)
+        g_s = buf("g_s", [P, J], U8)
+        g2_s = [buf("g2_s%d" % a, [P, J], U8) for a in range(2)]
+        wa_s = buf("wa_s", [P, R], U8)
+        warm = lists.tile([P, 2], F32, name="warm")
+        wa_rows = wa_words[0].rearrange("p c i -> p (c i)").bitcast(I32)
+        wa_w_raw = [buf("wa_w_raw%d" % b, [P, K_PASS], I32) for b in range(2)]
+        wa_w = {}
+        pieces = [(a, b) for b in range(2) for a in range(2)]
+        wb_bf = {ab: buf("wb_bf%d%d" % ab, [P, PACK * K_PASS], BF16) for ab in pieces}
+        wb_s = {ab: buf("wb_s%d%d" % ab, [P, K_PASS], U8) for ab in pieces}
+        wb_w = {}
+        en_raw = [buf("en_raw%d" % b, [P, PACK, N], F32) for b in range(2)]
+        en_s = [buf("en_s%d" % b, [P, N], U8) for b in range(2)]
+        en_bf, en_w = {}, {}
+        g_w = buf("g_w", [P, J], U32)
+        g2_pair = {}
+        g2_w, h_w, ha, hb_bank = {}, {}, {}, {}
+        h_s = [buf("h_s%d" % b, [P, J], U8) for b in range(2)]
+
+        def load_scale_rows(plane, rows):
             for q in range(4):
-                queue.dma_start(
+                nc.sync.dma_start(
                     out=plane[32 * q : 32 * q + 4, :].bitcast(I32), in_=rows[4 * q : 4 * q + 4, :].bitcast(I32)
                 )
 
@@ -82,23 +90,27 @@ def tile_list_kg_max_sig_kernel(
         def load_wa(b):
             nc.sync.dma_start(out=wa_w_raw[b][:], in_=wa_rows[:, b * K_PASS : (b + 1) * K_PASS])
 
-        def load_wb(a, b):
-            rows = wb[a * K_PASS : (a + 1) * K_PASS, b * K_PASS : (b + 1) * K_PASS]
-            nc.sync.dma_start(out=wb_raw[a, b][:], in_=rows.rearrange("(p i) r -> p i r", i=PACK))
+        def load_wb(name, a, b, c0, c1):
+            raw = buf(name, [P, PACK, c1 - c0], F32)
+            rows = wb[a * K_PASS : (a + 1) * K_PASS, b * K_PASS + c0 : b * K_PASS + c1]
+            nc.sync.dma_start(out=raw[:], in_=rows.rearrange("(p i) r -> p i r", i=PACK))
+            dst = wb_bf[a, b][:].rearrange("p (t g e i) -> p t g e i", t=PACK, e=8, i=PACK)
+            return dst[:, :, c0 // 32 : c1 // 32], raw[:].rearrange("p i (g t e) -> p t g e i", t=PACK, e=8)
 
         def load_en(b):
             en_rows = en.rearrange("(b g t e) n -> b t g e n", b=2, t=PACK, e=8)
             for t in range(PACK):
                 nc.sync.dma_start(out=en_raw[b][:, t, :], in_=en_rows[b, t])
 
-        def order_wa(b, engine):
-            engine.tensor_copy(
+        def order_wa(b, after=None, shift=0):
+            wa_w[b] = buf("wa_w%d" % b, [P, K_PASS], I32, after, shift)
+            nc.gpsimd.tensor_copy(
                 out=wa_w[b][:].rearrange("p (t g e) -> p t g e", t=PACK, e=8),
                 in_=wa_w_raw[b][:].rearrange("p (g t e) -> p t g e", t=PACK, e=8),
             )
 
-        def order_wa_scales(engine):
-            engine.tensor_copy(
+        def order_wa_scales():
+            nc.gpsimd.tensor_copy(
                 out=wa_s[:].bitcast(I32).rearrange("p (t g e) -> p t g e", t=PACK, e=2),
                 in_=wa_s_raw[:].bitcast(I32).rearrange("p (g t e) -> p t g e", t=PACK, e=2),
             )
@@ -106,61 +118,40 @@ def tile_list_kg_max_sig_kernel(
         def half_of(entries, h):
             return entries[:, h * HALF // 16 : (h + 1) * HALF // 16]
 
-        def gather_tab2(h):
+        def gather_tab2(h, after=None, shift=0):
+            g2_pair[h] = buf("g2_pair%d" % h, [P, HALF], U32, after, shift)
             nc.vector.tensor_copy(g2_pair[h][:], tab2_w[:].bitcast(U32).indirect(half_of(list2, h)))
 
-        def part(h, tag):
-            g2_w[h] = keep.tile([P, 2, 2 * HALF], U8, name="g2_w", tag=tag, align_bytes=64)
+        def part(h, after=None):
+            g2_w[h] = buf("g2_w%d" % h, [P, 2, 2 * HALF], U8, after)
             nc.vector.tensor_copy(
                 out=g2_w[h][:].bitcast(U16),
                 in_=g2_pair[h][:].bitcast(U16).rearrange("p (j d) -> p d j", d=2),
             )
 
-        def wb_views(a, b):
-            dst = wb_bf[a, b].rearrange("p (t g e i) -> p t g e i", t=PACK, e=8, i=PACK)
-            src = wb_raw[a, b][:].rearrange("p i (g t e) -> p t g e i", t=PACK, e=8)
-            return dst, src
+        def round_on_gpsimd(dst, src):
+            nc.gpsimd.tensor_scalar(out=dst, in0=src, scalar1=1.0, scalar2=0.0, op0=MULT, op1=ADD)
 
-        def round_wb_on_scalar(a, b, t0, t1):
-            dst, src = wb_views(a, b)
-            nc.scalar.copy(out=dst[:, t0:t1], in_=src[:, t0:t1])
+        def quantize(codes, scales, values):
+            nc.vector.quantize_mx(out=codes.bitcast(FP8X4), scales=scales, in_=values)
 
-        def round_wb_on_gpsimd(a, b, t0, t1):
-            dst, src = wb_views(a, b)
-            for t in range(t0, t1):
-                nc.gpsimd.tensor_scalar(out=dst[:, t], in0=src[:, t], scalar1=1.0, scalar2=0.0, op0=MULT, op1=ADD)
+        def quantize_wb(a, b, after=None):
+            wb_w[a, b] = buf("wb_w%d%d" % (a, b), [P, K_PASS], U32, after)
+            quantize(wb_w[a, b][:], wb_s[a, b][:], wb_bf[a, b][:])
 
-        def round_wb_on_vector(a, b, t0, t1):
-            dst, src = wb_views(a, b)
-            nc.vector.tensor_copy(out=dst[:, t0:t1], in_=src[:, t0:t1])
+        def en_views(b, after=None):
+            en_bf[b] = buf("en_bf%d" % b, [P, N * PACK], BF16, after)
+            return en_bf[b][:].rearrange("p (n t) -> p n t", t=PACK), en_raw[b][:].rearrange("p t n -> p n t")
 
-        def quantize_wb0(a):
-            cols = slice(a * K_PASS, (a + 1) * K_PASS)
-            nc.vector.quantize_mx(out=wb_w[0][:, cols].bitcast(FP8X4), scales=wb_s[0][:, cols], in_=wb_bf[a, 0])
+        def quantize_en(b, after):
+            en_w[b] = buf("en_w%d" % b, [P, N], U32, after)
+            quantize(en_w[b][:], en_s[b][:], en_bf[b][:])
 
-        def quantize_wb1():
-            nc.vector.quantize_mx(out=wb_w[1][:].bitcast(FP8X4), scales=wb_s[1][:], in_=wb_bf1[:])
+        def woven(ap):
+            return ap.rearrange("p (j t) -> p j t", t=PACK)
 
-        def en_views(b):
-            dst = en_bf[b][:].rearrange("p (n t) -> p n t", t=PACK)
-            return dst, en_raw[b][:].rearrange("p t n -> p n t")
-
-        def round_en_on_scalar(b):
-            dst, src = en_views(b)
-            nc.scalar.copy(out=dst, in_=src)
-
-        def round_en_on_gpsimd(b):
-            dst, src = en_views(b)
-            for m in range(PACK):
-                cols = slice(m * N // PACK, (m + 1) * N // PACK)
-                nc.gpsimd.tensor_scalar(out=dst[:, cols], in0=src[:, cols], scalar1=1.0, scalar2=0.0, op0=MULT, op1=ADD)
-
-        def quantize_en(b):
-            cols = slice(b * N, (b + 1) * N)
-            nc.vector.quantize_mx(out=en_w[:, cols].bitcast(FP8X4), scales=en_s[:, cols], in_=en_bf[b][:])
-
-        def product_a(b, c):
-            bank = psum.tile([P, PACK, CHUNK], F32, name="bank_a", tag="bank%d" % c)
+        def product_a(b, c, k):
+            bank = psum.tile([P, PACK, CHUNK], F32, name="bank_a", tag="bank%d" % k)
             for t in range(PACK):
                 cols = slice(t * 2 * P + b * P, t * 2 * P + (b + 1) * P)
                 nc.tensor.matmul_mx(
@@ -172,69 +163,57 @@ def tile_list_kg_max_sig_kernel(
                     start=True,
                     stop=True,
                 )
-            return bank
+            return bank[:].rearrange("p t j -> p j t")
 
-        def product_b(b, c):
+        def copy_a(b, c, k, room):
+            ha[b, c] = room
+            nc.scalar.copy(out=woven(room), in_=product_a(b, c, k))
+
+        def pass_b(a, b, c, k=None):
             h, j0 = divmod(c * CHUNK, HALF)
-            bank = psum.tile([P, PACK, CHUNK], F32, name="bank_b", tag="bank%d" % c)
+            if a == 0:
+                hb_bank[b, c] = psum.tile([P, PACK, CHUNK], F32, name="bank_b", tag="bank%d" % k)
             for t in range(PACK):
-                for a in range(2):
-                    cols = slice(a * K_PASS + t * P, a * K_PASS + (t + 1) * P)
-                    nc.tensor.matmul_mx(
-                        out=bank[:, t, :],
-                        lhsT=wb_w[b][:, cols].bitcast(FP8X4),
-                        lhsT_scale=wb_s[b][:, cols],
-                        rhs=g2_w[h][:, a, 2 * j0 : 2 * (j0 + CHUNK)].bitcast(FP4X4),
-                        rhs_scale=g2_s[a][:, c * CHUNK : (c + 1) * CHUNK],
-                        start=(a == 0),
-                        stop=(a == 1),
-                    )
-            return bank
+                nc.tensor.matmul_mx(
+                    out=hb_bank[b, c][:, t, :],
+                    lhsT=wb_w[a, b][:, t * P : (t + 1) * P].bitcast(FP8X4),
+                    lhsT_scale=wb_s[a, b][:, t * P : (t + 1) * P],
+                    rhs=g2_w[h][:, a, 2 * j0 : 2 * (j0 + CHUNK)].bitcast(FP4X4),
+                    rhs_scale=g2_s[a][:, c * CHUNK : (c + 1) * CHUNK],
+                    start=(a == 0 and t == 0),
+                    stop=(a == 1 and t == PACK - 1),
+                )
 
-        def copy_rounded(bank, room, s):
-            nc.scalar.copy(
-                out=room[:, s * CHUNK * PACK : (s + 1) * CHUNK * PACK].rearrange("p (j t) -> p j t", t=PACK),
-                in_=bank[:].rearrange("p t j -> p j t"),
-            )
-
-        def room_for(banks, tag):
-            return keep.tile([P, banks * CHUNK * PACK], F32, name="room", tag=tag, align_bytes=64)
-
-        def copy_ha(b, c0, c1, room):
-            for c in range(c0, c1):
-                ha[b, c] = room[:, (c - c0) * CHUNK * PACK : (c - c0 + 1) * CHUNK * PACK].rearrange("p (j t) -> p j t", t=PACK)
-                nc.scalar.copy(out=ha[b, c], in_=product_a(b, c)[:].rearrange("p t j -> p j t"))
-
-        def maximum(bank, copied, h_bf, s):
+        def maximum(b, c, h_bf):
             nc.vector.tensor_tensor(
-                out=h_bf[:, s * CHUNK * PACK : (s + 1) * CHUNK * PACK].rearrange("p (j t) -> p j t", t=PACK),
-                in0=bank[:].rearrange("p t j -> p j t"),
-                in1=copied,
-                op=MAX,
+                out=woven(h_bf), in0=hb_bank[b, c][:].rearrange("p t j -> p j t"), in1=woven(ha[b, c]), op=MAX
             )
 
         def quantize_h(b, c0, count, h_bf):
             cols = slice(c0 * CHUNK, (c0 + count) * CHUNK)
-            nc.vector.quantize_mx(out=h_w[b][:, cols].bitcast(FP8X4), scales=h_s[b][:, cols], in_=h_bf)
+            quantize(h_w[b][:, cols], h_s[b][:, cols], h_bf)
 
-        def score(c0, count):
+        def score(c0, count, k):
             queries = slice(c0 * CHUNK, (c0 + count) * CHUNK)
-            bank = psum.tile([P, N // P, count * CHUNK], F32, name="bank_y", tag="bank%d" % c0)
+            bank = psum.tile([P, N // P, count * CHUNK], F32, name="bank_y", tag="bank%d" % k)
             for m in range(N // P):
                 for b in range(2):
-                    cols = slice(b * N + m * P, b * N + (m + 1) * P)
+                    cols = slice(m * P, (m + 1) * P)
                     nc.tensor.matmul_mx(
                         out=bank[:, m, :],
-                        lhsT=en_w[:, cols].bitcast(FP8X4),
-                        lhsT_scale=en_s[:, cols],
+                        lhsT=en_w[b][:, cols].bitcast(FP8X4),
+                        lhsT_scale=en_s[b][:, cols],
                         rhs=h_w[b][:, queries].bitcast(FP8X4),
                         rhs_scale=h_s[b][:, queries],
                         start=(b == 0),
                         stop=(b == 1),
                     )
-            result = keep.tile([P, N // P, count * CHUNK], F32, name="result%d" % c0)
+            result = buf("result%d" % c0, [P, N // P, count * CHUNK], F32)
             nc.scalar.activation(out=result[:], in_=bank[:], func=SIGMOID)
             nc.sync.dma_start(out=out[:, queries].rearrange("(m p) j -> p m j", p=P), in_=result[:])
+
+        def slot(tile, s, count=1):
+            return tile[:, s * BANK : (s + count) * BANK]
 
         nc.vector.memset(tab_s[:, : T // 2].bitcast(I32), 0)
         nc.gpsimd.memset(tab_s[:, T // 2 :].bitcast(I32), 0)
@@ -246,79 +225,93 @@ def tile_list_kg_max_sig_kernel(
 
         nc.sync.dma_start(list1[:], offs)
         nc.sync.dma_start(list2[:], offs2)
-        load_scale_rows(nc.sync, tab_s, tab_scales[0])
-        load_tab2_scales()
+        load_scale_rows(tab_s, tab_scales[0])
         load_words(tab_w, tab_words)
         load_wa(0)
+        load_scale_rows(wa_s_raw, wa_scales[0])
         load_words(tab2_w, tab2_words)
-        load_scale_rows(nc.sync, wa_s_raw, wa_scales[0])
-        load_wb(0, 0)
-        load_wb(1, 0)
-        nc.vector.tensor_copy(g_s[:], tab_s[:].indirect(list1[:]))
-        nc.vector.tensor_copy(g2_s[0][:], tab2_s[:].indirect(list2[:]))
-        nc.vector.tensor_copy(g_w[:], tab_w[:].bitcast(U32).indirect(list1[:]))
-        nc.sync.dma_start(out=g2_s[1][: P - PARKED, :].bitcast(I32), in_=g2_s[0][PARKED:, :].bitcast(I32))
+        load_tab2_scales()
         load_wa(1)
-        load_wb(0, 1)
-        load_wb(1, 1)
+        wb00 = load_wb("raw00", 0, 0, 0, K_PASS)
+        wb10a = load_wb("raw10a", 1, 0, 0, K_PASS // 2)
+        wb10b = load_wb("raw10b", 1, 0, K_PASS // 2, K_PASS)
+        wb01 = load_wb("raw01", 0, 1, 0, K_PASS)
+        nc.vector.tensor_copy(g_s[:], tab_s[:].indirect(list1[:]))
+        for h in range(2):
+            nc.vector.tensor_copy(g_w[:, h * HALF : (h + 1) * HALF], tab_w[:].bitcast(U32).indirect(half_of(list1, h)))
+        gather_tab2(0)
+        nc.vector.tensor_copy(g2_s[0][:], tab2_s[:].indirect(list2[:]))
+        nc.sync.dma_start(out=g2_s[1][: P - PARKED, :].bitcast(I32), in_=g2_s[0][PARKED:, :].bitcast(I32))
+        wb11 = load_wb("raw11", 1, 1, 0, K_PASS)
         load_en(0)
         load_en(1)
 
-        order_wa(0, nc.gpsimd)
-        order_wa_scales(nc.gpsimd)
-        gather_tab2(0)
-        gather_tab2(1)
-        part(0, "g2_w0")
-        round_wb_on_scalar(0, 0, 0, 4)
-        quantize_wb0(0)
-        round_wb_on_scalar(1, 0, 0, 2)
-        round_wb_on_vector(1, 0, 2, 4)
-        quantize_wb0(1)
+        order_wa(0)
+        order_wa_scales()
+        for c in range(4):
+            copy_a(0, c, c, buf("ha%d" % c, [P, BANK], F32)[:])
+        nc.scalar.copy(out=wb00[0], in_=wb00[1])
+        gather_tab2(1, "tab2_s", T // 2)
+        order_wa(1, "tab2_s", -T // 2)
+        nc.scalar.copy(out=wb10a[0], in_=wb10a[1])
+        part(0, "tab2_w")
+        nc.vector.tensor_copy(out=wb10b[0], in_=wb10b[1])
+        quantize_wb(0, 0, "raw10b")
+        quantize_wb(1, 0)
         part(1, "wb_bf10")
-        wa_w[1] = keep.tile([P, K_PASS], I32, name="wa_w1", tag="wb_bf00", align_bytes=64)
-        order_wa(1, nc.vector)
-        copy_ha(0, 0, 2, room_for(2, "ha0"))
-        copy_ha(0, 2, CHUNKS, room_for(6, "wb_raw10"))
-        round_wb_on_gpsimd(0, 1, 0, 4)
-        round_wb_on_scalar(1, 1, 0, 4)
-
-        def maxima(b, c0, count, h_bf):
-            for s in range(count):
-                maximum(product_b(b, c0 + s), ha[b, c0 + s], h_bf, s)
-            return c0, count, h_bf
-
-        first = keep.tile([P, 6 * CHUNK * PACK], BF16, name="first", align_bytes=64)
-        maxima(0, 0, 6, first[:])
-        quantize_wb1()
-        late = room_for(5, "wb_raw11")
-        run_last = maxima(0, 6, 2, late[:, 4 * CHUNK * PACK :].bitcast(BF16))
-        h_w[0] = keep.tile([P, J], U32, name="h_w0", tag="wb_bf1", align_bytes=64)
-        quantize_h(0, 0, 4, first[:, : 4 * CHUNK * PACK])
-        quantize_h(0, 4, 2, first[:, 4 * CHUNK * PACK :])
-        quantize_h(0, *run_last)
-        copy_ha(1, 0, 4, late[:, : 4 * CHUNK * PACK])
-        en_bf = [keep.tile([P, N * PACK], BF16, name="en_bf", tag=tag, align_bytes=64) for tag in ("en_bf0", "first")]
-        round_en_on_gpsimd(0)
-        round_en_on_gpsimd(1)
-        ha_late = keep.tile([P, HALF * PACK], BF16, name="ha_late", align_bytes=64)
-        hb_late = keep.tile([P, HALF * PACK], BF16, name="hb_late", align_bytes=64)
-        for s in range(4):
-            copy_rounded(product_a(1, 4 + s), ha_late, s)
-        h_early = keep.tile([P, HALF * PACK], BF16, name="h_early", align_bytes=64)
-        run_early = maxima(1, 0, 4, h_early[:])
-        for s in range(4):
-            copy_rounded(product_b(1, 4 + s), hb_late, s)
-        quantize_en(0)
-        quantize_h(1, *run_early)
-        quantize_en(1)
-        score(0, 2)
-        score(2, 2)
-        h_late = keep.tile([P, HALF * PACK], BF16, name="h_late", tag="first", align_bytes=64)
-        pairs = [slice(s * 2 * CHUNK * PACK, (s + 1) * 2 * CHUNK * PACK) for s in range(2)]
-        for pair in pairs:
-            nc.vector.tensor_tensor(out=h_late[:, pair], in0=ha_late[:, pair], in1=hb_late[:, pair], op=MAX)
-        quantize_h(1, 4, 2, h_late[:, pairs[0]])
-        score(4, 2)
-        for c in range(6, CHUNKS):
-            quantize_h(1, c, 1, h_late[:, (c - 4) * CHUNK * PACK : (c - 3) * CHUNK * PACK])
-            score(c, 1)
+        for c in range(4, 11):
+            copy_a(c // 8, c % 8, c % 8, buf("ha%d" % c, [P, BANK], BF16, "raw00", (c - 4) * 2 * BANK)[:])
+        h_first = buf("h_first", [P, CHUNKS * BANK], BF16)
+        for c in range(5):
+            pass_b(0, 0, c, 3 + c)
+            pass_b(1, 0, c)
+            maximum(0, c, slot(h_first, c))
+            if c == 1:
+                copy_a(1, 3, 0, buf("ha11", [P, BANK], BF16, "raw00", 7 * 2 * BANK)[:])
+        for t in range(PACK):
+            round_on_gpsimd(wb01[0][:, t], wb01[1][:, t])
+        for c in range(5, 8):
+            pass_b(0, 0, c, c - 2)
+            pass_b(1, 0, c)
+            maximum(0, c, slot(h_first, c))
+            if c == 6:
+                quantize_wb(0, 1, "ha6")
+        nc.scalar.copy(out=wb11[0], in_=wb11[1])
+        ha_late = buf("ha_late", [P, 4 * BANK], BF16, "raw11")
+        for s, k in enumerate((6, 7, 3, 4)):
+            copy_a(1, 4 + s, k, slot(ha_late, s))
+        quantize_wb(1, 1, "wb_bf01")
+        h_w[0] = buf("h_w0", [P, J], U32, "wb_bf11")
+        quantize_h(0, 0, CHUNKS, h_first[:])
+        for c, k in enumerate((1, 2, 0, 5)):
+            pass_b(0, 1, c, k)
+        dst, src = en_views(1)
+        nc.scalar.copy(out=dst, in_=src)
+        dst, src = en_views(0, "h_first")
+        for m in range(PACK):
+            cols = slice(m * N // PACK, (m + 1) * N // PACK)
+            round_on_gpsimd(dst[:, cols], src[:, cols])
+        h_early = buf("h_early", [P, 4 * BANK], BF16)
+        for c in range(4):
+            pass_b(1, 1, c)
+            maximum(1, c, slot(h_early, c))
+            if c == 1:
+                quantize_en(1, "ha9")
+        hb_late = buf("hb_late", [P, 4 * BANK], BF16, "en_raw1")
+        for s, k in enumerate((6, 7, 3, 4)):
+            pass_b(0, 1, 4 + s, k)
+            pass_b(1, 1, 4 + s)
+            nc.scalar.copy(out=woven(slot(hb_late, s)), in_=hb_bank[1, 4 + s][:].rearrange("p t j -> p j t"))
+        quantize_en(0, "ha11")
+        h_w[1] = buf("h_w1", [P, J], U32, "h_first")
+        quantize_h(1, 0, 4, h_early[:])
+        score(0, 2, 1)
+        score(2, 2, 2)
+        h_late = buf("h_late", [P, 4 * BANK], BF16, "h_early")
+        for s in (0, 2):
+            nc.vector.tensor_tensor(out=slot(h_late, s, 2), in0=slot(ha_late, s, 2), in1=slot(hb_late, s, 2), op=MAX)
+        quantize_h(1, 4, 2, slot(h_late, 0, 2))
+        score(4, 2, 0)
+        for c, k in ((6, 5), (7, 6)):
+            quantize_h(1, c, 1, slot(h_late, c - 4))
+            score(c, 1, k)

@@ -14,7 +14,7 @@ U16 = mybir.dt.uint16
 U8 = mybir.dt.uint8
 FP8X4 = mybir.dt.float8_e4m3fn_x4
 FP4X4 = mybir.dt.float4_e2m1fn_x4
-MULT, ADD, MAX = mybir.AluOpType.mult, mybir.AluOpType.add, mybir.AluOpType.max
+MAX = mybir.AluOpType.max
 
 P = 128
 PACK = 4
@@ -51,7 +51,7 @@ def tile_list_kg_max_sig_kernel(
         list2 = lists.tile([P, J // 16], U16, name="list2")
         tab_s = buf("tab_s", [P, T], U8)
         tab2_s = buf("tab2_s", [P, T], U8, room=T // 2)
-        wa_s_raw = buf("wa_s_raw", [P, R], U8)
+        wa_s_raw = buf("wa_s_raw", [P, R], U8, room=R)
         tab_w = buf("tab_w", [P, T], I32)
         tab2_w = buf("tab2_w", [P, T], I32)
         g_s = buf("g_s", [P, J], U8)
@@ -68,7 +68,7 @@ def tile_list_kg_max_sig_kernel(
         en_raw = [buf("en_raw%d" % b, [P, PACK, N], F32) for b in range(2)]
         en_s = [buf("en_s%d" % b, [P, N], U8) for b in range(2)]
         en_bf, en_w = {}, {}
-        g_w = buf("g_w", [P, J], U32)
+        g_w = {}
         g2_pair = {}
         g2_w, h_w, ha, hb_bank = {}, {}, {}, {}
         h_s = [buf("h_s%d" % b, [P, J], U8) for b in range(2)]
@@ -104,19 +104,23 @@ def tile_list_kg_max_sig_kernel(
 
         def order_wa(b, after=None, shift=0):
             wa_w[b] = buf("wa_w%d" % b, [P, K_PASS], I32, after, shift)
-            nc.gpsimd.tensor_copy(
+            nc.vector.tensor_copy(
                 out=wa_w[b][:].rearrange("p (t g e) -> p t g e", t=PACK, e=8),
                 in_=wa_w_raw[b][:].rearrange("p (g t e) -> p t g e", t=PACK, e=8),
             )
 
         def order_wa_scales():
-            nc.gpsimd.tensor_copy(
+            nc.vector.tensor_copy(
                 out=wa_s[:].bitcast(I32).rearrange("p (t g e) -> p t g e", t=PACK, e=2),
                 in_=wa_s_raw[:].bitcast(I32).rearrange("p (g t e) -> p t g e", t=PACK, e=2),
             )
 
         def half_of(entries, h):
             return entries[:, h * HALF // 16 : (h + 1) * HALF // 16]
+
+        def gather_tab(h, after=None):
+            g_w[h] = buf("g_w%d" % h, [P, HALF], U32, after)
+            nc.vector.tensor_copy(g_w[h][:], tab_w[:].bitcast(U32).indirect(half_of(list1, h)))
 
         def gather_tab2(h, after=None, shift=0):
             g2_pair[h] = buf("g2_pair%d" % h, [P, HALF], U32, after, shift)
@@ -128,9 +132,6 @@ def tile_list_kg_max_sig_kernel(
                 out=g2_w[h][:].bitcast(U16),
                 in_=g2_pair[h][:].bitcast(U16).rearrange("p (j d) -> p d j", d=2),
             )
-
-        def round_on_gpsimd(dst, src):
-            nc.gpsimd.tensor_scalar(out=dst, in0=src, scalar1=1.0, scalar2=0.0, op0=MULT, op1=ADD)
 
         def quantize(codes, scales, values):
             nc.vector.quantize_mx(out=codes.bitcast(FP8X4), scales=scales, in_=values)
@@ -158,7 +159,7 @@ def tile_list_kg_max_sig_kernel(
                     out=bank[:, t, :],
                     lhsT=wa_w[b][:, t * P : (t + 1) * P].bitcast(FP8X4),
                     lhsT_scale=wa_s[:, cols],
-                    rhs=g_w[:, c * CHUNK : (c + 1) * CHUNK].bitcast(FP8X4),
+                    rhs=g_w[c // 4][:, c % 4 * CHUNK : (c % 4 + 1) * CHUNK].bitcast(FP8X4),
                     rhs_scale=g_s[:, c * CHUNK : (c + 1) * CHUNK],
                     start=True,
                     stop=True,
@@ -237,8 +238,10 @@ def tile_list_kg_max_sig_kernel(
         wb10b = load_wb("raw10b", 1, 0, K_PASS // 2, K_PASS)
         wb01 = load_wb("raw01", 0, 1, 0, K_PASS)
         nc.vector.tensor_copy(g_s[:], tab_s[:].indirect(list1[:]))
-        for h in range(2):
-            nc.vector.tensor_copy(g_w[:, h * HALF : (h + 1) * HALF], tab_w[:].bitcast(U32).indirect(half_of(list1, h)))
+        gather_tab(0)
+        order_wa(0)
+        order_wa_scales()
+        gather_tab(1, "wa_s_raw")
         gather_tab2(0)
         nc.vector.tensor_copy(g2_s[0][:], tab2_s[:].indirect(list2[:]))
         nc.sync.dma_start(out=g2_s[1][: P - PARKED, :].bitcast(I32), in_=g2_s[0][PARKED:, :].bitcast(I32))
@@ -246,13 +249,11 @@ def tile_list_kg_max_sig_kernel(
         load_en(0)
         load_en(1)
 
-        order_wa(0)
-        order_wa_scales()
         for c in range(4):
             copy_a(0, c, c, buf("ha%d" % c, [P, BANK], F32)[:])
         nc.scalar.copy(out=wb00[0], in_=wb00[1])
-        gather_tab2(1, "tab2_s", T // 2)
         order_wa(1, "tab2_s", -T // 2)
+        gather_tab2(1, "tab2_s", T // 2)
         nc.scalar.copy(out=wb10a[0], in_=wb10a[1])
         part(0, "tab2_w")
         nc.vector.tensor_copy(out=wb10b[0], in_=wb10b[1])
@@ -268,8 +269,7 @@ def tile_list_kg_max_sig_kernel(
             maximum(0, c, slot(h_first, c))
             if c == 1:
                 copy_a(1, 3, 0, buf("ha11", [P, BANK], BF16, "raw00", 7 * 2 * BANK)[:])
-        for t in range(PACK):
-            round_on_gpsimd(wb01[0][:, t], wb01[1][:, t])
+        nc.vector.tensor_copy(out=wb01[0], in_=wb01[1])
         for c in range(5, 8):
             pass_b(0, 0, c, c - 2)
             pass_b(1, 0, c)
@@ -288,9 +288,7 @@ def tile_list_kg_max_sig_kernel(
         dst, src = en_views(1)
         nc.scalar.copy(out=dst, in_=src)
         dst, src = en_views(0, "h_first")
-        for m in range(PACK):
-            cols = slice(m * N // PACK, (m + 1) * N // PACK)
-            round_on_gpsimd(dst[:, cols], src[:, cols])
+        nc.vector.tensor_copy(out=dst, in_=src)
         h_early = buf("h_early", [P, 4 * BANK], BF16)
         for c in range(4):
             pass_b(1, 1, c)

@@ -140,8 +140,8 @@ def tile_list_kg_max_sig_kernel(
             wb_w[a, b] = buf("wb_w%d%d" % (a, b), [P, K_PASS], U32, after)
             quantize(wb_w[a, b][:], wb_s[a, b][:], wb_bf[a, b][:])
 
-        def en_views(b, after=None):
-            en_bf[b] = buf("en_bf%d" % b, [P, N * PACK], BF16, after)
+        def en_views(b):
+            en_bf[b] = buf("en_bf%d" % b, [P, N * PACK], BF16, room=N * PACK * 2 * b)
             return en_bf[b][:].rearrange("p (n t) -> p n t", t=PACK), en_raw[b][:].rearrange("p t n -> p n t")
 
         def quantize_en(b, after):
@@ -234,8 +234,7 @@ def tile_list_kg_max_sig_kernel(
         load_tab2_scales()
         load_wa(1)
         wb00 = load_wb("raw00", 0, 0, 0, K_PASS)
-        wb10a = load_wb("raw10a", 1, 0, 0, K_PASS // 2)
-        wb10b = load_wb("raw10b", 1, 0, K_PASS // 2, K_PASS)
+        wb10 = load_wb("raw10", 1, 0, 0, K_PASS)
         wb01 = load_wb("raw01", 0, 1, 0, K_PASS)
         nc.vector.tensor_copy(g_s[:], tab_s[:].indirect(list1[:]))
         gather_tab(0)
@@ -254,62 +253,55 @@ def tile_list_kg_max_sig_kernel(
         nc.scalar.copy(out=wb00[0], in_=wb00[1])
         order_wa(1, "tab2_s", -T // 2)
         gather_tab2(1, "tab2_s", T // 2)
-        nc.scalar.copy(out=wb10a[0], in_=wb10a[1])
+        nc.scalar.copy(out=wb10[0], in_=wb10[1])
         part(0, "tab2_w")
-        nc.vector.tensor_copy(out=wb10b[0], in_=wb10b[1])
-        quantize_wb(0, 0, "raw10b")
+        quantize_wb(0, 0, "g2_pair0")
+        part(1, "wb_bf00")
         quantize_wb(1, 0)
-        part(1, "wb_bf10")
-        for c in range(4, 11):
-            copy_a(c // 8, c % 8, c % 8, buf("ha%d" % c, [P, BANK], BF16, "raw00", (c - 4) * 2 * BANK)[:])
+        for c in range(4, 8):
+            copy_a(0, c, c, buf("ha%d" % c, [P, BANK], BF16, "raw10", (c - 4) * 2 * BANK)[:])
+        nc.scalar.copy(out=wb01[0], in_=wb01[1])
+        for c in range(3):
+            copy_a(1, c, c, buf("ha%d" % (8 + c), [P, BANK], BF16, "raw01", c * 2 * BANK)[:])
         h_first = buf("h_first", [P, CHUNKS * BANK], BF16)
-        for c in range(5):
-            pass_b(0, 0, c, 3 + c)
+        for c in range(CHUNKS):
+            pass_b(0, 0, c, 3 + c % 5)
             pass_b(1, 0, c)
             maximum(0, c, slot(h_first, c))
-            if c == 1:
-                copy_a(1, 3, 0, buf("ha11", [P, BANK], BF16, "raw00", 7 * 2 * BANK)[:])
-        nc.vector.tensor_copy(out=wb01[0], in_=wb01[1])
-        for c in range(5, 8):
-            pass_b(0, 0, c, c - 2)
-            pass_b(1, 0, c)
-            maximum(0, c, slot(h_first, c))
-            if c == 6:
-                quantize_wb(0, 1, "ha6")
+        copy_a(1, 3, 6, buf("ha11", [P, BANK], BF16, "raw01", 3 * 2 * BANK)[:])
+        quantize_wb(0, 1, "ha7")
         nc.scalar.copy(out=wb11[0], in_=wb11[1])
         ha_late = buf("ha_late", [P, 4 * BANK], BF16, "raw11")
-        for s, k in enumerate((6, 7, 3, 4)):
+        for s, k in enumerate((7, 3, 4, 5)):
             copy_a(1, 4 + s, k, slot(ha_late, s))
         quantize_wb(1, 1, "wb_bf01")
         h_w[0] = buf("h_w0", [P, J], U32, "wb_bf11")
         quantize_h(0, 0, CHUNKS, h_first[:])
-        for c, k in enumerate((1, 2, 0, 5)):
+        for c, k in enumerate((0, 1, 2, 6)):
             pass_b(0, 1, c, k)
-        dst, src = en_views(1)
-        nc.scalar.copy(out=dst, in_=src)
-        dst, src = en_views(0, "h_first")
-        nc.vector.tensor_copy(out=dst, in_=src)
+        for b in range(2):
+            dst, src = en_views(b)
+            nc.scalar.copy(out=dst, in_=src)
         h_early = buf("h_early", [P, 4 * BANK], BF16)
         for c in range(4):
             pass_b(1, 1, c)
             maximum(1, c, slot(h_early, c))
-            if c == 1:
-                quantize_en(1, "ha9")
         hb_late = buf("hb_late", [P, 4 * BANK], BF16, "en_raw1")
-        for s, k in enumerate((6, 7, 3, 4)):
+        for s, k in enumerate((7, 3, 4, 5)):
             pass_b(0, 1, 4 + s, k)
             pass_b(1, 1, 4 + s)
             nc.scalar.copy(out=woven(slot(hb_late, s)), in_=hb_bank[1, 4 + s][:].rearrange("p t j -> p j t"))
-        quantize_en(0, "ha11")
-        h_w[1] = buf("h_w1", [P, J], U32, "h_first")
+        quantize_en(0, "ha10")
+        quantize_en(1, "ha11")
+        h_w[1] = buf("h_w1", [P, J], U32, "en_bf1")
         quantize_h(1, 0, 4, h_early[:])
-        score(0, 2, 1)
-        score(2, 2, 2)
+        score(0, 2, 0)
+        score(2, 2, 1)
         h_late = buf("h_late", [P, 4 * BANK], BF16, "h_early")
         for s in (0, 2):
             nc.vector.tensor_tensor(out=slot(h_late, s, 2), in0=slot(ha_late, s, 2), in1=slot(hb_late, s, 2), op=MAX)
         quantize_h(1, 4, 2, slot(h_late, 0, 2))
-        score(4, 2, 0)
-        for c, k in ((6, 5), (7, 6)):
+        score(4, 2, 2)
+        for c, k in ((6, 6), (7, 7)):
             quantize_h(1, c, 1, slot(h_late, c - 4))
             score(c, 1, k)

@@ -94,8 +94,12 @@ def tile_list_kg_max_sig_kernel(
             raw = buf(name, [P, PACK, c1 - c0], F32)
             rows = wb[a * K_PASS : (a + 1) * K_PASS, b * K_PASS + c0 : b * K_PASS + c1]
             nc.sync.dma_start(out=raw[:], in_=rows.rearrange("(p i) r -> p i r", i=PACK))
-            dst = wb_bf[a, b][:].rearrange("p (t g e i) -> p t g e i", t=PACK, e=8, i=PACK)
-            return dst[:, :, c0 // 32 : c1 // 32], raw[:].rearrange("p i (g t e) -> p t g e i", t=PACK, e=8)
+            dst = wb_bf[a, b][:].rearrange("p (t g e u i) -> p t g e i u", t=PACK, e=4, u=2, i=PACK)
+            return dst[:, :, c0 // 32 : c1 // 32], raw[:].rearrange("p i (g t e u) -> p t g e i u", t=PACK, e=4, u=2)
+
+        def round_wb(piece):
+            for t in range(PACK):
+                nc.scalar.copy(out=piece[0][:, t], in_=piece[1][:, t])
 
         def load_en(b):
             en_rows = en.rearrange("(b g t e) n -> b t g e n", b=2, t=PACK, e=8)
@@ -142,7 +146,8 @@ def tile_list_kg_max_sig_kernel(
 
         def en_views(b):
             en_bf[b] = buf("en_bf%d" % b, [P, N * PACK], BF16, room=N * PACK * 2 * b)
-            return en_bf[b][:].rearrange("p (n t) -> p n t", t=PACK), en_raw[b][:].rearrange("p t n -> p n t")
+            dst = en_bf[b][:].rearrange("p (n u t) -> p n t u", u=2, t=PACK)
+            return dst, en_raw[b][:].rearrange("p t (n u) -> p n t u", u=2)
 
         def quantize_en(b, after):
             en_w[b] = buf("en_w%d" % b, [P, N], U32, after)
@@ -250,17 +255,17 @@ def tile_list_kg_max_sig_kernel(
 
         for c in range(4):
             copy_a(0, c, c, buf("ha%d" % c, [P, BANK], F32)[:])
-        nc.scalar.copy(out=wb00[0], in_=wb00[1])
+        round_wb(wb00)
         order_wa(1, "tab2_s", -T // 2)
         gather_tab2(1, "tab2_s", T // 2)
-        nc.scalar.copy(out=wb10[0], in_=wb10[1])
+        round_wb(wb10)
         part(0, "tab2_w")
         quantize_wb(0, 0, "g2_pair0")
         part(1, "wb_bf00")
         quantize_wb(1, 0)
         for c in range(4, 8):
             copy_a(0, c, c, buf("ha%d" % c, [P, BANK], BF16, "raw10", (c - 4) * 2 * BANK)[:])
-        nc.scalar.copy(out=wb01[0], in_=wb01[1])
+        round_wb(wb01)
         for c in range(3):
             copy_a(1, c, c, buf("ha%d" % (8 + c), [P, BANK], BF16, "raw01", c * 2 * BANK)[:])
         h_first = buf("h_first", [P, CHUNKS * BANK], BF16)
@@ -270,7 +275,7 @@ def tile_list_kg_max_sig_kernel(
             maximum(0, c, slot(h_first, c))
         copy_a(1, 3, 6, buf("ha11", [P, BANK], BF16, "raw01", 3 * 2 * BANK)[:])
         quantize_wb(0, 1, "ha7")
-        nc.scalar.copy(out=wb11[0], in_=wb11[1])
+        round_wb(wb11)
         ha_late = buf("ha_late", [P, 4 * BANK], BF16, "raw11")
         for s, k in enumerate((7, 3, 4, 5)):
             copy_a(1, 4 + s, k, slot(ha_late, s))

@@ -51,7 +51,7 @@ def tile_list_kg_max_sig_kernel(
         list2 = lists.tile([P, J // 16], U16, name="list2")
         tab_s = buf("tab_s", [P, T], U8)
         tab2_s = buf("tab2_s", [P, T], U8, room=T // 2)
-        wa_s_raw = buf("wa_s_raw", [P, R], U8, room=R)
+        wa_s_raw = buf("wa_s_raw", [P, R], U8)
         tab_w = buf("tab_w", [P, T], I32)
         tab2_w = buf("tab2_w", [P, T], I32)
         g_s = buf("g_s", [P, J], U8)
@@ -62,7 +62,7 @@ def tile_list_kg_max_sig_kernel(
         wa_w_raw = [buf("wa_w_raw%d" % b, [P, K_PASS], I32) for b in range(2)]
         wa_w = {}
         pieces = [(a, b) for b in range(2) for a in range(2)]
-        wb_bf = {ab: buf("wb_bf%d%d" % ab, [P, PACK * K_PASS], BF16) for ab in pieces}
+        wb_bf = {}
         wb_s = {ab: buf("wb_s%d%d" % ab, [P, K_PASS], U8) for ab in pieces}
         wb_w = {}
         en_raw = [buf("en_raw%d" % b, [P, PACK, N], F32) for b in range(2)]
@@ -90,16 +90,17 @@ def tile_list_kg_max_sig_kernel(
         def load_wa(b):
             nc.sync.dma_start(out=wa_w_raw[b][:], in_=wa_rows[:, b * K_PASS : (b + 1) * K_PASS])
 
-        def load_wb(name, a, b, c0, c1):
+        def load_wb(name, a, b, c0, c1, after=None):
+            wb_bf[a, b] = buf("wb_bf%d%d" % (a, b), [P, PACK * K_PASS], BF16, after)
             raw = buf(name, [P, PACK, c1 - c0], F32)
             rows = wb[a * K_PASS : (a + 1) * K_PASS, b * K_PASS + c0 : b * K_PASS + c1]
             nc.sync.dma_start(out=raw[:], in_=rows.rearrange("(p i) r -> p i r", i=PACK))
             dst = wb_bf[a, b][:].rearrange("p (t g e u i) -> p t g e i u", t=PACK, e=4, u=2, i=PACK)
             return dst[:, :, c0 // 32 : c1 // 32], raw[:].rearrange("p i (g t e u) -> p t g e i u", t=PACK, e=4, u=2)
 
-        def round_wb(piece):
-            for t in range(PACK):
-                nc.scalar.copy(out=piece[0][:, t], in_=piece[1][:, t])
+        def round_wb(copy, piece, t0=0, t1=PACK):
+            for t in range(t0, t1):
+                copy(out=piece[0][:, t], in_=piece[1][:, t])
 
         def load_en(b):
             en_rows = en.rearrange("(b g t e) n -> b t g e n", b=2, t=PACK, e=8)
@@ -108,13 +109,13 @@ def tile_list_kg_max_sig_kernel(
 
         def order_wa(b, after=None, shift=0):
             wa_w[b] = buf("wa_w%d" % b, [P, K_PASS], I32, after, shift)
-            nc.vector.tensor_copy(
+            nc.gpsimd.tensor_copy(
                 out=wa_w[b][:].rearrange("p (t g e) -> p t g e", t=PACK, e=8),
                 in_=wa_w_raw[b][:].rearrange("p (g t e) -> p t g e", t=PACK, e=8),
             )
 
         def order_wa_scales():
-            nc.vector.tensor_copy(
+            nc.gpsimd.tensor_copy(
                 out=wa_s[:].bitcast(I32).rearrange("p (t g e) -> p t g e", t=PACK, e=2),
                 in_=wa_s_raw[:].bitcast(I32).rearrange("p (g t e) -> p t g e", t=PACK, e=2),
             )
@@ -130,8 +131,8 @@ def tile_list_kg_max_sig_kernel(
             g2_pair[h] = buf("g2_pair%d" % h, [P, HALF], U32, after, shift)
             nc.vector.tensor_copy(g2_pair[h][:], tab2_w[:].bitcast(U32).indirect(half_of(list2, h)))
 
-        def part(h, after=None):
-            g2_w[h] = buf("g2_w%d" % h, [P, 2, 2 * HALF], U8, after)
+        def part(h, after, shift=0):
+            g2_w[h] = buf("g2_w%d" % h, [P, 2, 2 * HALF], U8, after, shift)
             nc.vector.tensor_copy(
                 out=g2_w[h][:].bitcast(U16),
                 in_=g2_pair[h][:].bitcast(U16).rearrange("p (j d) -> p d j", d=2),
@@ -230,22 +231,22 @@ def tile_list_kg_max_sig_kernel(
         nc.scalar.activation(out=warm[:, 1:2], in_=warm[:, 0:1], func=SIGMOID)
 
         nc.sync.dma_start(list1[:], offs)
-        nc.sync.dma_start(list2[:], offs2)
-        load_scale_rows(tab_s, tab_scales[0])
         load_words(tab_w, tab_words)
+        load_scale_rows(tab_s, tab_scales[0])
+        wb00 = load_wb("raw00", 0, 0, 0, K_PASS)
         load_wa(0)
+        nc.sync.dma_start(list2[:], offs2)
         load_scale_rows(wa_s_raw, wa_scales[0])
         load_words(tab2_w, tab2_words)
         load_tab2_scales()
         load_wa(1)
-        wb00 = load_wb("raw00", 0, 0, 0, K_PASS)
         wb10 = load_wb("raw10", 1, 0, 0, K_PASS)
         wb01 = load_wb("raw01", 0, 1, 0, K_PASS)
-        nc.vector.tensor_copy(g_s[:], tab_s[:].indirect(list1[:]))
         gather_tab(0)
+        nc.vector.tensor_copy(g_s[:], tab_s[:].indirect(list1[:]))
         order_wa(0)
+        gather_tab(1, "tab_s")
         order_wa_scales()
-        gather_tab(1, "wa_s_raw")
         gather_tab2(0)
         nc.vector.tensor_copy(g2_s[0][:], tab2_s[:].indirect(list2[:]))
         nc.sync.dma_start(out=g2_s[1][: P - PARKED, :].bitcast(I32), in_=g2_s[0][PARKED:, :].bitcast(I32))
@@ -253,36 +254,39 @@ def tile_list_kg_max_sig_kernel(
         load_en(0)
         load_en(1)
 
-        for c in range(4):
-            copy_a(0, c, c, buf("ha%d" % c, [P, BANK], F32)[:])
-        round_wb(wb00)
-        order_wa(1, "tab2_s", -T // 2)
+        round_wb(nc.scalar.copy, wb00)
+        quantize_wb(0, 0, "tab_w")
+        for c in range(5):
+            copy_a(0, c, c, buf("ha%d" % c, [P, BANK], BF16)[:])
+        order_wa(1)
+        part(0, "tab2_s", -T // 2)
         gather_tab2(1, "tab2_s", T // 2)
-        round_wb(wb10)
-        part(0, "tab2_w")
-        quantize_wb(0, 0, "g2_pair0")
-        part(1, "wb_bf00")
-        quantize_wb(1, 0)
-        for c in range(4, 8):
-            copy_a(0, c, c, buf("ha%d" % c, [P, BANK], BF16, "raw10", (c - 4) * 2 * BANK)[:])
-        round_wb(wb01)
-        for c in range(3):
-            copy_a(1, c, c, buf("ha%d" % (8 + c), [P, BANK], BF16, "raw01", c * 2 * BANK)[:])
+        for c in range(4):
+            pass_b(0, 0, c, c)
+        round_wb(nc.scalar.copy, wb10)
+        quantize_wb(1, 0, "tab2_w")
+        part(1, "wb_bf10")
+        for c in range(5, 8):
+            copy_a(0, c, c, buf("ha%d" % c, [P, BANK], BF16, "raw10", (c - 5) * 2 * BANK)[:])
+        round_wb(nc.scalar.copy, wb01)
         h_first = buf("h_first", [P, CHUNKS * BANK], BF16)
         for c in range(CHUNKS):
-            pass_b(0, 0, c, 3 + c % 5)
+            if c >= 4:
+                pass_b(0, 0, c, c % 5)
             pass_b(1, 0, c)
             maximum(0, c, slot(h_first, c))
-        copy_a(1, 3, 6, buf("ha11", [P, BANK], BF16, "raw01", 3 * 2 * BANK)[:])
+        for c, k in enumerate((5, 6, 7, 3)):
+            copy_a(1, c, k, buf("ha%d" % (8 + c), [P, BANK], BF16, "raw01", c * 2 * BANK)[:])
         quantize_wb(0, 1, "ha7")
-        round_wb(wb11)
-        ha_late = buf("ha_late", [P, 4 * BANK], BF16, "raw11")
-        for s, k in enumerate((7, 3, 4, 5)):
+        round_wb(nc.scalar.copy, wb11, 0, 2)
+        round_wb(nc.vector.tensor_copy, wb11, 2, 4)
+        ha_late = buf("ha_late", [P, 4 * BANK], BF16, "raw01", 4 * 2 * BANK)
+        for s, k in enumerate((4, 0, 1, 2)):
             copy_a(1, 4 + s, k, slot(ha_late, s))
         quantize_wb(1, 1, "wb_bf01")
         h_w[0] = buf("h_w0", [P, J], U32, "wb_bf11")
         quantize_h(0, 0, CHUNKS, h_first[:])
-        for c, k in enumerate((0, 1, 2, 6)):
+        for c, k in enumerate((5, 6, 7, 3)):
             pass_b(0, 1, c, k)
         for b in range(2):
             dst, src = en_views(b)
@@ -292,7 +296,7 @@ def tile_list_kg_max_sig_kernel(
             pass_b(1, 1, c)
             maximum(1, c, slot(h_early, c))
         hb_late = buf("hb_late", [P, 4 * BANK], BF16, "en_raw1")
-        for s, k in enumerate((7, 3, 4, 5)):
+        for s, k in enumerate((4, 0, 1, 2)):
             pass_b(0, 1, 4 + s, k)
             pass_b(1, 1, 4 + s)
             nc.scalar.copy(out=woven(slot(hb_late, s)), in_=hb_bank[1, 4 + s][:].rearrange("p t j -> p j t"))
@@ -300,13 +304,13 @@ def tile_list_kg_max_sig_kernel(
         quantize_en(1, "ha11")
         h_w[1] = buf("h_w1", [P, J], U32, "en_bf1")
         quantize_h(1, 0, 4, h_early[:])
-        score(0, 2, 0)
-        score(2, 2, 1)
+        score(0, 2, 5)
+        score(2, 2, 6)
         h_late = buf("h_late", [P, 4 * BANK], BF16, "h_early")
         for s in (0, 2):
             nc.vector.tensor_tensor(out=slot(h_late, s, 2), in0=slot(ha_late, s, 2), in1=slot(hb_late, s, 2), op=MAX)
         quantize_h(1, 4, 2, slot(h_late, 0, 2))
-        score(4, 2, 2)
-        for c, k in ((6, 6), (7, 7)):
+        score(4, 2, 7)
+        for c, k in ((6, 3), (7, 4)):
             quantize_h(1, c, 1, slot(h_late, c - 4))
             score(c, 1, k)

@@ -14,7 +14,7 @@ U16 = mybir.dt.uint16
 U8 = mybir.dt.uint8
 FP8X4 = mybir.dt.float8_e4m3fn_x4
 FP4X4 = mybir.dt.float4_e2m1fn_x4
-MAX = mybir.AluOpType.max
+MULT, ADD, MAX = mybir.AluOpType.mult, mybir.AluOpType.add, mybir.AluOpType.max
 
 P = 128
 PACK = 4
@@ -50,7 +50,7 @@ def tile_list_kg_max_sig_kernel(
         list1 = lists.tile([P, J // 16], U16, name="list1")
         list2 = lists.tile([P, J // 16], U16, name="list2")
         tab_s = buf("tab_s", [P, T], U8)
-        tab2_s = buf("tab2_s", [P, T], U8, room=T // 2)
+        tab2_s = buf("tab2_s", [P, T], U8, room=3 * T // 2)
         wa_s_raw = buf("wa_s_raw", [P, R], U8)
         tab_w = buf("tab_w", [P, T], I32)
         tab2_w = buf("tab2_w", [P, T], I32)
@@ -62,13 +62,12 @@ def tile_list_kg_max_sig_kernel(
         wa_w_raw = [buf("wa_w_raw%d" % b, [P, K_PASS], I32) for b in range(2)]
         wa_w = {}
         pieces = [(a, b) for b in range(2) for a in range(2)]
-        wb_bf = {}
+        wb_raw, wb_bf = {}, {}
         wb_s = {ab: buf("wb_s%d%d" % ab, [P, K_PASS], U8) for ab in pieces}
         wb_w = {}
         en_raw = [buf("en_raw%d" % b, [P, PACK, N], F32) for b in range(2)]
-        en_s = [buf("en_s%d" % b, [P, N], U8) for b in range(2)]
-        en_bf, en_w = {}, {}
-        g_w = {}
+        en_s = buf("en_s", [P, 2 * N], U8)
+        g_w = buf("g_w", [P, J], U32)
         g2_pair = {}
         g2_w, h_w, ha, hb_bank = {}, {}, {}, {}
         h_s = [buf("h_s%d" % b, [P, J], U8) for b in range(2)]
@@ -90,17 +89,21 @@ def tile_list_kg_max_sig_kernel(
         def load_wa(b):
             nc.sync.dma_start(out=wa_w_raw[b][:], in_=wa_rows[:, b * K_PASS : (b + 1) * K_PASS])
 
-        def load_wb(name, a, b, c0, c1, after=None):
-            wb_bf[a, b] = buf("wb_bf%d%d" % (a, b), [P, PACK * K_PASS], BF16, after)
-            raw = buf(name, [P, PACK, c1 - c0], F32)
-            rows = wb[a * K_PASS : (a + 1) * K_PASS, b * K_PASS + c0 : b * K_PASS + c1]
-            nc.sync.dma_start(out=raw[:], in_=rows.rearrange("(p i) r -> p i r", i=PACK))
-            dst = wb_bf[a, b][:].rearrange("p (t g e u i) -> p t g e i u", t=PACK, e=4, u=2, i=PACK)
-            return dst[:, :, c0 // 32 : c1 // 32], raw[:].rearrange("p i (g t e u) -> p t g e i u", t=PACK, e=4, u=2)
+        def load_wb(a, b):
+            wb_raw[a, b] = buf("raw%d%d" % (a, b), [P, PACK, K_PASS], F32)
+            rows = wb[a * K_PASS : (a + 1) * K_PASS, b * K_PASS : (b + 1) * K_PASS]
+            nc.sync.dma_start(out=wb_raw[a, b][:], in_=rows.rearrange("(p i) r -> p i r", i=PACK))
 
-        def round_wb(copy, piece, t0=0, t1=PACK):
-            for t in range(t0, t1):
-                copy(out=piece[0][:, t], in_=piece[1][:, t])
+        def round_wb(a, b, after=None, on_scalar=PACK):
+            wb_bf[a, b] = buf("wb_bf%d%d" % (a, b), [P, PACK * K_PASS], BF16, after)
+            dst = wb_bf[a, b][:].rearrange("p (t g e u i) -> p t g e i u", t=PACK, e=4, u=2, i=PACK)
+            src = wb_raw[a, b][:].rearrange("p i (g t e u) -> p t g e i u", t=PACK, e=4, u=2)
+            for t in range(on_scalar):
+                nc.scalar.copy(out=dst[:, t], in_=src[:, t])
+            dst = wb_bf[a, b][:].rearrange("p (t g e i) -> p t g e i", t=PACK, e=8, i=PACK)
+            src = wb_raw[a, b][:].rearrange("p i (g t e) -> p t g e i", t=PACK, e=8)
+            for t in range(on_scalar, PACK):
+                round_on_gpsimd(dst[:, t], src[:, t])
 
         def load_en(b):
             en_rows = en.rearrange("(b g t e) n -> b t g e n", b=2, t=PACK, e=8)
@@ -123,10 +126,6 @@ def tile_list_kg_max_sig_kernel(
         def half_of(entries, h):
             return entries[:, h * HALF // 16 : (h + 1) * HALF // 16]
 
-        def gather_tab(h, after=None):
-            g_w[h] = buf("g_w%d" % h, [P, HALF], U32, after)
-            nc.vector.tensor_copy(g_w[h][:], tab_w[:].bitcast(U32).indirect(half_of(list1, h)))
-
         def gather_tab2(h, after=None, shift=0):
             g2_pair[h] = buf("g2_pair%d" % h, [P, HALF], U32, after, shift)
             nc.vector.tensor_copy(g2_pair[h][:], tab2_w[:].bitcast(U32).indirect(half_of(list2, h)))
@@ -138,21 +137,19 @@ def tile_list_kg_max_sig_kernel(
                 in_=g2_pair[h][:].bitcast(U16).rearrange("p (j d) -> p d j", d=2),
             )
 
+        def round_on_gpsimd(dst, src):
+            nc.gpsimd.tensor_scalar(out=dst, in0=src, scalar1=1.0, scalar2=0.0, op0=MULT, op1=ADD)
+
         def quantize(codes, scales, values):
             nc.vector.quantize_mx(out=codes.bitcast(FP8X4), scales=scales, in_=values)
 
-        def quantize_wb(a, b, after=None):
-            wb_w[a, b] = buf("wb_w%d%d" % (a, b), [P, K_PASS], U32, after)
+        def quantize_wb(a, b, after=None, shift=0):
+            wb_w[a, b] = buf("wb_w%d%d" % (a, b), [P, K_PASS], U32, after, shift)
             quantize(wb_w[a, b][:], wb_s[a, b][:], wb_bf[a, b][:])
 
         def en_views(b):
-            en_bf[b] = buf("en_bf%d" % b, [P, N * PACK], BF16, room=N * PACK * 2 * b)
-            dst = en_bf[b][:].rearrange("p (n u t) -> p n t u", u=2, t=PACK)
+            dst = en_bf[:, b * N * PACK : (b + 1) * N * PACK].rearrange("p (n u t) -> p n t u", u=2, t=PACK)
             return dst, en_raw[b][:].rearrange("p t (n u) -> p n t u", u=2)
-
-        def quantize_en(b, after):
-            en_w[b] = buf("en_w%d" % b, [P, N], U32, after)
-            quantize(en_w[b][:], en_s[b][:], en_bf[b][:])
 
         def woven(ap):
             return ap.rearrange("p (j t) -> p j t", t=PACK)
@@ -165,7 +162,7 @@ def tile_list_kg_max_sig_kernel(
                     out=bank[:, t, :],
                     lhsT=wa_w[b][:, t * P : (t + 1) * P].bitcast(FP8X4),
                     lhsT_scale=wa_s[:, cols],
-                    rhs=g_w[c // 4][:, c % 4 * CHUNK : (c % 4 + 1) * CHUNK].bitcast(FP8X4),
+                    rhs=g_w[:, c * CHUNK : (c + 1) * CHUNK].bitcast(FP8X4),
                     rhs_scale=g_s[:, c * CHUNK : (c + 1) * CHUNK],
                     start=True,
                     stop=True,
@@ -205,11 +202,11 @@ def tile_list_kg_max_sig_kernel(
             bank = psum.tile([P, N // P, count * CHUNK], F32, name="bank_y", tag="bank%d" % k)
             for m in range(N // P):
                 for b in range(2):
-                    cols = slice(m * P, (m + 1) * P)
+                    cols = slice(b * N + m * P, b * N + (m + 1) * P)
                     nc.tensor.matmul_mx(
                         out=bank[:, m, :],
-                        lhsT=en_w[b][:, cols].bitcast(FP8X4),
-                        lhsT_scale=en_s[b][:, cols],
+                        lhsT=en_w[:, cols].bitcast(FP8X4),
+                        lhsT_scale=en_s[:, cols],
                         rhs=h_w[b][:, queries].bitcast(FP8X4),
                         rhs_scale=h_s[b][:, queries],
                         start=(b == 0),
@@ -233,29 +230,28 @@ def tile_list_kg_max_sig_kernel(
         nc.sync.dma_start(list1[:], offs)
         load_words(tab_w, tab_words)
         load_scale_rows(tab_s, tab_scales[0])
-        wb00 = load_wb("raw00", 0, 0, 0, K_PASS)
+        load_wb(0, 0)
         load_wa(0)
         nc.sync.dma_start(list2[:], offs2)
         load_scale_rows(wa_s_raw, wa_scales[0])
         load_words(tab2_w, tab2_words)
         load_tab2_scales()
         load_wa(1)
-        wb10 = load_wb("raw10", 1, 0, 0, K_PASS)
-        wb01 = load_wb("raw01", 0, 1, 0, K_PASS)
-        gather_tab(0)
+        load_wb(1, 0)
+        load_wb(0, 1)
+        nc.vector.tensor_copy(g_w[:], tab_w[:].bitcast(U32).indirect(list1[:]))
         nc.vector.tensor_copy(g_s[:], tab_s[:].indirect(list1[:]))
         order_wa(0)
-        gather_tab(1, "tab_s")
         order_wa_scales()
         gather_tab2(0)
         nc.vector.tensor_copy(g2_s[0][:], tab2_s[:].indirect(list2[:]))
         nc.sync.dma_start(out=g2_s[1][: P - PARKED, :].bitcast(I32), in_=g2_s[0][PARKED:, :].bitcast(I32))
-        wb11 = load_wb("raw11", 1, 1, 0, K_PASS)
+        load_wb(1, 1)
         load_en(0)
         load_en(1)
 
-        round_wb(nc.scalar.copy, wb00)
-        quantize_wb(0, 0, "tab_w")
+        round_wb(0, 0)
+        quantize_wb(0, 0)
         for c in range(5):
             copy_a(0, c, c, buf("ha%d" % c, [P, BANK], BF16)[:])
         order_wa(1)
@@ -263,12 +259,12 @@ def tile_list_kg_max_sig_kernel(
         gather_tab2(1, "tab2_s", T // 2)
         for c in range(4):
             pass_b(0, 0, c, c)
-        round_wb(nc.scalar.copy, wb10)
-        quantize_wb(1, 0, "tab2_w")
+        round_wb(1, 0)
+        quantize_wb(1, 0)
         part(1, "wb_bf10")
         for c in range(5, 8):
-            copy_a(0, c, c, buf("ha%d" % c, [P, BANK], BF16, "raw10", (c - 5) * 2 * BANK)[:])
-        round_wb(nc.scalar.copy, wb01)
+            copy_a(0, c, c, buf("ha%d" % c, [P, BANK], BF16, "raw10", (c - 4) * 2 * BANK)[:])
+        round_wb(0, 1, "g2_pair1", 1)
         h_first = buf("h_first", [P, CHUNKS * BANK], BF16)
         for c in range(CHUNKS):
             if c >= 4:
@@ -276,11 +272,10 @@ def tile_list_kg_max_sig_kernel(
             pass_b(1, 0, c)
             maximum(0, c, slot(h_first, c))
         for c, k in enumerate((5, 6, 7, 3)):
-            copy_a(1, c, k, buf("ha%d" % (8 + c), [P, BANK], BF16, "raw01", c * 2 * BANK)[:])
-        quantize_wb(0, 1, "ha7")
-        round_wb(nc.scalar.copy, wb11, 0, 2)
-        round_wb(nc.vector.tensor_copy, wb11, 2, 4)
-        ha_late = buf("ha_late", [P, 4 * BANK], BF16, "raw01", 4 * 2 * BANK)
+            copy_a(1, c, k, buf("ha%d" % (8 + c), [P, BANK], BF16, "raw10", (4 + c) * 2 * BANK)[:])
+        quantize_wb(0, 1, "ha5", -2 * BANK)
+        round_wb(1, 1)
+        ha_late = buf("ha_late", [P, 4 * BANK], BF16, "raw11")
         for s, k in enumerate((4, 0, 1, 2)):
             copy_a(1, 4 + s, k, slot(ha_late, s))
         quantize_wb(1, 1, "wb_bf01")
@@ -288,9 +283,13 @@ def tile_list_kg_max_sig_kernel(
         quantize_h(0, 0, CHUNKS, h_first[:])
         for c, k in enumerate((5, 6, 7, 3)):
             pass_b(0, 1, c, k)
-        for b in range(2):
-            dst, src = en_views(b)
-            nc.scalar.copy(out=dst, in_=src)
+        en_bf = buf("en_bf", [P, 2 * N * PACK], BF16, "h_first")
+        dst, src = en_views(1)
+        nc.scalar.copy(out=dst, in_=src)
+        dst = en_bf[:, : N * PACK].rearrange("p (n t) -> p n t", t=PACK)
+        src = en_raw[0][:].rearrange("p t n -> p n t")
+        for n0 in range(0, N, N // 2):
+            round_on_gpsimd(dst[:, n0 : n0 + N // 2], src[:, n0 : n0 + N // 2])
         h_early = buf("h_early", [P, 4 * BANK], BF16)
         for c in range(4):
             pass_b(1, 1, c)
@@ -300,13 +299,13 @@ def tile_list_kg_max_sig_kernel(
             pass_b(0, 1, 4 + s, k)
             pass_b(1, 1, 4 + s)
             nc.scalar.copy(out=woven(slot(hb_late, s)), in_=hb_bank[1, 4 + s][:].rearrange("p t j -> p j t"))
-        quantize_en(0, "ha10")
-        quantize_en(1, "ha11")
-        h_w[1] = buf("h_w1", [P, J], U32, "en_bf1")
+        en_w = buf("en_w", [P, 2 * N], U32, "ha9")
+        quantize(en_w[:], en_s[:], en_bf[:])
+        h_w[1] = buf("h_w1", [P, J], U32, "en_bf")
         quantize_h(1, 0, 4, h_early[:])
         score(0, 2, 5)
         score(2, 2, 6)
-        h_late = buf("h_late", [P, 4 * BANK], BF16, "h_early")
+        h_late = buf("h_late", [P, 4 * BANK], BF16)
         for s in (0, 2):
             nc.vector.tensor_tensor(out=slot(h_late, s, 2), in0=slot(ha_late, s, 2), in1=slot(hb_late, s, 2), op=MAX)
         quantize_h(1, 4, 2, slot(h_late, 0, 2))

@@ -24,6 +24,7 @@ CHUNK = 128
 CHUNKS = J // CHUNK
 BANK = CHUNK * PACK
 PARKED = 16
+TAB_ROW, WA_ROW = 4, 8
 WIDTH = {F32: 4, I32: 4, U32: 4, BF16: 2, U8: 1}
 SIGMOID = mybir.ActivationFunctionType.Sigmoid
 
@@ -69,14 +70,13 @@ def tile_list_kg_max_sig_kernel(
         en_s = buf("en_s", [P, 2 * N], U8)
         g_w = buf("g_w", [P, J], U32)
         g2_pair = {}
-        g2_w, h_w, ha, hb_bank = {}, {}, {}, {}
+        g2_w, h_w, ha, hb_bank, y_bank = {}, {}, {}, {}, {}
         h_s = [buf("h_s%d" % b, [P, J], U8) for b in range(2)]
 
-        def load_scale_rows(plane, rows):
-            for q in range(4):
-                nc.sync.dma_start(
-                    out=plane[32 * q : 32 * q + 4, :].bitcast(I32), in_=rows[4 * q : 4 * q + 4, :].bitcast(I32)
-                )
+        def load_scale_rows(plane, first, rows):
+            by_row = rows.bitcast(I32).rearrange("(q r) c -> r q c", r=4)
+            for r in range(4):
+                nc.sync.dma_start(out=plane[first + r : P : 32, :].bitcast(I32), in_=by_row[r])
 
         def load_tab2_scales():
             rows = tab2_scales.bitcast(I32).rearrange("a (q r) c -> r q a c", r=4)
@@ -161,9 +161,9 @@ def tile_list_kg_max_sig_kernel(
                 nc.tensor.matmul_mx(
                     out=bank[:, t, :],
                     lhsT=wa_w[b][:, t * P : (t + 1) * P].bitcast(FP8X4),
-                    lhsT_scale=wa_s[:, cols],
+                    lhsT_scale=wa_s[WA_ROW:, cols],
                     rhs=g_w[:, c * CHUNK : (c + 1) * CHUNK].bitcast(FP8X4),
-                    rhs_scale=g_s[:, c * CHUNK : (c + 1) * CHUNK],
+                    rhs_scale=g_s[TAB_ROW:, c * CHUNK : (c + 1) * CHUNK],
                     start=True,
                     stop=True,
                 )
@@ -197,24 +197,28 @@ def tile_list_kg_max_sig_kernel(
             cols = slice(c0 * CHUNK, (c0 + count) * CHUNK)
             quantize(h_w[b][:, cols], h_s[b][:, cols], h_bf)
 
-        def score(c0, count, k):
+        def score_pass(b, c0, count, k=None):
             queries = slice(c0 * CHUNK, (c0 + count) * CHUNK)
-            bank = psum.tile([P, N // P, count * CHUNK], F32, name="bank_y", tag="bank%d" % k)
+            if b == 0:
+                y_bank[c0] = psum.tile([P, N // P, count * CHUNK], F32, name="bank_y", tag="bank%d" % k)
             for m in range(N // P):
-                for b in range(2):
-                    cols = slice(b * N + m * P, b * N + (m + 1) * P)
-                    nc.tensor.matmul_mx(
-                        out=bank[:, m, :],
-                        lhsT=en_w[:, cols].bitcast(FP8X4),
-                        lhsT_scale=en_s[:, cols],
-                        rhs=h_w[b][:, queries].bitcast(FP8X4),
-                        rhs_scale=h_s[b][:, queries],
-                        start=(b == 0),
-                        stop=(b == 1),
-                    )
+                cols = slice(b * N + m * P, b * N + (m + 1) * P)
+                nc.tensor.matmul_mx(
+                    out=y_bank[c0][:, m, :],
+                    lhsT=en_w[:, cols].bitcast(FP8X4),
+                    lhsT_scale=en_s[:, cols],
+                    rhs=h_w[b][:, queries].bitcast(FP8X4),
+                    rhs_scale=h_s[b][:, queries],
+                    start=(b == 0 and m == 0),
+                    stop=(b == 1 and m == N // P - 1),
+                )
+
+        def finish(c0, count, queue):
+            score_pass(1, c0, count)
+            queries = slice(c0 * CHUNK, (c0 + count) * CHUNK)
             result = buf("result%d" % c0, [P, N // P, count * CHUNK], F32)
-            nc.scalar.activation(out=result[:], in_=bank[:], func=SIGMOID)
-            nc.sync.dma_start(out=out[:, queries].rearrange("(m p) j -> p m j", p=P), in_=result[:])
+            nc.scalar.activation(out=result[:], in_=y_bank[c0][:], func=SIGMOID)
+            queue.dma_start(out=out[:, queries].rearrange("(m p) j -> p m j", p=P), in_=result[:])
 
         def slot(tile, s, count=1):
             return tile[:, s * BANK : (s + count) * BANK]
@@ -229,11 +233,11 @@ def tile_list_kg_max_sig_kernel(
 
         nc.sync.dma_start(list1[:], offs)
         load_words(tab_w, tab_words)
-        load_scale_rows(tab_s, tab_scales[0])
+        load_scale_rows(tab_s, TAB_ROW, tab_scales[0])
         load_wb(0, 0)
         load_wa(0)
         nc.sync.dma_start(list2[:], offs2)
-        load_scale_rows(wa_s_raw, wa_scales[0])
+        load_scale_rows(wa_s_raw, WA_ROW, wa_scales[0])
         load_words(tab2_w, tab2_words)
         load_tab2_scales()
         load_wa(1)
@@ -303,13 +307,17 @@ def tile_list_kg_max_sig_kernel(
         quantize(en_w[:], en_s[:], en_bf[:])
         h_w[1] = buf("h_w1", [P, J], U32, "en_bf")
         quantize_h(1, 0, 4, h_early[:])
-        score(0, 2, 5)
-        score(2, 2, 6)
+        for c0, k in ((0, 5), (2, 6)):
+            score_pass(0, c0, 2, k)
+        for c0 in (0, 2):
+            finish(c0, 2, nc.sync)
+        for c0, count, k in ((4, 2, 7), (6, 1, 3), (7, 1, 4)):
+            score_pass(0, c0, count, k)
         h_late = buf("h_late", [P, 4 * BANK], BF16)
         for s in (0, 2):
             nc.vector.tensor_tensor(out=slot(h_late, s, 2), in0=slot(ha_late, s, 2), in1=slot(hb_late, s, 2), op=MAX)
         quantize_h(1, 4, 2, slot(h_late, 0, 2))
-        score(4, 2, 7)
-        for c, k in ((6, 3), (7, 4)):
+        finish(4, 2, nc.sync)
+        for c in (6, 7):
             quantize_h(1, c, 1, slot(h_late, c - 4))
-            score(c, 1, k)
+            finish(c, 1, nc.scalar if c == 7 else nc.sync)

@@ -278,11 +278,11 @@ def tile_list_kg_max_sig_kernel(
         for c, k in enumerate((5, 6, 7, 3)):
             copy_a(1, c, k, buf("ha%d" % (8 + c), [P, BANK], BF16, "raw10", (4 + c) * 2 * BANK)[:])
         quantize_wb(0, 1, "ha5", -2 * BANK)
-        round_wb(1, 1)
-        ha_late = buf("ha_late", [P, 4 * BANK], BF16, "raw11")
+        round_wb(1, 1, None, 3)
+        ha_late = buf("ha_late", [P, 4 * BANK], BF16)
         for s, k in enumerate((4, 0, 1, 2)):
             copy_a(1, 4 + s, k, slot(ha_late, s))
-        quantize_wb(1, 1, "wb_bf01")
+        quantize_wb(1, 1)
         h_w[0] = buf("h_w0", [P, J], U32, "wb_bf11")
         quantize_h(0, 0, CHUNKS, h_first[:])
         for c, k in enumerate((5, 6, 7, 3)):

@@ -15,6 +15,8 @@ U8 = mybir.dt.uint8
 FP8X4 = mybir.dt.float8_e4m3fn_x4
 FP4X4 = mybir.dt.float4_e2m1fn_x4
 MULT, ADD, MAX = mybir.AluOpType.mult, mybir.AluOpType.add, mybir.AluOpType.max
+SIGMOID = mybir.ActivationFunctionType.Sigmoid
+BYTES_OF = {F32: 4, I32: 4, U32: 4, BF16: 2, U8: 1}
 
 P = 128
 PACK = 4
@@ -23,10 +25,15 @@ HALF = J // 2
 CHUNK = 128
 CHUNKS = J // CHUNK
 BANK = CHUNK * PACK
+BANK_BYTES = 2 * BANK
+BANKS = 8
 PARKED = 16
 TAB_ROW, WA_ROW = 4, 8
-WIDTH = {F32: 4, I32: 4, U32: 4, BF16: 2, U8: 1}
-SIGMOID = mybir.ActivationFunctionType.Sigmoid
+RING = 5
+HA_AHEAD = 5
+AHEAD = 4
+DIRECT = 4
+ON_SCALAR = {(0, 0): 4, (1, 0): 4, (0, 1): 1, (1, 1): 3}
 
 
 def tile_list_kg_max_sig_kernel(
@@ -36,16 +43,15 @@ def tile_list_kg_max_sig_kernel(
     with ExitStack() as ctx:
         keep = ctx.enter_context(tc.tile_pool(name="keep", bufs=1))
         psum = ctx.enter_context(tc.psum_pool(name="psum", bufs=1))
-
         lists = ctx.enter_context(tc.tile_pool(name="lists", bufs=1))
         place = {"end": 0}
 
-        def buf(name, shape, dtype, after=None, shift=0, room=0):
-            if after is None:
+        def buf(name, shape, dtype, on=None, shift=0, room=0):
+            if on is None:
                 place[name] = place["end"] + room
-                place["end"] = place[name] + math.prod(shape[1:]) * WIDTH[dtype] + room
+                place["end"] = place[name] + math.prod(shape[1:]) * BYTES_OF[dtype] + room
             else:
-                place[name] = place[after] + shift
+                place[name] = place[on] + shift
             return keep.tile(shape, dtype, name=name, align_bytes=64, offset=place[name])
 
         list1 = lists.tile([P, J // 16], U16, name="list1")
@@ -59,59 +65,42 @@ def tile_list_kg_max_sig_kernel(
         g2_s = [buf("g2_s%d" % a, [P, J], U8) for a in range(2)]
         wa_s = buf("wa_s", [P, R], U8)
         warm = lists.tile([P, 2], F32, name="warm")
-        wa_rows = wa_words[0].rearrange("p c i -> p (c i)").bitcast(I32)
         wa_w_raw = [buf("wa_w_raw%d" % b, [P, K_PASS], I32) for b in range(2)]
-        wa_w = {}
-        pieces = [(a, b) for b in range(2) for a in range(2)]
-        wb_raw, wb_bf = {}, {}
-        wb_s = {ab: buf("wb_s%d%d" % ab, [P, K_PASS], U8) for ab in pieces}
-        wb_w = {}
+        wb_s = {(a, b): buf("wb_s%d%d" % (a, b), [P, K_PASS], U8) for b in range(2) for a in range(2)}
         en_raw = [buf("en_raw%d" % b, [P, PACK, N], F32) for b in range(2)]
         en_s = buf("en_s", [P, 2 * N], U8)
         g_w = buf("g_w", [P, J], U32)
-        g2_pair = {}
-        g2_w, h_w, ha, hb_bank, y_bank = {}, {}, {}, {}, {}
         h_s = [buf("h_s%d" % b, [P, J], U8) for b in range(2)]
+        wa_w, wb_raw, wb_bf, wb_w, g2_pair, g2_w, h_w, ha, hb_bank, y_bank = [{} for unused in range(10)]
 
         def load_scale_rows(plane, first, rows):
-            by_row = rows.bitcast(I32).rearrange("(q r) c -> r q c", r=4)
-            for r in range(4):
-                nc.sync.dma_start(out=plane[first + r : P : 32, :].bitcast(I32), in_=by_row[r])
+            by_row = rows.bitcast(I32).rearrange("(q s) c -> s q c", s=4)
+            for s in range(4):
+                nc.sync.dma_start(out=plane[first + s : P : 32, :].bitcast(I32), in_=by_row[s])
 
         def load_tab2_scales():
-            rows = tab2_scales.bitcast(I32).rearrange("a (q r) c -> r q a c", r=4)
-            for r in range(4):
-                nc.sync.dma_start(out=tab2_s[r:P:PARKED, :].bitcast(I32), in_=rows[r])
+            rows = tab2_scales.bitcast(I32).rearrange("a (q s) c -> s q a c", s=4)
+            for s in range(4):
+                nc.sync.dma_start(out=tab2_s[s:P:PARKED, :].bitcast(I32), in_=rows[s])
 
-        def load_words(words, packed):
-            nc.sync.dma_start(out=words[:], in_=packed[0].rearrange("p c i -> p (c i)").bitcast(I32))
+        def as_words(packed):
+            return packed[0].rearrange("p c i -> p (c i)").bitcast(I32)
 
         def load_wa(b):
-            nc.sync.dma_start(out=wa_w_raw[b][:], in_=wa_rows[:, b * K_PASS : (b + 1) * K_PASS])
+            nc.sync.dma_start(out=wa_w_raw[b][:], in_=as_words(wa_words)[:, b * K_PASS : (b + 1) * K_PASS])
 
         def load_wb(a, b):
-            wb_raw[a, b] = buf("raw%d%d" % (a, b), [P, PACK, K_PASS], F32)
+            wb_raw[a, b] = buf("wb_raw%d%d" % (a, b), [P, PACK, K_PASS], F32)
             rows = wb[a * K_PASS : (a + 1) * K_PASS, b * K_PASS : (b + 1) * K_PASS]
             nc.sync.dma_start(out=wb_raw[a, b][:], in_=rows.rearrange("(p i) r -> p i r", i=PACK))
 
-        def round_wb(a, b, after=None, on_scalar=PACK):
-            wb_bf[a, b] = buf("wb_bf%d%d" % (a, b), [P, PACK * K_PASS], BF16, after)
-            dst = wb_bf[a, b][:].rearrange("p (t g e u i) -> p t g e i u", t=PACK, e=4, u=2, i=PACK)
-            src = wb_raw[a, b][:].rearrange("p i (g t e u) -> p t g e i u", t=PACK, e=4, u=2)
-            for t in range(on_scalar):
-                nc.scalar.copy(out=dst[:, t], in_=src[:, t])
-            dst = wb_bf[a, b][:].rearrange("p (t g e i) -> p t g e i", t=PACK, e=8, i=PACK)
-            src = wb_raw[a, b][:].rearrange("p i (g t e) -> p t g e i", t=PACK, e=8)
-            for t in range(on_scalar, PACK):
-                round_on_gpsimd(dst[:, t], src[:, t])
-
         def load_en(b):
-            en_rows = en.rearrange("(b g t e) n -> b t g e n", b=2, t=PACK, e=8)
+            rows = en.rearrange("(b g t e) n -> b t g e n", b=2, t=PACK, e=8)
             for t in range(PACK):
-                nc.sync.dma_start(out=en_raw[b][:, t, :], in_=en_rows[b, t])
+                nc.sync.dma_start(out=en_raw[b][:, t, :], in_=rows[b, t])
 
-        def order_wa(b, after=None, shift=0):
-            wa_w[b] = buf("wa_w%d" % b, [P, K_PASS], I32, after, shift)
+        def order_wa(b):
+            wa_w[b] = buf("wa_w%d" % b, [P, K_PASS], I32)
             nc.gpsimd.tensor_copy(
                 out=wa_w[b][:].rearrange("p (t g e) -> p t g e", t=PACK, e=8),
                 in_=wa_w_raw[b][:].rearrange("p (g t e) -> p t g e", t=PACK, e=8),
@@ -126,12 +115,12 @@ def tile_list_kg_max_sig_kernel(
         def half_of(entries, h):
             return entries[:, h * HALF // 16 : (h + 1) * HALF // 16]
 
-        def gather_tab2(h, after=None, shift=0):
-            g2_pair[h] = buf("g2_pair%d" % h, [P, HALF], U32, after, shift)
+        def gather_tab2(h, on=None, shift=0):
+            g2_pair[h] = buf("g2_pair%d" % h, [P, HALF], U32, on, shift)
             nc.vector.tensor_copy(g2_pair[h][:], tab2_w[:].bitcast(U32).indirect(half_of(list2, h)))
 
-        def part(h, after, shift=0):
-            g2_w[h] = buf("g2_w%d" % h, [P, 2, 2 * HALF], U8, after, shift)
+        def part(h, on, shift=0):
+            g2_w[h] = buf("g2_w%d" % h, [P, 2, 2 * HALF], U8, on, shift)
             nc.vector.tensor_copy(
                 out=g2_w[h][:].bitcast(U16),
                 in_=g2_pair[h][:].bitcast(U16).rearrange("p (j d) -> p d j", d=2),
@@ -140,21 +129,41 @@ def tile_list_kg_max_sig_kernel(
         def round_on_gpsimd(dst, src):
             nc.gpsimd.tensor_scalar(out=dst, in0=src, scalar1=1.0, scalar2=0.0, op0=MULT, op1=ADD)
 
+        def round_wb(a, b, on=None):
+            wb_bf[a, b] = buf("wb_bf%d%d" % (a, b), [P, PACK * K_PASS], BF16, on)
+            dst = wb_bf[a, b][:].rearrange("p (t g e u i) -> p t g e i u", t=PACK, e=4, u=2, i=PACK)
+            src = wb_raw[a, b][:].rearrange("p i (g t e u) -> p t g e i u", t=PACK, e=4, u=2)
+            for t in range(ON_SCALAR[a, b]):
+                nc.scalar.copy(out=dst[:, t], in_=src[:, t])
+            dst = wb_bf[a, b][:].rearrange("p (t g e i) -> p t g e i", t=PACK, e=8, i=PACK)
+            src = wb_raw[a, b][:].rearrange("p i (g t e) -> p t g e i", t=PACK, e=8)
+            for t in range(ON_SCALAR[a, b], PACK):
+                round_on_gpsimd(dst[:, t], src[:, t])
+
         def quantize(codes, scales, values):
             nc.vector.quantize_mx(out=codes.bitcast(FP8X4), scales=scales, in_=values)
 
-        def quantize_wb(a, b, after=None, shift=0):
-            wb_w[a, b] = buf("wb_w%d%d" % (a, b), [P, K_PASS], U32, after, shift)
+        def quantize_wb(a, b, on=None, shift=0):
+            wb_w[a, b] = buf("wb_w%d%d" % (a, b), [P, K_PASS], U32, on, shift)
             quantize(wb_w[a, b][:], wb_s[a, b][:], wb_bf[a, b][:])
 
-        def en_views(b):
-            dst = en_bf[:, b * N * PACK : (b + 1) * N * PACK].rearrange("p (n u t) -> p n t u", u=2, t=PACK)
-            return dst, en_raw[b][:].rearrange("p t (n u) -> p n t u", u=2)
+        def quantize_h(b, c0, count, values):
+            cols = slice(c0 * CHUNK, (c0 + count) * CHUNK)
+            quantize(h_w[b][:, cols], h_s[b][:, cols], values)
 
-        def woven(ap):
-            return ap.rearrange("p (j t) -> p j t", t=PACK)
+        def by_query(values):
+            return values.rearrange("p (j t) -> p j t", t=PACK)
 
-        def product_a(b, c, k):
+        def bank_by_query(bank):
+            return bank[:].rearrange("p t j -> p j t")
+
+        def chunks_of(tile, s, count=1):
+            return tile[:, s * BANK : (s + count) * BANK]
+
+        def second_bank(c):
+            return RING + c if c < BANKS - RING else c % RING
+
+        def make_ha(b, c, k, values):
             bank = psum.tile([P, PACK, CHUNK], F32, name="bank_a", tag="bank%d" % k)
             for t in range(PACK):
                 cols = slice(t * 2 * P + b * P, t * 2 * P + (b + 1) * P)
@@ -167,13 +176,10 @@ def tile_list_kg_max_sig_kernel(
                     start=True,
                     stop=True,
                 )
-            return bank[:].rearrange("p t j -> p j t")
+            ha[b, c] = values
+            nc.scalar.copy(out=by_query(values), in_=bank_by_query(bank))
 
-        def copy_a(b, c, k, room):
-            ha[b, c] = room
-            nc.scalar.copy(out=woven(room), in_=product_a(b, c, k))
-
-        def pass_b(a, b, c, k=None):
+        def hb_pass(a, b, c, k=None):
             h, j0 = divmod(c * CHUNK, HALF)
             if a == 0:
                 hb_bank[b, c] = psum.tile([P, PACK, CHUNK], F32, name="bank_b", tag="bank%d" % k)
@@ -188,14 +194,10 @@ def tile_list_kg_max_sig_kernel(
                     stop=(a == 1 and t == PACK - 1),
                 )
 
-        def maximum(b, c, h_bf):
+        def maximum(b, c, values):
             nc.vector.tensor_tensor(
-                out=woven(h_bf), in0=hb_bank[b, c][:].rearrange("p t j -> p j t"), in1=woven(ha[b, c]), op=MAX
+                out=by_query(values), in0=bank_by_query(hb_bank[b, c]), in1=by_query(ha[b, c]), op=MAX
             )
-
-        def quantize_h(b, c0, count, h_bf):
-            cols = slice(c0 * CHUNK, (c0 + count) * CHUNK)
-            quantize(h_w[b][:, cols], h_s[b][:, cols], h_bf)
 
         def score_pass(b, c0, count, k=None):
             queries = slice(c0 * CHUNK, (c0 + count) * CHUNK)
@@ -213,15 +215,13 @@ def tile_list_kg_max_sig_kernel(
                     stop=(b == 1 and m == N // P - 1),
                 )
 
-        def finish(c0, count, queue):
+        def finish(c0, count, values, queue):
+            quantize_h(1, c0, count, values)
             score_pass(1, c0, count)
             queries = slice(c0 * CHUNK, (c0 + count) * CHUNK)
             result = buf("result%d" % c0, [P, N // P, count * CHUNK], F32)
             nc.scalar.activation(out=result[:], in_=y_bank[c0][:], func=SIGMOID)
             queue.dma_start(out=out[:, queries].rearrange("(m p) j -> p m j", p=P), in_=result[:])
-
-        def slot(tile, s, count=1):
-            return tile[:, s * BANK : (s + count) * BANK]
 
         nc.vector.memset(tab_s[:, : T // 2].bitcast(I32), 0)
         nc.gpsimd.memset(tab_s[:, T // 2 :].bitcast(I32), 0)
@@ -231,14 +231,14 @@ def tile_list_kg_max_sig_kernel(
         nc.gpsimd.memset(g2_s[1][:].bitcast(I32), 0)
         nc.scalar.activation(out=warm[:, 1:2], in_=warm[:, 0:1], func=SIGMOID)
 
+        nc.sync.dma_start(out=tab_w[:], in_=as_words(tab_words))
         nc.sync.dma_start(list1[:], offs)
-        load_words(tab_w, tab_words)
         load_scale_rows(tab_s, TAB_ROW, tab_scales[0])
         load_wb(0, 0)
         load_wa(0)
         nc.sync.dma_start(list2[:], offs2)
         load_scale_rows(wa_s_raw, WA_ROW, wa_scales[0])
-        load_words(tab2_w, tab2_words)
+        nc.sync.dma_start(out=tab2_w[:], in_=as_words(tab2_words))
         load_tab2_scales()
         load_wa(1)
         load_wb(1, 0)
@@ -248,76 +248,87 @@ def tile_list_kg_max_sig_kernel(
         order_wa(0)
         order_wa_scales()
         gather_tab2(0)
-        nc.vector.tensor_copy(g2_s[0][:], tab2_s[:].indirect(list2[:]))
-        nc.sync.dma_start(out=g2_s[1][: P - PARKED, :].bitcast(I32), in_=g2_s[0][PARKED:, :].bitcast(I32))
+        for h in range(2):
+            cols = slice(h * HALF, (h + 1) * HALF)
+            nc.vector.tensor_copy(g2_s[0][:, cols], tab2_s[:].indirect(half_of(list2, h)))
+            nc.sync.dma_start(out=g2_s[1][: P - PARKED, cols].bitcast(I32), in_=g2_s[0][PARKED:, cols].bitcast(I32))
         load_wb(1, 1)
         load_en(0)
         load_en(1)
 
         round_wb(0, 0)
         quantize_wb(0, 0)
-        for c in range(5):
-            copy_a(0, c, c, buf("ha%d" % c, [P, BANK], BF16)[:])
+        for c in range(HA_AHEAD):
+            make_ha(0, c, c, buf("ha0%d" % c, [P, BANK], BF16)[:])
         order_wa(1)
         part(0, "tab2_s", -T // 2)
         gather_tab2(1, "tab2_s", T // 2)
-        for c in range(4):
-            pass_b(0, 0, c, c)
+        for c in range(AHEAD):
+            hb_pass(0, 0, c, c % RING)
         round_wb(1, 0)
         quantize_wb(1, 0)
         part(1, "wb_bf10")
-        for c in range(5, 8):
-            copy_a(0, c, c, buf("ha%d" % c, [P, BANK], BF16, "raw10", (c - 4) * 2 * BANK)[:])
-        round_wb(0, 1, "g2_pair1", 1)
+        for c in range(HA_AHEAD, CHUNKS):
+            make_ha(0, c, c, buf("ha0%d" % c, [P, BANK], BF16, "wb_raw10", (c - HA_AHEAD + 1) * BANK_BYTES)[:])
+        round_wb(0, 1, "g2_pair1")
         h_first = buf("h_first", [P, CHUNKS * BANK], BF16)
         for c in range(CHUNKS):
-            if c >= 4:
-                pass_b(0, 0, c, c % 5)
-            pass_b(1, 0, c)
-            maximum(0, c, slot(h_first, c))
-        for c, k in enumerate((5, 6, 7, 3)):
-            copy_a(1, c, k, buf("ha%d" % (8 + c), [P, BANK], BF16, "raw10", (4 + c) * 2 * BANK)[:])
-        quantize_wb(0, 1, "ha5", -2 * BANK)
-        round_wb(1, 1, None, 3)
-        ha_late = buf("ha_late", [P, 4 * BANK], BF16)
-        for s, k in enumerate((4, 0, 1, 2)):
-            copy_a(1, 4 + s, k, slot(ha_late, s))
+            if c >= AHEAD:
+                hb_pass(0, 0, c, c % RING)
+            hb_pass(1, 0, c)
+            maximum(0, c, chunks_of(h_first, c))
+
+        for c in range(DIRECT):
+            make_ha(1, c, second_bank(c), buf("ha1%d" % c, [P, BANK], BF16, "wb_raw10", (DIRECT + c) * BANK_BYTES)[:])
+        quantize_wb(0, 1, "ha0%d" % HA_AHEAD, -BANK_BYTES)
+        round_wb(1, 1)
+        ha_late = buf("ha_late", [P, (CHUNKS - DIRECT) * BANK], BF16)
+        for c in range(DIRECT, CHUNKS):
+            make_ha(1, c, second_bank(c), chunks_of(ha_late, c - DIRECT))
         quantize_wb(1, 1)
         h_w[0] = buf("h_w0", [P, J], U32, "wb_bf11")
         quantize_h(0, 0, CHUNKS, h_first[:])
-        for c, k in enumerate((5, 6, 7, 3)):
-            pass_b(0, 1, c, k)
+        for c in range(DIRECT):
+            hb_pass(0, 1, c, second_bank(c))
         en_bf = buf("en_bf", [P, 2 * N * PACK], BF16, "h_first")
-        dst, src = en_views(1)
-        nc.scalar.copy(out=dst, in_=src)
+        nc.scalar.copy(
+            out=en_bf[:, N * PACK :].rearrange("p (n u t) -> p n t u", u=2, t=PACK),
+            in_=en_raw[1][:].rearrange("p t (n u) -> p n t u", u=2),
+        )
         dst = en_bf[:, : N * PACK].rearrange("p (n t) -> p n t", t=PACK)
         src = en_raw[0][:].rearrange("p t n -> p n t")
-        for n0 in range(0, N, N // 2):
-            round_on_gpsimd(dst[:, n0 : n0 + N // 2], src[:, n0 : n0 + N // 2])
-        h_early = buf("h_early", [P, 4 * BANK], BF16)
-        for c in range(4):
-            pass_b(1, 1, c)
-            maximum(1, c, slot(h_early, c))
-        hb_late = buf("hb_late", [P, 4 * BANK], BF16, "en_raw1")
-        for s, k in enumerate((4, 0, 1, 2)):
-            pass_b(0, 1, 4 + s, k)
-            pass_b(1, 1, 4 + s)
-            nc.scalar.copy(out=woven(slot(hb_late, s)), in_=hb_bank[1, 4 + s][:].rearrange("p t j -> p j t"))
-        en_w = buf("en_w", [P, 2 * N], U32, "ha9")
+        for n0 in range(0, N, P):
+            round_on_gpsimd(dst[:, n0 : n0 + P], src[:, n0 : n0 + P])
+        h_early = buf("h_early", [P, DIRECT * BANK], BF16)
+        for c in range(DIRECT):
+            hb_pass(1, 1, c)
+            maximum(1, c, chunks_of(h_early, c))
+        hb_late = buf("hb_late", [P, (CHUNKS - DIRECT) * BANK], BF16, "en_raw1")
+        for c in range(DIRECT, CHUNKS):
+            hb_pass(0, 1, c, second_bank(c))
+            hb_pass(1, 1, c)
+            nc.scalar.copy(out=by_query(chunks_of(hb_late, c - DIRECT)), in_=bank_by_query(hb_bank[1, c]))
+        en_w = buf("en_w", [P, 2 * N], U32, "ha11")
         quantize(en_w[:], en_s[:], en_bf[:])
+
         h_w[1] = buf("h_w1", [P, J], U32, "en_bf")
-        quantize_h(1, 0, 4, h_early[:])
-        for c0, k in ((0, 5), (2, 6)):
-            score_pass(0, c0, 2, k)
-        for c0 in (0, 2):
-            finish(c0, 2, nc.sync)
-        for c0, count, k in ((4, 2, 7), (6, 1, 3), (7, 1, 4)):
-            score_pass(0, c0, count, k)
-        h_late = buf("h_late", [P, 4 * BANK], BF16)
-        for s in (0, 2):
-            nc.vector.tensor_tensor(out=slot(h_late, s, 2), in0=slot(ha_late, s, 2), in1=slot(hb_late, s, 2), op=MAX)
-        quantize_h(1, 4, 2, slot(h_late, 0, 2))
-        finish(4, 2, nc.sync)
-        for c in (6, 7):
-            quantize_h(1, c, 1, slot(h_late, c - 4))
-            finish(c, 1, nc.scalar if c == 7 else nc.sync)
+        steps = [(0, 2), (2, 2), (4, 2), (6, 1), (7, 1)]
+        early_steps = DIRECT // 2
+        for s in range(early_steps):
+            score_pass(0, *steps[s], second_bank(s))
+        for c0, count in steps[:early_steps]:
+            finish(c0, count, chunks_of(h_early, c0, count), nc.sync)
+        for s in range(early_steps, len(steps)):
+            score_pass(0, *steps[s], second_bank(s))
+        h_late = buf("h_late", [P, (CHUNKS - DIRECT) * BANK], BF16)
+
+        def late_maximum(c0, count):
+            h_c, ha_c, hb_c = [chunks_of(tile, c0 - DIRECT, count) for tile in (h_late, ha_late, hb_late)]
+            nc.vector.tensor_tensor(out=h_c, in0=ha_c, in1=hb_c, op=MAX)
+
+        late = steps[early_steps:]
+        late_maximum(*late[0])
+        for s, (c0, count) in enumerate(late):
+            if s + 1 < len(late):
+                late_maximum(*late[s + 1])
+            finish(c0, count, chunks_of(h_late, c0 - DIRECT, count), nc.sync if s + 1 < len(late) else nc.scalar)

@@ -20,20 +20,17 @@ BYTES_OF = {F32: 4, I32: 4, U32: 4, BF16: 2, U8: 1}
 
 P = 128
 PACK = 4
+RUN = 4
 K_PASS = P * PACK
 HALF = J // 2
 CHUNK = 128
 CHUNKS = J // CHUNK
 BANK = CHUNK * PACK
 BANK_BYTES = 2 * BANK
-BANKS = 8
 PARKED = 16
 TAB_ROW, WA_ROW = 4, 8
-RING = 5
-HA_AHEAD = 5
 AHEAD = 4
 DIRECT = 4
-ON_SCALAR = {(0, 0): 4, (1, 0): 4, (0, 1): 1, (1, 1): 3}
 
 
 def tile_list_kg_max_sig_kernel(
@@ -56,68 +53,71 @@ def tile_list_kg_max_sig_kernel(
 
         list1 = lists.tile([P, J // 16], U16, name="list1")
         list2 = lists.tile([P, J // 16], U16, name="list2")
+        warm = lists.tile([P, 2], F32, name="warm")
         tab_s = buf("tab_s", [P, T], U8)
-        tab2_s = buf("tab2_s", [P, T], U8, room=3 * T // 2)
+        tab2_s = buf("tab2_s", [P, T], U8)
         wa_s_raw = buf("wa_s_raw", [P, R], U8)
         tab_w = buf("tab_w", [P, T], I32)
         tab2_w = buf("tab2_w", [P, T], I32)
+        wa_w_raw = buf("wa_w_raw", [P, R], I32)
+        wa_w = buf("wa_w", [P, R], I32)
+        wa_s = {}
         g_s = buf("g_s", [P, J], U8)
+        g_w = buf("g_w", [P, J], U32)
         g2_s = [buf("g2_s%d" % a, [P, J], U8) for a in range(2)]
-        wa_s = buf("wa_s", [P, R], U8)
-        warm = lists.tile([P, 2], F32, name="warm")
-        wa_w_raw = [buf("wa_w_raw%d" % b, [P, K_PASS], I32) for b in range(2)]
         wb_s = {(a, b): buf("wb_s%d%d" % (a, b), [P, K_PASS], U8) for b in range(2) for a in range(2)}
+        wb_raw = {(a, b): buf("wb_raw%d%d" % (a, b), [P, PACK, K_PASS], F32) for b in range(2) for a in range(2)}
         en_raw = [buf("en_raw%d" % b, [P, PACK, N], F32) for b in range(2)]
         en_s = buf("en_s", [P, 2 * N], U8)
-        g_w = buf("g_w", [P, J], U32)
         h_s = [buf("h_s%d" % b, [P, J], U8) for b in range(2)]
-        wa_w, wb_raw, wb_bf, wb_w, g2_pair, g2_w, h_w, ha, hb_bank, y_bank = [{} for unused in range(10)]
+        wb_bf, wb_w, g2_pair, g2_w, h_w, ha, hb_bank, y_bank = [{} for unused in range(8)]
 
-        def load_scale_rows(plane, first, rows):
+        def load_scale_rows(queues, plane, first, rows):
             by_row = rows.bitcast(I32).rearrange("(q s) c -> s q c", s=4)
             for s in range(4):
-                nc.sync.dma_start(out=plane[first + s : P : 32, :].bitcast(I32), in_=by_row[s])
+                queues[s].dma_start(out=plane[first + s : P : 32, :].bitcast(I32), in_=by_row[s])
 
-        def load_tab2_scales():
+        def load_tab2_scales(queues):
             rows = tab2_scales.bitcast(I32).rearrange("a (q s) c -> s q a c", s=4)
             for s in range(4):
-                nc.sync.dma_start(out=tab2_s[s:P:PARKED, :].bitcast(I32), in_=rows[s])
+                queues[s].dma_start(out=tab2_s[s:P:PARKED, :].bitcast(I32), in_=rows[s])
 
         def as_words(packed):
             return packed[0].rearrange("p c i -> p (c i)").bitcast(I32)
 
-        def load_wa(b):
-            nc.sync.dma_start(out=wa_w_raw[b][:], in_=as_words(wa_words)[:, b * K_PASS : (b + 1) * K_PASS])
-
-        def load_wb(a, b):
-            wb_raw[a, b] = buf("wb_raw%d%d" % (a, b), [P, PACK, K_PASS], F32)
-            rows = wb[a * K_PASS : (a + 1) * K_PASS, b * K_PASS : (b + 1) * K_PASS]
-            nc.sync.dma_start(out=wb_raw[a, b][:], in_=rows.rearrange("(p i) r -> p i r", i=PACK))
+        def load_wb(a, b, parts=1):
+            rows = wb[a * K_PASS : (a + 1) * K_PASS, b * K_PASS : (b + 1) * K_PASS].rearrange("(p i) r -> p i r", i=PACK)
+            width = K_PASS // parts
+            for c0 in range(0, K_PASS, width):
+                nc.sync.dma_start(out=wb_raw[a, b][:, :, c0 : c0 + width], in_=rows[:, :, c0 : c0 + width])
 
         def load_en(b):
-            rows = en.rearrange("(b g t e) n -> b t g e n", b=2, t=PACK, e=8)
+            rows = en.rearrange("(b m t e) n -> b t m e n", b=2, t=PACK, e=RUN)
             for t in range(PACK):
                 nc.sync.dma_start(out=en_raw[b][:, t, :], in_=rows[b, t])
 
-        def order_wa(b):
-            wa_w[b] = buf("wa_w%d" % b, [P, K_PASS], I32)
-            nc.gpsimd.tensor_copy(
-                out=wa_w[b][:].rearrange("p (t g e) -> p t g e", t=PACK, e=8),
-                in_=wa_w_raw[b][:].rearrange("p (g t e) -> p t g e", t=PACK, e=8),
-            )
-
-        def order_wa_scales():
-            nc.gpsimd.tensor_copy(
-                out=wa_s[:].bitcast(I32).rearrange("p (t g e) -> p t g e", t=PACK, e=2),
-                in_=wa_s_raw[:].bitcast(I32).rearrange("p (g t e) -> p t g e", t=PACK, e=2),
+        def order_wa_scales(b, on=None):
+            wa_s[b] = buf("wa_s%d" % b, [P, K_PASS], U8, on)
+            nc.scalar.copy(
+                out=wa_s[b][:].bitcast(U32).rearrange("p (t m) -> p t m", t=PACK),
+                in_=wa_s_raw[:, b * K_PASS : (b + 1) * K_PASS].bitcast(U32).rearrange("p (m t) -> p t m", t=PACK),
             )
 
         def half_of(entries, h):
             return entries[:, h * HALF // 16 : (h + 1) * HALF // 16]
 
-        def gather_tab2(h, on=None, shift=0):
-            g2_pair[h] = buf("g2_pair%d" % h, [P, HALF], U32, on, shift)
-            nc.vector.tensor_copy(g2_pair[h][:], tab2_w[:].bitcast(U32).indirect(half_of(list2, h)))
+        def gather_tab2_scales(h):
+            cols = slice(h * HALF, (h + 1) * HALF)
+            nc.vector.tensor_copy(g2_s[0][:, cols], tab2_s[:].indirect(half_of(list2, h)))
+
+        def move_parked_rows(h):
+            cols = slice(h * HALF, (h + 1) * HALF)
+            nc.sync.dma_start(out=g2_s[1][: P - PARKED, cols].bitcast(I32), in_=g2_s[0][PARKED:, cols].bitcast(I32))
+
+        def gather_tab2(h, j0, count):
+            first = (h * HALF + j0) // 16
+            entries = list2[:, first : first + count // 16]
+            nc.vector.tensor_copy(g2_pair[h][:, j0 : j0 + count], tab2_w[:].bitcast(U32).indirect(entries))
 
         def part(h, on, shift=0):
             g2_w[h] = buf("g2_w%d" % h, [P, 2, 2 * HALF], U8, on, shift)
@@ -129,15 +129,19 @@ def tile_list_kg_max_sig_kernel(
         def round_on_gpsimd(dst, src):
             nc.gpsimd.tensor_scalar(out=dst, in0=src, scalar1=1.0, scalar2=0.0, op0=MULT, op1=ADD)
 
-        def round_wb(a, b, on=None):
+        def wb_views(a, b):
+            dst = wb_bf[a, b][:].rearrange("p (t m e i) -> p t m i e", t=PACK, e=RUN, i=PACK)
+            src = wb_raw[a, b][:].rearrange("p i (m t e) -> p t m i e", t=PACK, e=RUN)
+            return dst, src
+
+        def round_wb(a, b, on_scalar, on=None):
             wb_bf[a, b] = buf("wb_bf%d%d" % (a, b), [P, PACK * K_PASS], BF16, on)
-            dst = wb_bf[a, b][:].rearrange("p (t g e u i) -> p t g e i u", t=PACK, e=4, u=2, i=PACK)
-            src = wb_raw[a, b][:].rearrange("p i (g t e u) -> p t g e i u", t=PACK, e=4, u=2)
-            for t in range(ON_SCALAR[a, b]):
-                nc.scalar.copy(out=dst[:, t], in_=src[:, t])
-            dst = wb_bf[a, b][:].rearrange("p (t g e i) -> p t g e i", t=PACK, e=8, i=PACK)
-            src = wb_raw[a, b][:].rearrange("p i (g t e) -> p t g e i", t=PACK, e=8)
-            for t in range(ON_SCALAR[a, b], PACK):
+            dst, src = wb_views(a, b)
+            if on_scalar:
+                nc.scalar.copy(out=dst[:, :on_scalar], in_=src[:, :on_scalar])
+            dst = wb_bf[a, b][:].rearrange("p (t m e i) -> p t m e i", t=PACK, e=RUN, i=PACK)
+            src = wb_raw[a, b][:].rearrange("p i (m t e) -> p t m e i", t=PACK, e=RUN)
+            for t in range(on_scalar, PACK):
                 round_on_gpsimd(dst[:, t], src[:, t])
 
         def quantize(codes, scales, values):
@@ -160,17 +164,14 @@ def tile_list_kg_max_sig_kernel(
         def chunks_of(tile, s, count=1):
             return tile[:, s * BANK : (s + count) * BANK]
 
-        def second_bank(c):
-            return RING + c if c < BANKS - RING else c % RING
-
         def make_ha(b, c, k, values):
             bank = psum.tile([P, PACK, CHUNK], F32, name="bank_a", tag="bank%d" % k)
             for t in range(PACK):
-                cols = slice(t * 2 * P + b * P, t * 2 * P + (b + 1) * P)
+                cols = slice(b * K_PASS + t * P, b * K_PASS + (t + 1) * P)
                 nc.tensor.matmul_mx(
                     out=bank[:, t, :],
-                    lhsT=wa_w[b][:, t * P : (t + 1) * P].bitcast(FP8X4),
-                    lhsT_scale=wa_s[WA_ROW:, cols],
+                    lhsT=wa_w[:, cols].bitcast(FP8X4),
+                    lhsT_scale=wa_s[b][WA_ROW:, t * P : (t + 1) * P],
                     rhs=g_w[:, c * CHUNK : (c + 1) * CHUNK].bitcast(FP8X4),
                     rhs_scale=g_s[TAB_ROW:, c * CHUNK : (c + 1) * CHUNK],
                     start=True,
@@ -223,78 +224,96 @@ def tile_list_kg_max_sig_kernel(
             nc.scalar.activation(out=result[:], in_=y_bank[c0][:], func=SIGMOID)
             queue.dma_start(out=out[:, queries].rearrange("(m p) j -> p m j", p=P), in_=result[:])
 
-        nc.vector.memset(tab_s[:, : T // 2].bitcast(I32), 0)
-        nc.gpsimd.memset(tab_s[:, T // 2 :].bitcast(I32), 0)
+        nc.gpsimd.memset(tab_s[:].bitcast(I32), 0)
         nc.vector.memset(warm[:, 0:1], 0.0)
-        nc.vector.memset(tab2_s[:].bitcast(I32), 0)
-        nc.gpsimd.memset(wa_s_raw[:].bitcast(I32), 0)
-        nc.gpsimd.memset(g2_s[1][:].bitcast(I32), 0)
+        nc.vector.memset(wa_s_raw[:].bitcast(I32), 0)
+        nc.gpsimd.memset(tab2_s[:].bitcast(I32), 0)
+        nc.vector.memset(g2_s[1][:].bitcast(I32), 0)
         nc.scalar.activation(out=warm[:, 1:2], in_=warm[:, 0:1], func=SIGMOID)
 
-        nc.sync.dma_start(out=tab_w[:], in_=as_words(tab_words))
         nc.sync.dma_start(list1[:], offs)
-        load_scale_rows(tab_s, TAB_ROW, tab_scales[0])
+        nc.sync.dma_start(out=wa_w_raw[:], in_=as_words(wa_words))
+        load_scale_rows([nc.sync] * 4, tab_s, TAB_ROW, tab_scales[0])
+        nc.sync.dma_start(out=tab_w[:], in_=as_words(tab_words))
+        load_scale_rows([nc.sync] * 3 + [nc.gpsimd], wa_s_raw, WA_ROW, wa_scales[0])
         load_wb(0, 0)
-        load_wa(0)
         nc.sync.dma_start(list2[:], offs2)
-        load_scale_rows(wa_s_raw, WA_ROW, wa_scales[0])
+        load_tab2_scales([nc.sync] * 3 + [nc.gpsimd])
         nc.sync.dma_start(out=tab2_w[:], in_=as_words(tab2_words))
-        load_tab2_scales()
-        load_wa(1)
-        load_wb(1, 0)
-        load_wb(0, 1)
-        nc.vector.tensor_copy(g_w[:], tab_w[:].bitcast(U32).indirect(list1[:]))
+        load_wb(1, 0, 2)
         nc.vector.tensor_copy(g_s[:], tab_s[:].indirect(list1[:]))
-        order_wa(0)
-        order_wa_scales()
-        gather_tab2(0)
         for h in range(2):
-            cols = slice(h * HALF, (h + 1) * HALF)
-            nc.vector.tensor_copy(g2_s[0][:, cols], tab2_s[:].indirect(half_of(list2, h)))
-            nc.sync.dma_start(out=g2_s[1][: P - PARKED, cols].bitcast(I32), in_=g2_s[0][PARKED:, cols].bitcast(I32))
+            nc.vector.tensor_copy(g_w[:, h * HALF : (h + 1) * HALF], tab_w[:].bitcast(U32).indirect(half_of(list1, h)))
+        for b in range(2):
+            cols = slice(b * K_PASS, (b + 1) * K_PASS)
+            nc.scalar.copy(
+                out=wa_w[:, cols].bitcast(U32).rearrange("p (t m e) -> p t m e", t=PACK, e=RUN),
+                in_=wa_w_raw[:, cols].bitcast(U32).rearrange("p (m t e) -> p t m e", t=PACK, e=RUN),
+            )
+        order_wa_scales(0)
+        gather_tab2_scales(0)
+        move_parked_rows(0)
+        load_wb(0, 1)
+        gather_tab2_scales(1)
+        move_parked_rows(1)
         load_wb(1, 1)
         load_en(0)
         load_en(1)
 
-        round_wb(0, 0)
-        quantize_wb(0, 0)
-        for c in range(HA_AHEAD):
-            make_ha(0, c, c, buf("ha0%d" % c, [P, BANK], BF16)[:])
-        order_wa(1)
-        part(0, "tab2_s", -T // 2)
-        gather_tab2(1, "tab2_s", T // 2)
-        for c in range(AHEAD):
-            hb_pass(0, 0, c, c % RING)
-        round_wb(1, 0)
-        quantize_wb(1, 0)
-        part(1, "wb_bf10")
-        for c in range(HA_AHEAD, CHUNKS):
-            make_ha(0, c, c, buf("ha0%d" % c, [P, BANK], BF16, "wb_raw10", (c - HA_AHEAD + 1) * BANK_BYTES)[:])
-        round_wb(0, 1, "g2_pair1")
-        h_first = buf("h_first", [P, CHUNKS * BANK], BF16)
-        for c in range(CHUNKS):
-            if c >= AHEAD:
-                hb_pass(0, 0, c, c % RING)
-            hb_pass(1, 0, c)
-            maximum(0, c, chunks_of(h_first, c))
-
-        for c in range(DIRECT):
-            make_ha(1, c, second_bank(c), buf("ha1%d" % c, [P, BANK], BF16, "wb_raw10", (DIRECT + c) * BANK_BYTES)[:])
-        quantize_wb(0, 1, "ha0%d" % HA_AHEAD, -BANK_BYTES)
-        round_wb(1, 1)
-        ha_late = buf("ha_late", [P, (CHUNKS - DIRECT) * BANK], BF16)
+        round_wb(0, 0, 0)
+        for c in range(6):
+            make_ha(0, c, c % 4, buf("ha0%d" % c, [P, BANK], BF16)[:])
+        g2_pair[0] = buf("g2_pair0", [P, HALF], U32)
+        g2_pair[1] = buf("g2_pair1", [P, HALF], U32, room=2 * BANK_BYTES)
+        gather_tab2(0, 0, HALF)
+        gather_tab2(1, 0, HALF)
+        part(0, None)
+        quantize_wb(0, 0, "tab2_w")
+        order_wa_scales(1, "tab2_s")
+        wb_bf[1, 0] = buf("wb_bf10", [P, PACK * K_PASS], BF16)
+        dst, src = wb_views(1, 0)
+        nc.scalar.copy(out=dst[:, :2, :16], in_=src[:, :2, :16])
+        nc.scalar.copy(out=dst[:, :, 16:], in_=src[:, :, 16:])
+        dst = wb_bf[1, 0][:].rearrange("p (t m e i) -> p t m e i", t=PACK, e=RUN, i=PACK)
+        src = wb_raw[1, 0][:].rearrange("p i (m t e) -> p t m e i", t=PACK, e=RUN)
+        for t in (2, 3):
+            round_on_gpsimd(dst[:, t, :16], src[:, t, :16])
+        make_ha(0, 6, 2, buf("ha06", [P, BANK], BF16, "wb_raw10", 7 * BANK_BYTES)[:])
+        make_ha(0, 7, 3, buf("ha07", [P, BANK], BF16, "wb_raw10")[:])
+        ha_late = buf("ha_late", [P, (CHUNKS - DIRECT) * BANK], BF16, "wb_raw10", BANK_BYTES)
         for c in range(DIRECT, CHUNKS):
-            make_ha(1, c, second_bank(c), chunks_of(ha_late, c - DIRECT))
-        quantize_wb(1, 1)
-        h_w[0] = buf("h_w0", [P, J], U32, "wb_bf11")
-        quantize_h(0, 0, CHUNKS, h_first[:])
+            make_ha(1, c, c, chunks_of(ha_late, c - DIRECT))
+        for c in range(2):
+            hb_pass(0, 0, c, c)
+        quantize_wb(1, 0)
+        part(1, "wb_raw10", 5 * BANK_BYTES)
+        round_wb(0, 1, 0, "g2_pair1")
+        h_first = buf("h_first", [P, 6 * BANK], BF16)
+        first_bank = [0, 1, 2, 3, 4, 5, 6, 7]
+        for c in range(CHUNKS):
+            if c >= 2:
+                hb_pass(0, 0, c, first_bank[c])
+            hb_pass(1, 0, c)
+            if c == 6:
+                quantize_wb(0, 1)
+                h_last = buf("h_last", [P, 2 * BANK], BF16, "wb_raw01")
+            maximum(0, c, chunks_of(h_first, c) if c < 6 else chunks_of(h_last, c - 6))
+            if c == AHEAD - 1:
+                round_wb(1, 1, 4)
         for c in range(DIRECT):
-            hb_pass(0, 1, c, second_bank(c))
-        en_bf = buf("en_bf", [P, 2 * N * PACK], BF16, "h_first")
-        nc.scalar.copy(
-            out=en_bf[:, N * PACK :].rearrange("p (n u t) -> p n t u", u=2, t=PACK),
-            in_=en_raw[1][:].rearrange("p t (n u) -> p n t u", u=2),
-        )
+            make_ha(1, c, c, buf("ha1%d" % c, [P, BANK], BF16, "wb_raw11", c * BANK_BYTES)[:])
+        quantize_wb(1, 1, "wb_raw01", 4 * BANK_BYTES)
+        h_w[0] = buf("h_w0", [P, J], U32, "wb_raw11", 4 * BANK_BYTES)
+        quantize_h(0, 0, 4, chunks_of(h_first, 0, 4))
+        quantize_h(0, 4, 2, chunks_of(h_first, 4, 2))
+        quantize_h(0, 6, 2, h_last[:])
+        second_bank = [4, 5, 0, 6, 1, 2, 3, 7]
+        for c in range(DIRECT):
+            hb_pass(0, 1, c, second_bank[c])
+        en_bf = buf("en_bf", [P, 2 * N * PACK], BF16, "h_last")
+        dst = en_bf[:].rearrange("p (b n u t) -> p b n t u", b=2, u=RUN, t=PACK)
+        src = [en_raw[b][:].rearrange("p t (n u) -> p n t u", u=RUN) for b in range(2)]
+        nc.scalar.copy(out=dst[:, 1], in_=src[1])
         dst = en_bf[:, : N * PACK].rearrange("p (n t) -> p n t", t=PACK)
         src = en_raw[0][:].rearrange("p t n -> p n t")
         for n0 in range(0, N, P):
@@ -305,7 +324,7 @@ def tile_list_kg_max_sig_kernel(
             maximum(1, c, chunks_of(h_early, c))
         hb_late = buf("hb_late", [P, (CHUNKS - DIRECT) * BANK], BF16, "en_raw1")
         for c in range(DIRECT, CHUNKS):
-            hb_pass(0, 1, c, second_bank(c))
+            hb_pass(0, 1, c, second_bank[c])
             hb_pass(1, 1, c)
             nc.scalar.copy(out=by_query(chunks_of(hb_late, c - DIRECT)), in_=bank_by_query(hb_bank[1, c]))
         en_w = buf("en_w", [P, 2 * N], U32, "ha11")
@@ -315,11 +334,11 @@ def tile_list_kg_max_sig_kernel(
         steps = [(0, 2), (2, 2), (4, 2), (6, 1), (7, 1)]
         early_steps = DIRECT // 2
         for s in range(early_steps):
-            score_pass(0, *steps[s], second_bank(s))
+            score_pass(0, *steps[s], second_bank[s])
         for c0, count in steps[:early_steps]:
             finish(c0, count, chunks_of(h_early, c0, count), nc.sync)
         for s in range(early_steps, len(steps)):
-            score_pass(0, *steps[s], second_bank(s))
+            score_pass(0, *steps[s], second_bank[s])
         h_late = buf("h_late", [P, (CHUNKS - DIRECT) * BANK], BF16)
 
         def late_maximum(c0, count):

@@ -30,6 +30,7 @@ BANK_BYTES = 2 * BANK
 PARKED = 16
 TAB_ROW, WA_ROW = 4, 8
 AHEAD = 4
+ALL = slice(None)
 DIRECT = 4
 
 
@@ -66,7 +67,13 @@ def tile_list_kg_max_sig_kernel(
         g_w = buf("g_w", [P, J], U32)
         g2_s = [buf("g2_s%d" % a, [P, J], U8) for a in range(2)]
         wb_s = {(a, b): buf("wb_s%d%d" % (a, b), [P, K_PASS], U8) for b in range(2) for a in range(2)}
-        wb_raw = {(a, b): buf("wb_raw%d%d" % (a, b), [P, PACK, K_PASS], F32) for b in range(2) for a in range(2)}
+        wb_raw = {}
+        for b in range(2):
+            for a in range(2):
+                parts = 2 if (a, b) in ((1, 0),) else 1
+                names = ["wb_raw%d%d" % (a, b), "wb_right%d%d" % (a, b)]
+                wb_raw[a, b] = [buf(names[h], [P, PACK, K_PASS // parts], F32) for h in range(parts)]
+                place["end"] += BANK_BYTES
         en_raw = [buf("en_raw%d" % b, [P, PACK, N], F32) for b in range(2)]
         en_s = buf("en_s", [P, 2 * N], U8)
         h_s = [buf("h_s%d" % b, [P, J], U8) for b in range(2)]
@@ -85,11 +92,11 @@ def tile_list_kg_max_sig_kernel(
         def as_words(packed):
             return packed[0].rearrange("p c i -> p (c i)").bitcast(I32)
 
-        def load_wb(a, b, parts=1):
-            rows = wb[a * K_PASS : (a + 1) * K_PASS, b * K_PASS : (b + 1) * K_PASS].rearrange("(p i) r -> p i r", i=PACK)
-            width = K_PASS // parts
-            for c0 in range(0, K_PASS, width):
-                nc.sync.dma_start(out=wb_raw[a, b][:, :, c0 : c0 + width], in_=rows[:, :, c0 : c0 + width])
+        def load_wb(a, b, h=0):
+            width = K_PASS // len(wb_raw[a, b])
+            c0 = b * K_PASS + h * width
+            rows = wb[a * K_PASS : (a + 1) * K_PASS, c0 : c0 + width]
+            nc.sync.dma_start(out=wb_raw[a, b][h][:], in_=rows.rearrange("(p i) r -> p i r", i=PACK))
 
         def load_en(b):
             rows = en.rearrange("(b m t e) n -> b t m e n", b=2, t=PACK, e=RUN)
@@ -129,20 +136,17 @@ def tile_list_kg_max_sig_kernel(
         def round_on_gpsimd(dst, src):
             nc.gpsimd.tensor_scalar(out=dst, in0=src, scalar1=1.0, scalar2=0.0, op0=MULT, op1=ADD)
 
-        def wb_views(a, b):
-            dst = wb_bf[a, b][:].rearrange("p (t m e i) -> p t m i e", t=PACK, e=RUN, i=PACK)
-            src = wb_raw[a, b][:].rearrange("p i (m t e) -> p t m i e", t=PACK, e=RUN)
-            return dst, src
-
-        def round_wb(a, b, on_scalar, on=None):
+        def round_wb(a, b, on=None, scalar=(), gpsimd=(), vector=()):
             wb_bf[a, b] = buf("wb_bf%d%d" % (a, b), [P, PACK * K_PASS], BF16, on)
-            dst, src = wb_views(a, b)
-            if on_scalar:
-                nc.scalar.copy(out=dst[:, :on_scalar], in_=src[:, :on_scalar])
-            dst = wb_bf[a, b][:].rearrange("p (t m e i) -> p t m e i", t=PACK, e=RUN, i=PACK)
-            src = wb_raw[a, b][:].rearrange("p i (m t e) -> p t m e i", t=PACK, e=RUN)
-            for t in range(on_scalar, PACK):
-                round_on_gpsimd(dst[:, t], src[:, t])
+            parts = len(wb_raw[a, b])
+            dst = wb_bf[a, b][:].rearrange("p (t h m e i) -> p h t m i e", t=PACK, h=parts, e=RUN, i=PACK)
+            src = [raw[:].rearrange("p i (m t e) -> p t m i e", t=PACK, e=RUN) for raw in wb_raw[a, b]]
+            for h, t in gpsimd:
+                round_on_gpsimd(*[side[:, t].rearrange("p m i e -> p m e i") for side in (dst[:, h], src[h])])
+            for h, slots in scalar:
+                nc.scalar.copy(out=dst[:, h, slots], in_=src[h][:, slots])
+            for h, slots in vector:
+                nc.vector.tensor_copy(out=dst[:, h, slots], in_=src[h][:, slots])
 
         def quantize(codes, scales, values):
             nc.vector.quantize_mx(out=codes.bitcast(FP8X4), scales=scales, in_=values)
@@ -240,7 +244,8 @@ def tile_list_kg_max_sig_kernel(
         nc.sync.dma_start(list2[:], offs2)
         load_tab2_scales([nc.sync] * 3 + [nc.gpsimd])
         nc.sync.dma_start(out=tab2_w[:], in_=as_words(tab2_words))
-        load_wb(1, 0, 2)
+        load_wb(1, 0, 0)
+        load_wb(1, 0, 1)
         nc.vector.tensor_copy(g_s[:], tab_s[:].indirect(list1[:]))
         for h in range(2):
             nc.vector.tensor_copy(g_w[:, h * HALF : (h + 1) * HALF], tab_w[:].bitcast(U32).indirect(half_of(list1, h)))
@@ -260,7 +265,7 @@ def tile_list_kg_max_sig_kernel(
         load_en(0)
         load_en(1)
 
-        round_wb(0, 0, 0)
+        round_wb(0, 0, gpsimd=[(0, t) for t in range(PACK)])
         for c in range(6):
             make_ha(0, c, c % 4, buf("ha0%d" % c, [P, BANK], BF16)[:])
         g2_pair[0] = buf("g2_pair0", [P, HALF], U32)
@@ -270,24 +275,17 @@ def tile_list_kg_max_sig_kernel(
         part(0, None)
         quantize_wb(0, 0, "tab2_w")
         order_wa_scales(1, "tab2_s")
-        wb_bf[1, 0] = buf("wb_bf10", [P, PACK * K_PASS], BF16)
-        dst, src = wb_views(1, 0)
-        nc.scalar.copy(out=dst[:, :2, :16], in_=src[:, :2, :16])
-        nc.scalar.copy(out=dst[:, :, 16:], in_=src[:, :, 16:])
-        dst = wb_bf[1, 0][:].rearrange("p (t m e i) -> p t m e i", t=PACK, e=RUN, i=PACK)
-        src = wb_raw[1, 0][:].rearrange("p i (m t e) -> p t m e i", t=PACK, e=RUN)
-        for t in (2, 3):
-            round_on_gpsimd(dst[:, t, :16], src[:, t, :16])
-        make_ha(0, 6, 2, buf("ha06", [P, BANK], BF16, "wb_raw10", 7 * BANK_BYTES)[:])
-        make_ha(0, 7, 3, buf("ha07", [P, BANK], BF16, "wb_raw10")[:])
-        ha_late = buf("ha_late", [P, (CHUNKS - DIRECT) * BANK], BF16, "wb_raw10", BANK_BYTES)
+        round_wb(1, 0, scalar=[(0, slice(0, 3)), (1, ALL)], gpsimd=[(0, 3)])
+        make_ha(0, 6, 2, buf("ha06", [P, BANK], BF16, "wb_raw10", 7 * BANK_BYTES - 64)[:])
+        make_ha(0, 7, 3, buf("ha07", [P, BANK], BF16, "wb_raw10", 8 * BANK_BYTES - 64)[:])
+        ha_late = buf("ha_late", [P, (CHUNKS - DIRECT) * BANK], BF16, "wb_raw10", BANK_BYTES - 64)
         for c in range(DIRECT, CHUNKS):
             make_ha(1, c, c, chunks_of(ha_late, c - DIRECT))
         for c in range(2):
             hb_pass(0, 0, c, c)
         quantize_wb(1, 0)
-        part(1, "wb_raw10", 5 * BANK_BYTES)
-        round_wb(0, 1, 0, "g2_pair1")
+        part(1, "wb_raw10", 5 * BANK_BYTES - 64)
+        round_wb(0, 1, "g2_pair1", scalar=[(0, slice(0, 1))], gpsimd=[(0, t) for t in range(1, PACK)])
         h_first = buf("h_first", [P, 6 * BANK], BF16)
         first_bank = [0, 1, 2, 3, 4, 5, 6, 7]
         for c in range(CHUNKS):
@@ -299,7 +297,7 @@ def tile_list_kg_max_sig_kernel(
                 h_last = buf("h_last", [P, 2 * BANK], BF16, "wb_raw01")
             maximum(0, c, chunks_of(h_first, c) if c < 6 else chunks_of(h_last, c - 6))
             if c == AHEAD - 1:
-                round_wb(1, 1, 4)
+                round_wb(1, 1, scalar=[(0, ALL)])
         for c in range(DIRECT):
             make_ha(1, c, c, buf("ha1%d" % c, [P, BANK], BF16, "wb_raw11", c * BANK_BYTES)[:])
         quantize_wb(1, 1, "wb_raw01", 4 * BANK_BYTES)
@@ -314,10 +312,9 @@ def tile_list_kg_max_sig_kernel(
         dst = en_bf[:].rearrange("p (b n u t) -> p b n t u", b=2, u=RUN, t=PACK)
         src = [en_raw[b][:].rearrange("p t (n u) -> p n t u", u=RUN) for b in range(2)]
         nc.scalar.copy(out=dst[:, 1], in_=src[1])
-        dst = en_bf[:, : N * PACK].rearrange("p (n t) -> p n t", t=PACK)
-        src = en_raw[0][:].rearrange("p t n -> p n t")
-        for n0 in range(0, N, P):
-            round_on_gpsimd(dst[:, n0 : n0 + P], src[:, n0 : n0 + P])
+        round_on_gpsimd(
+            en_bf[:, : N * PACK].rearrange("p (n t) -> p n t", t=PACK), en_raw[0][:].rearrange("p t n -> p n t")
+        )
         h_early = buf("h_early", [P, DIRECT * BANK], BF16)
         for c in range(DIRECT):
             hb_pass(1, 1, c)

@@ -144,7 +144,9 @@ def tile_list_kg_max_sig_kernel(
             for h, t in gpsimd:
                 round_on_gpsimd(*[side[:, t].rearrange("p m i e -> p m e i") for side in (dst[:, h], src[h])])
             for h, slots in scalar:
-                nc.scalar.copy(out=dst[:, h, slots], in_=src[h][:, slots])
+                for t in range(PACK)[slots]:
+                    pairs = [side[:, t].rearrange("p m i (e u) -> p m e i u", u=2) for side in (dst[:, h], src[h])]
+                    nc.scalar.copy(out=pairs[0], in_=pairs[1])
             for h, slots in vector:
                 nc.vector.tensor_copy(out=dst[:, h, slots], in_=src[h][:, slots])
 
@@ -309,8 +311,8 @@ def tile_list_kg_max_sig_kernel(
         for c in range(DIRECT):
             hb_pass(0, 1, c, second_bank[c])
         en_bf = buf("en_bf", [P, 2 * N * PACK], BF16, "h_last")
-        dst = en_bf[:].rearrange("p (b n u t) -> p b n t u", b=2, u=RUN, t=PACK)
-        src = [en_raw[b][:].rearrange("p t (n u) -> p n t u", u=RUN) for b in range(2)]
+        dst = en_bf[:].rearrange("p (b n u t) -> p b n t u", b=2, u=2, t=PACK)
+        src = [en_raw[b][:].rearrange("p t (n u) -> p n t u", u=2) for b in range(2)]
         nc.scalar.copy(out=dst[:, 1], in_=src[1])
         round_on_gpsimd(
             en_bf[:, : N * PACK].rearrange("p (n t) -> p n t", t=PACK), en_raw[0][:].rearrange("p t n -> p n t")

@@ -249,8 +249,8 @@ def tile_list_kg_max_sig_kernel(
         load_wb(1, 0, 0)
         load_wb(1, 0, 1)
         nc.vector.tensor_copy(g_s[:], tab_s[:].indirect(list1[:]))
-        for h in range(2):
-            nc.vector.tensor_copy(g_w[:, h * HALF : (h + 1) * HALF], tab_w[:].bitcast(U32).indirect(half_of(list1, h)))
+        for j0, j1 in ((0, J // 4), (J // 4, HALF), (HALF, J)):
+            nc.vector.tensor_copy(g_w[:, j0:j1], tab_w[:].bitcast(U32).indirect(list1[:, j0 // 16 : j1 // 16]))
         for b in range(2):
             cols = slice(b * K_PASS, (b + 1) * K_PASS)
             nc.scalar.copy(

@@ -268,8 +268,8 @@ def tile_list_kg_max_sig_kernel(
         load_en(1)
 
         round_wb(0, 0, gpsimd=[(0, t) for t in range(PACK)])
-        for c in range(6):
-            make_ha(0, c, c % 4, buf("ha0%d" % c, [P, BANK], BF16)[:])
+        for c in range(7):
+            make_ha(0, c, [0, 1, 2, 3, 0, 1, 3][c], buf("ha0%d" % c, [P, BANK], BF16)[:])
         g2_pair[0] = buf("g2_pair0", [P, HALF], U32)
         g2_pair[1] = buf("g2_pair1", [P, HALF], U32, room=2 * BANK_BYTES)
         gather_tab2(0, 0, HALF)
@@ -278,18 +278,18 @@ def tile_list_kg_max_sig_kernel(
         quantize_wb(0, 0, "tab2_w")
         order_wa_scales(1, "tab2_s")
         round_wb(1, 0, scalar=[(0, slice(0, 3)), (1, ALL)], gpsimd=[(0, 3)])
-        make_ha(0, 6, 2, buf("ha06", [P, BANK], BF16, "wb_raw10", 7 * BANK_BYTES - 64)[:])
-        make_ha(0, 7, 3, buf("ha07", [P, BANK], BF16, "wb_raw10", 8 * BANK_BYTES - 64)[:])
+        make_ha(0, 7, 1, buf("ha07", [P, BANK], BF16, "wb_raw10", 8 * BANK_BYTES - 64)[:])
         ha_late = buf("ha_late", [P, (CHUNKS - DIRECT) * BANK], BF16, "wb_raw10", BANK_BYTES - 64)
         for c in range(DIRECT, CHUNKS):
             make_ha(1, c, c, chunks_of(ha_late, c - DIRECT))
+        make_ha(1, 0, 2, buf("ha10", [P, BANK], BF16, "wb_raw10", 7 * BANK_BYTES - 64)[:])
         for c in range(2):
-            hb_pass(0, 0, c, c)
+            hb_pass(0, 0, c, 3 * c)
         quantize_wb(1, 0)
         part(1, "wb_raw10", 5 * BANK_BYTES - 64)
         round_wb(0, 1, "g2_pair1", scalar=[(0, slice(0, 1))], gpsimd=[(0, t) for t in range(1, PACK)])
         h_first = buf("h_first", [P, 6 * BANK], BF16)
-        first_bank = [0, 1, 2, 3, 4, 5, 6, 7]
+        first_bank = [0, 3, 1, 4, 5, 6, 7, 2]
         for c in range(CHUNKS):
             if c >= 2:
                 hb_pass(0, 0, c, first_bank[c])
@@ -300,14 +300,14 @@ def tile_list_kg_max_sig_kernel(
             maximum(0, c, chunks_of(h_first, c) if c < 6 else chunks_of(h_last, c - 6))
             if c == AHEAD - 1:
                 round_wb(1, 1, scalar=[(0, ALL)])
-        for c in range(DIRECT):
-            make_ha(1, c, c, buf("ha1%d" % c, [P, BANK], BF16, "wb_raw11", c * BANK_BYTES)[:])
+        for c in range(1, DIRECT):
+            make_ha(1, c, first_bank[c - 1], buf("ha1%d" % c, [P, BANK], BF16, "wb_raw11", c * BANK_BYTES)[:])
         quantize_wb(1, 1, "wb_raw01", 4 * BANK_BYTES)
         h_w[0] = buf("h_w0", [P, J], U32, "wb_raw11", 4 * BANK_BYTES)
         quantize_h(0, 0, 4, chunks_of(h_first, 0, 4))
         quantize_h(0, 4, 2, chunks_of(h_first, 4, 2))
         quantize_h(0, 6, 2, h_last[:])
-        second_bank = [4, 5, 0, 6, 1, 2, 3, 7]
+        second_bank = [4, 5, 6, 7, 2, 0, 3, 1]
         for c in range(DIRECT):
             hb_pass(0, 1, c, second_bank[c])
         en_bf = buf("en_bf", [P, 2 * N * PACK], BF16, "h_last")

@@ -299,10 +299,17 @@ def tile_list_kg_max_sig_kernel(
                 h_last = buf("h_last", [P, 2 * BANK], BF16, "wb_raw01")
             maximum(0, c, chunks_of(h_first, c) if c < 6 else chunks_of(h_last, c - 6))
             if c == AHEAD - 1:
-                round_wb(1, 1, scalar=[(0, ALL)])
+                round_wb(1, 1, scalar=[(0, slice(0, 3))])
+        last = buf("wb_last11", [P, K_PASS], BF16, "wb_bf01")
+        round_on_gpsimd(
+            last[:].rearrange("p (m e i) -> p m e i", e=RUN, i=PACK),
+            wb_raw[1, 1][0][:].rearrange("p i (m t e) -> p t m e i", t=PACK, e=RUN)[:, 3],
+        )
         for c in range(1, DIRECT):
             make_ha(1, c, first_bank[c - 1], buf("ha1%d" % c, [P, BANK], BF16, "wb_raw11", c * BANK_BYTES)[:])
-        quantize_wb(1, 1, "wb_raw01", 4 * BANK_BYTES)
+        wb_w[1, 1] = buf("wb_w11", [P, K_PASS], U32, "wb_raw01", 4 * BANK_BYTES)
+        quantize(wb_w[1, 1][:, : 3 * P], wb_s[1, 1][:, : 3 * P], wb_bf[1, 1][:, : 3 * K_PASS])
+        quantize(wb_w[1, 1][:, 3 * P :], wb_s[1, 1][:, 3 * P :], last[:])
         h_w[0] = buf("h_w0", [P, J], U32, "wb_raw11", 4 * BANK_BYTES)
         quantize_h(0, 0, 4, chunks_of(h_first, 0, 4))
         quantize_h(0, 4, 2, chunks_of(h_first, 4, 2))

@@ -75,7 +75,7 @@ def tile_list_kg_max_sig_kernel(
                 wb_raw[a, b] = [buf(names[h], [P, PACK, K_PASS // parts], F32) for h in range(parts)]
                 place["end"] += BANK_BYTES
         en_raw = [buf("en_raw%d" % b, [P, PACK, N], F32) for b in range(2)]
-        en_s = buf("en_s", [P, 2 * N], U8)
+        en_s = [buf("en_s%d" % b, [P, N], U8) for b in range(2)]
         h_s = [buf("h_s%d" % b, [P, J], U8) for b in range(2)]
         wb_bf, wb_w, g2_pair, g2_w, h_w, ha, hb_bank, y_bank = [{} for unused in range(8)]
 
@@ -157,9 +157,13 @@ def tile_list_kg_max_sig_kernel(
             wb_w[a, b] = buf("wb_w%d%d" % (a, b), [P, K_PASS], U32, on, shift)
             quantize(wb_w[a, b][:], wb_s[a, b][:], wb_bf[a, b][:])
 
+        def h_codes(b, c0, count):
+            first = max(c for half, c in h_w if half == b and c <= c0)
+            return h_w[b, first][:, (c0 - first) * CHUNK : (c0 - first + count) * CHUNK]
+
         def quantize_h(b, c0, count, values):
             cols = slice(c0 * CHUNK, (c0 + count) * CHUNK)
-            quantize(h_w[b][:, cols], h_s[b][:, cols], values)
+            quantize(h_codes(b, c0, count), h_s[b][:, cols], values)
 
         def by_query(values):
             return values.rearrange("p (j t) -> p j t", t=PACK)
@@ -211,12 +215,12 @@ def tile_list_kg_max_sig_kernel(
             if b == 0:
                 y_bank[c0] = psum.tile([P, N // P, count * CHUNK], F32, name="bank_y", tag="bank%d" % k)
             for m in range(N // P):
-                cols = slice(b * N + m * P, b * N + (m + 1) * P)
+                cols = slice(m * P, (m + 1) * P)
                 nc.tensor.matmul_mx(
                     out=y_bank[c0][:, m, :],
-                    lhsT=en_w[:, cols].bitcast(FP8X4),
-                    lhsT_scale=en_s[:, cols],
-                    rhs=h_w[b][:, queries].bitcast(FP8X4),
+                    lhsT=en_w[b][:, cols].bitcast(FP8X4),
+                    lhsT_scale=en_s[b][:, cols],
+                    rhs=h_codes(b, c0, count).bitcast(FP8X4),
                     rhs_scale=h_s[b][:, queries],
                     start=(b == 0 and m == 0),
                     stop=(b == 1 and m == N // P - 1),
@@ -305,55 +309,66 @@ def tile_list_kg_max_sig_kernel(
             last[:].rearrange("p (m e i) -> p m e i", e=RUN, i=PACK),
             wb_raw[1, 1][0][:].rearrange("p i (m t e) -> p t m e i", t=PACK, e=RUN)[:, 3],
         )
+        en_bf = [buf("en_bf0", [P, N * PACK], BF16, room=2 * BANK_BYTES), buf("en_bf1", [P, N * PACK], BF16, "h_last")]
+        nc.scalar.copy(
+            out=en_bf[0][:].rearrange("p (n u t) -> p n t u", u=2, t=PACK),
+            in_=en_raw[0][:].rearrange("p t (n u) -> p n t u", u=2),
+        )
         for c in range(1, DIRECT):
-            make_ha(1, c, first_bank[c - 1], buf("ha1%d" % c, [P, BANK], BF16, "wb_raw11", c * BANK_BYTES)[:])
+            make_ha(1, c, first_bank[c - 1], buf("ha1%d" % c, [P, BANK], BF16, "en_raw0", c * BANK_BYTES)[:])
         wb_w[1, 1] = buf("wb_w11", [P, K_PASS], U32, "wb_raw01", 4 * BANK_BYTES)
         quantize(wb_w[1, 1][:, : 3 * P], wb_s[1, 1][:, : 3 * P], wb_bf[1, 1][:, : 3 * K_PASS])
         quantize(wb_w[1, 1][:, 3 * P :], wb_s[1, 1][:, 3 * P :], last[:])
-        h_w[0] = buf("h_w0", [P, J], U32, "wb_raw11", 4 * BANK_BYTES)
+        h_w[0, 0] = buf("h_w0", [P, 6 * CHUNK], U32, "wb_raw11", 4 * BANK_BYTES)
+        h_w[0, 6] = buf("h_w0_last", [P, 2 * CHUNK], U32, "en_raw0")
+        en_w = [buf("en_w%d" % b, [P, N], U32) for b in range(2)]
         quantize_h(0, 0, 4, chunks_of(h_first, 0, 4))
         quantize_h(0, 4, 2, chunks_of(h_first, 4, 2))
+        quantize(en_w[0][:], en_s[0][:], en_bf[0][:])
         quantize_h(0, 6, 2, h_last[:])
         second_bank = [4, 5, 6, 7, 2, 0, 3, 1]
         for c in range(DIRECT):
             hb_pass(0, 1, c, second_bank[c])
-        en_bf = buf("en_bf", [P, 2 * N * PACK], BF16, "h_last")
-        dst = en_bf[:].rearrange("p (b n u t) -> p b n t u", b=2, u=2, t=PACK)
-        src = [en_raw[b][:].rearrange("p t (n u) -> p n t u", u=2) for b in range(2)]
-        nc.scalar.copy(out=dst[:, 1], in_=src[1])
-        round_on_gpsimd(
-            en_bf[:, : N * PACK].rearrange("p (n t) -> p n t", t=PACK), en_raw[0][:].rearrange("p t n -> p n t")
+        nc.scalar.copy(
+            out=en_bf[1][:].rearrange("p (n u t) -> p n t u", u=2, t=PACK)[:, : N // 4],
+            in_=en_raw[1][:].rearrange("p t (n u) -> p n t u", u=2)[:, : N // 4],
         )
-        h_early = buf("h_early", [P, DIRECT * BANK], BF16)
-        for c in range(DIRECT):
-            hb_pass(1, 1, c)
-            maximum(1, c, chunks_of(h_early, c))
-        hb_late = buf("hb_late", [P, (CHUNKS - DIRECT) * BANK], BF16, "en_raw1")
-        for c in range(DIRECT, CHUNKS):
+        round_on_gpsimd(
+            en_bf[1][:].rearrange("p (n t) -> p n t", t=PACK)[:, N // 2 :],
+            en_raw[1][:].rearrange("p t n -> p n t")[:, N // 2 :],
+        )
+        h_early = buf("h_early", [P, DIRECT * BANK], BF16, "en_bf0")
+        hb_late = buf("hb_late", [P, (CHUNKS - DIRECT) * BANK], BF16)
+        h_late = buf("h_late", [P, (CHUNKS - DIRECT) * BANK], BF16, "en_bf1")
+        h_w[1, 0] = buf("h_w1", [P, J], U32, "en_raw1")
+
+        def late_bank(c):
             hb_pass(0, 1, c, second_bank[c])
             hb_pass(1, 1, c)
             nc.scalar.copy(out=by_query(chunks_of(hb_late, c - DIRECT)), in_=bank_by_query(hb_bank[1, c]))
-        en_w = buf("en_w", [P, 2 * N], U32, "ha11")
-        quantize(en_w[:], en_s[:], en_bf[:])
 
-        h_w[1] = buf("h_w1", [P, J], U32, "en_bf")
-        steps = [(0, 2), (2, 2), (4, 2), (6, 1), (7, 1)]
-        early_steps = DIRECT // 2
-        for s in range(early_steps):
-            score_pass(0, *steps[s], second_bank[s])
-        for c0, count in steps[:early_steps]:
-            finish(c0, count, chunks_of(h_early, c0, count), nc.sync)
-        for s in range(early_steps, len(steps)):
-            score_pass(0, *steps[s], second_bank[s])
-        h_late = buf("h_late", [P, (CHUNKS - DIRECT) * BANK], BF16)
-
-        def late_maximum(c0, count):
-            h_c, ha_c, hb_c = [chunks_of(tile, c0 - DIRECT, count) for tile in (h_late, ha_late, hb_late)]
+        def late_maximum(c):
+            h_c, ha_c, hb_c = [chunks_of(tile, c - DIRECT) for tile in (h_late, ha_late, hb_late)]
             nc.vector.tensor_tensor(out=h_c, in0=ha_c, in1=hb_c, op=MAX)
 
-        late = steps[early_steps:]
-        late_maximum(*late[0])
-        for s, (c0, count) in enumerate(late):
-            if s + 1 < len(late):
-                late_maximum(*late[s + 1])
-            finish(c0, count, chunks_of(h_late, c0 - DIRECT, count), nc.sync if s + 1 < len(late) else nc.scalar)
+        for c in range(DIRECT):
+            hb_pass(1, 1, c)
+        for c in range(DIRECT - 1):
+            maximum(1, c, chunks_of(h_early, c))
+        late_bank(4)
+        late_bank(5)
+        score_pass(0, 0, 2, second_bank[0])
+        late_bank(6)
+        quantize(en_w[1][:], en_s[1][:], en_bf[1][:])
+        finish(0, 2, chunks_of(h_early, 0, 2), nc.sync)
+        late_bank(7)
+        maximum(1, 3, chunks_of(h_early, 3))
+        late_maximum(4)
+        score_pass(0, 2, 2, second_bank[1])
+        finish(2, 2, chunks_of(h_early, 2, 2), nc.sync)
+        for c in range(DIRECT, CHUNKS):
+            score_pass(0, c, 1, second_bank[c - 2])
+        for c in range(DIRECT, CHUNKS):
+            if c + 1 < CHUNKS:
+                late_maximum(c + 1)
+            finish(c, 1, chunks_of(h_late, c - DIRECT), nc.sync if c + 1 < CHUNKS else nc.scalar)

@@ -192,7 +192,8 @@ def tile_list_kg_max_sig_kernel(
 
         def hb_pass(a, b, c, k=None):
             h, j0 = divmod(c * CHUNK, HALF)
-            if a == 0:
+            opens = k is not None
+            if opens:
                 hb_bank[b, c] = psum.tile([P, PACK, CHUNK], F32, name="bank_b", tag="bank%d" % k)
             for t in range(PACK):
                 nc.tensor.matmul_mx(
@@ -201,8 +202,8 @@ def tile_list_kg_max_sig_kernel(
                     lhsT_scale=wb_s[a, b][:, t * P : (t + 1) * P],
                     rhs=g2_w[h][:, a, 2 * j0 : 2 * (j0 + CHUNK)].bitcast(FP4X4),
                     rhs_scale=g2_s[a][:, c * CHUNK : (c + 1) * CHUNK],
-                    start=(a == 0 and t == 0),
-                    stop=(a == 1 and t == PACK - 1),
+                    start=(opens and t == 0),
+                    stop=(not opens and t == PACK - 1),
                 )
 
         def maximum(b, c, values):
@@ -296,8 +297,8 @@ def tile_list_kg_max_sig_kernel(
         first_bank = [0, 3, 1, 4, 5, 6, 7, 2]
         for c in range(CHUNKS):
             if c >= 2:
-                hb_pass(0, 0, c, first_bank[c])
-            hb_pass(1, 0, c)
+                hb_pass(1, 0, c, first_bank[c])
+            hb_pass(1 if c < 2 else 0, 0, c)
             if c == 6:
                 quantize_wb(0, 1)
                 h_last = buf("h_last", [P, 2 * BANK], BF16, "wb_raw01")
@@ -330,12 +331,12 @@ def tile_list_kg_max_sig_kernel(
         for c in range(DIRECT):
             hb_pass(0, 1, c, second_bank[c])
         nc.scalar.copy(
-            out=en_bf[1][:].rearrange("p (n u t) -> p n t u", u=2, t=PACK)[:, : N // 4],
-            in_=en_raw[1][:].rearrange("p t (n u) -> p n t u", u=2)[:, : N // 4],
+            out=en_bf[1][:].rearrange("p (n u t) -> p n t u", u=2, t=PACK)[:, : N // 8],
+            in_=en_raw[1][:].rearrange("p t (n u) -> p n t u", u=2)[:, : N // 8],
         )
         round_on_gpsimd(
-            en_bf[1][:].rearrange("p (n t) -> p n t", t=PACK)[:, N // 2 :],
-            en_raw[1][:].rearrange("p t n -> p n t")[:, N // 2 :],
+            en_bf[1][:].rearrange("p (n t) -> p n t", t=PACK)[:, N // 4 :],
+            en_raw[1][:].rearrange("p t n -> p n t")[:, N // 4 :],
         )
         h_early = buf("h_early", [P, DIRECT * BANK], BF16, "en_bf0")
         hb_late = buf("hb_late", [P, (CHUNKS - DIRECT) * BANK], BF16)

@@ -32,6 +32,7 @@ TAB_ROW, WA_ROW = 4, 8
 AHEAD = 4
 ALL = slice(None)
 DIRECT = 4
+HELD = 6
 
 
 def tile_list_kg_max_sig_kernel(
@@ -72,6 +73,7 @@ def tile_list_kg_max_sig_kernel(
             for a in range(2):
                 parts = 2 if (a, b) in ((1, 0),) else 1
                 names = ["wb_raw%d%d" % (a, b), "wb_right%d%d" % (a, b)]
+                place["end"] += 2 * BANK_BYTES
                 wb_raw[a, b] = [buf(names[h], [P, PACK, K_PASS // parts], F32) for h in range(parts)]
                 place["end"] += BANK_BYTES
         en_raw = [buf("en_raw%d" % b, [P, PACK, N], F32) for b in range(2)]
@@ -273,8 +275,8 @@ def tile_list_kg_max_sig_kernel(
         load_en(1)
 
         round_wb(0, 0, gpsimd=[(0, t) for t in range(PACK)])
-        for c in range(7):
-            make_ha(0, c, [0, 1, 2, 3, 0, 1, 3][c], buf("ha0%d" % c, [P, BANK], BF16)[:])
+        for c in range(CHUNKS):
+            make_ha(0, c, c if c < 4 else c % 2, buf("ha0%d" % c, [P, BANK], BF16)[:])
         g2_pair[0] = buf("g2_pair0", [P, HALF], U32)
         g2_pair[1] = buf("g2_pair1", [P, HALF], U32, room=2 * BANK_BYTES)
         gather_tab2(0, 0, HALF)
@@ -283,18 +285,16 @@ def tile_list_kg_max_sig_kernel(
         quantize_wb(0, 0, "tab2_w")
         order_wa_scales(1, "tab2_s")
         round_wb(1, 0, scalar=[(0, slice(0, 3)), (1, ALL)], gpsimd=[(0, 3)])
-        make_ha(0, 7, 1, buf("ha07", [P, BANK], BF16, "wb_raw10", 8 * BANK_BYTES - 64)[:])
-        ha_late = buf("ha_late", [P, (CHUNKS - DIRECT) * BANK], BF16, "wb_raw10", BANK_BYTES - 64)
-        for c in range(DIRECT, CHUNKS):
-            make_ha(1, c, c, chunks_of(ha_late, c - DIRECT))
-        make_ha(1, 0, 2, buf("ha10", [P, BANK], BF16, "wb_raw10", 7 * BANK_BYTES - 64)[:])
+        ha_held = buf("ha_held", [P, HELD * BANK], BF16, "wb_raw10", 64 - 2 * BANK_BYTES)
+        for c in range(HELD):
+            make_ha(1, c, 2 + c, chunks_of(ha_held, c))
         for c in range(2):
-            hb_pass(0, 0, c, 3 * c)
+            hb_pass(0, 0, c, c)
         quantize_wb(1, 0)
         part(1, "wb_raw10", 5 * BANK_BYTES - 64)
         round_wb(0, 1, "g2_pair1", scalar=[(0, slice(0, 1))], gpsimd=[(0, t) for t in range(1, PACK)])
         h_first = buf("h_first", [P, 6 * BANK], BF16)
-        first_bank = [0, 3, 1, 4, 5, 6, 7, 2]
+        first_bank = list(range(CHUNKS))
         for c in range(CHUNKS):
             if c >= 2:
                 hb_pass(1, 0, c, first_bank[c])
@@ -315,8 +315,8 @@ def tile_list_kg_max_sig_kernel(
             out=en_bf[0][:].rearrange("p (n u t) -> p n t u", u=2, t=PACK),
             in_=en_raw[0][:].rearrange("p t (n u) -> p n t u", u=2),
         )
-        for c in range(1, DIRECT):
-            make_ha(1, c, first_bank[c - 1], buf("ha1%d" % c, [P, BANK], BF16, "en_raw0", c * BANK_BYTES)[:])
+        for c in range(HELD, CHUNKS):
+            make_ha(1, c, c - HELD, buf("ha1%d" % c, [P, BANK], BF16, "en_raw0", (c - 5) * BANK_BYTES)[:])
         wb_w[1, 1] = buf("wb_w11", [P, K_PASS], U32, "wb_raw01", 4 * BANK_BYTES)
         quantize(wb_w[1, 1][:, : 3 * P], wb_s[1, 1][:, : 3 * P], wb_bf[1, 1][:, : 3 * K_PASS])
         quantize(wb_w[1, 1][:, 3 * P :], wb_s[1, 1][:, 3 * P :], last[:])
@@ -327,16 +327,16 @@ def tile_list_kg_max_sig_kernel(
         quantize_h(0, 4, 2, chunks_of(h_first, 4, 2))
         quantize(en_w[0][:], en_s[0][:], en_bf[0][:])
         quantize_h(0, 6, 2, h_last[:])
-        second_bank = [4, 5, 6, 7, 2, 0, 3, 1]
+        second_bank = [2, 3, 4, 5, 6, 7, 0, 1]
         for c in range(DIRECT):
             hb_pass(0, 1, c, second_bank[c])
         nc.scalar.copy(
-            out=en_bf[1][:].rearrange("p (n u t) -> p n t u", u=2, t=PACK)[:, : N // 8],
-            in_=en_raw[1][:].rearrange("p t (n u) -> p n t u", u=2)[:, : N // 8],
+            out=en_bf[1][:].rearrange("p (n u t) -> p n t u", u=2, t=PACK)[:, : N // 4],
+            in_=en_raw[1][:].rearrange("p t (n u) -> p n t u", u=2)[:, : N // 4],
         )
         round_on_gpsimd(
-            en_bf[1][:].rearrange("p (n t) -> p n t", t=PACK)[:, N // 4 :],
-            en_raw[1][:].rearrange("p t n -> p n t")[:, N // 4 :],
+            en_bf[1][:].rearrange("p (n t) -> p n t", t=PACK)[:, N // 2 :],
+            en_raw[1][:].rearrange("p t n -> p n t")[:, N // 2 :],
         )
         h_early = buf("h_early", [P, DIRECT * BANK], BF16, "en_bf0")
         hb_late = buf("hb_late", [P, (CHUNKS - DIRECT) * BANK], BF16)
@@ -349,8 +349,8 @@ def tile_list_kg_max_sig_kernel(
             nc.scalar.copy(out=by_query(chunks_of(hb_late, c - DIRECT)), in_=bank_by_query(hb_bank[1, c]))
 
         def late_maximum(c):
-            h_c, ha_c, hb_c = [chunks_of(tile, c - DIRECT) for tile in (h_late, ha_late, hb_late)]
-            nc.vector.tensor_tensor(out=h_c, in0=ha_c, in1=hb_c, op=MAX)
+            h_c, hb_c = [chunks_of(tile, c - DIRECT) for tile in (h_late, hb_late)]
+            nc.vector.tensor_tensor(out=h_c, in0=ha[1, c], in1=hb_c, op=MAX)
 
         for c in range(DIRECT):
             hb_pass(1, 1, c)

@@ -105,12 +105,12 @@ def tile_list_kg_max_sig_kernel(
             for t in range(PACK):
                 nc.sync.dma_start(out=en_raw[b][:, t, :], in_=rows[b, t])
 
-        def order_wa_scales(b, on=None):
-            wa_s[b] = buf("wa_s%d" % b, [P, K_PASS], U8, on)
-            nc.scalar.copy(
-                out=wa_s[b][:].bitcast(U32).rearrange("p (t m) -> p t m", t=PACK),
-                in_=wa_s_raw[:, b * K_PASS : (b + 1) * K_PASS].bitcast(U32).rearrange("p (m t) -> p t m", t=PACK),
-            )
+        def order_wa_scales(b, t0, t1, on=None):
+            ordered = buf("wa_s%d%d" % (b, t0), [P, (t1 - t0) * P], U8, on)
+            runs = wa_s_raw[:, b * K_PASS : (b + 1) * K_PASS].bitcast(U32).rearrange("p (m t) -> p t m", t=PACK)
+            nc.scalar.copy(out=ordered[:].bitcast(U32).rearrange("p (t m) -> p t m", t=t1 - t0), in_=runs[:, t0:t1])
+            for t in range(t0, t1):
+                wa_s[b, t] = ordered[WA_ROW:, (t - t0) * P : (t - t0 + 1) * P]
 
         def half_of(entries, h):
             return entries[:, h * HALF // 16 : (h + 1) * HALF // 16]
@@ -183,7 +183,7 @@ def tile_list_kg_max_sig_kernel(
                 nc.tensor.matmul_mx(
                     out=bank[:, t, :],
                     lhsT=wa_w[:, cols].bitcast(FP8X4),
-                    lhsT_scale=wa_s[b][WA_ROW:, t * P : (t + 1) * P],
+                    lhsT_scale=wa_s[b, t],
                     rhs=g_w[:, c * CHUNK : (c + 1) * CHUNK].bitcast(FP8X4),
                     rhs_scale=g_s[TAB_ROW:, c * CHUNK : (c + 1) * CHUNK],
                     start=True,
@@ -264,7 +264,8 @@ def tile_list_kg_max_sig_kernel(
                 out=wa_w[:, cols].bitcast(U32).rearrange("p (t m e) -> p t m e", t=PACK, e=RUN),
                 in_=wa_w_raw[:, cols].bitcast(U32).rearrange("p (m t e) -> p t m e", t=PACK, e=RUN),
             )
-        order_wa_scales(0)
+        order_wa_scales(0, 0, PACK)
+        order_wa_scales(1, 1, PACK)
         gather_tab2_scales(0)
         move_parked_rows(0)
         load_wb(0, 1)
@@ -283,7 +284,7 @@ def tile_list_kg_max_sig_kernel(
         gather_tab2(1, 0, HALF)
         part(0, None)
         quantize_wb(0, 0, "tab2_w")
-        order_wa_scales(1, "tab2_s")
+        order_wa_scales(1, 0, 1, "tab2_s")
         round_wb(1, 0, scalar=[(0, slice(0, 3)), (1, ALL)], gpsimd=[(0, 3)])
         ha_held = buf("ha_held", [P, HELD * BANK], BF16, "wb_raw10", 64 - 2 * BANK_BYTES)
         for c in range(HELD):
@@ -330,13 +331,8 @@ def tile_list_kg_max_sig_kernel(
         second_bank = [2, 3, 4, 5, 6, 7, 0, 1]
         for c in range(DIRECT):
             hb_pass(0, 1, c, second_bank[c])
-        nc.scalar.copy(
-            out=en_bf[1][:].rearrange("p (n u t) -> p n t u", u=2, t=PACK)[:, : N // 4],
-            in_=en_raw[1][:].rearrange("p t (n u) -> p n t u", u=2)[:, : N // 4],
-        )
         round_on_gpsimd(
-            en_bf[1][:].rearrange("p (n t) -> p n t", t=PACK)[:, N // 2 :],
-            en_raw[1][:].rearrange("p t n -> p n t")[:, N // 2 :],
+            en_bf[1][:].rearrange("p (n t) -> p n t", t=PACK), en_raw[1][:].rearrange("p t n -> p n t")
         )
         h_early = buf("h_early", [P, DIRECT * BANK], BF16, "en_bf0")
         hb_late = buf("hb_late", [P, (CHUNKS - DIRECT) * BANK], BF16)
@@ -354,7 +350,7 @@ def tile_list_kg_max_sig_kernel(
 
         for c in range(DIRECT):
             hb_pass(1, 1, c)
-        for c in range(DIRECT - 1):
+        for c in range(DIRECT):
             maximum(1, c, chunks_of(h_early, c))
         late_bank(4)
         late_bank(5)
@@ -363,7 +359,6 @@ def tile_list_kg_max_sig_kernel(
         quantize(en_w[1][:], en_s[1][:], en_bf[1][:])
         finish(0, 2, chunks_of(h_early, 0, 2), nc.sync)
         late_bank(7)
-        maximum(1, 3, chunks_of(h_early, 3))
         late_maximum(4)
         score_pass(0, 2, 2, second_bank[1])
         finish(2, 2, chunks_of(h_early, 2, 2), nc.sync)

@@ -275,7 +275,7 @@ def tile_list_kg_max_sig_kernel(
         load_en(0)
         load_en(1)
 
-        round_wb(0, 0, gpsimd=[(0, t) for t in range(PACK)])
+        round_wb(0, 0, gpsimd=[(0, t) for t in range(PACK - 1)])
         for c in range(CHUNKS):
             make_ha(0, c, c if c < 4 else c % 2, buf("ha0%d" % c, [P, BANK], BF16)[:])
         g2_pair[0] = buf("g2_pair0", [P, HALF], U32)
@@ -283,7 +283,14 @@ def tile_list_kg_max_sig_kernel(
         gather_tab2(0, 0, HALF)
         gather_tab2(1, 0, HALF)
         part(0, None)
-        quantize_wb(0, 0, "tab2_w")
+        fourth = buf("wb_fourth00", [P, K_PASS], BF16, "tab2_w", 2 * BANK_BYTES)
+        nc.vector.tensor_copy(
+            out=fourth[:].rearrange("p (m e i) -> p m i e", e=RUN, i=PACK),
+            in_=wb_raw[0, 0][0][:].rearrange("p i (m t e) -> p t m i e", t=PACK, e=RUN)[:, 3],
+        )
+        wb_w[0, 0] = buf("wb_w00", [P, K_PASS], U32, "tab2_w")
+        quantize(wb_w[0, 0][:, : 3 * P], wb_s[0, 0][:, : 3 * P], wb_bf[0, 0][:, : 3 * K_PASS])
+        quantize(wb_w[0, 0][:, 3 * P :], wb_s[0, 0][:, 3 * P :], fourth[:])
         order_wa_scales(1, 0, 1, "tab2_s")
         round_wb(1, 0, scalar=[(0, slice(0, 3)), (1, ALL)], gpsimd=[(0, 3)])
         ha_held = buf("ha_held", [P, HELD * BANK], BF16, "wb_raw10", 64 - 2 * BANK_BYTES)
@@ -331,8 +338,13 @@ def tile_list_kg_max_sig_kernel(
         second_bank = [2, 3, 4, 5, 6, 7, 0, 1]
         for c in range(DIRECT):
             hb_pass(0, 1, c, second_bank[c])
+        nc.scalar.copy(
+            out=en_bf[1][:].rearrange("p (n u t) -> p n t u", u=2, t=PACK)[:, : N // 8],
+            in_=en_raw[1][:].rearrange("p t (n u) -> p n t u", u=2)[:, : N // 8],
+        )
         round_on_gpsimd(
-            en_bf[1][:].rearrange("p (n t) -> p n t", t=PACK), en_raw[1][:].rearrange("p t n -> p n t")
+            en_bf[1][:].rearrange("p (n t) -> p n t", t=PACK)[:, N // 4 :],
+            en_raw[1][:].rearrange("p t n -> p n t")[:, N // 4 :],
         )
         h_early = buf("h_early", [P, DIRECT * BANK], BF16, "en_bf0")
         hb_late = buf("hb_late", [P, (CHUNKS - DIRECT) * BANK], BF16)

@@ -152,6 +152,13 @@ def tile_list_kg_max_sig_kernel(
             for h, slots in vector:
                 nc.vector.tensor_copy(out=dst[:, h, slots], in_=src[h][:, slots])
 
+        def round_halved(values, raw):
+            dst = values.rearrange("p (s m e i) -> p s m i e", s=2, e=RUN, i=PACK)
+            src = raw[:].rearrange("p i (s m t e) -> p t s m i e", s=2, t=PACK, e=RUN)[:, 3]
+            round_on_gpsimd(*[side[:, 0].rearrange("p m i e -> p m e i") for side in (dst, src)])
+            pairs = [side[:, 1].rearrange("p m i (e u) -> p m e i u", u=2) for side in (dst, src)]
+            nc.scalar.copy(out=pairs[0], in_=pairs[1])
+
         def quantize(codes, scales, values):
             nc.vector.quantize_mx(out=codes.bitcast(FP8X4), scales=scales, in_=values)
 
@@ -275,7 +282,7 @@ def tile_list_kg_max_sig_kernel(
         load_en(0)
         load_en(1)
 
-        round_wb(0, 0, gpsimd=[(0, t) for t in range(PACK - 1)])
+        round_wb(0, 0, gpsimd=[(0, t) for t in range(PACK)])
         for c in range(CHUNKS):
             make_ha(0, c, c if c < 4 else c % 2, buf("ha0%d" % c, [P, BANK], BF16)[:])
         g2_pair[0] = buf("g2_pair0", [P, HALF], U32)
@@ -283,14 +290,7 @@ def tile_list_kg_max_sig_kernel(
         gather_tab2(0, 0, HALF)
         gather_tab2(1, 0, HALF)
         part(0, None)
-        fourth = buf("wb_fourth00", [P, K_PASS], BF16, "tab2_w", 2 * BANK_BYTES)
-        nc.vector.tensor_copy(
-            out=fourth[:].rearrange("p (m e i) -> p m i e", e=RUN, i=PACK),
-            in_=wb_raw[0, 0][0][:].rearrange("p i (m t e) -> p t m i e", t=PACK, e=RUN)[:, 3],
-        )
-        wb_w[0, 0] = buf("wb_w00", [P, K_PASS], U32, "tab2_w")
-        quantize(wb_w[0, 0][:, : 3 * P], wb_s[0, 0][:, : 3 * P], wb_bf[0, 0][:, : 3 * K_PASS])
-        quantize(wb_w[0, 0][:, 3 * P :], wb_s[0, 0][:, 3 * P :], fourth[:])
+        quantize_wb(0, 0, "tab2_w")
         order_wa_scales(1, 0, 1, "tab2_s")
         round_wb(1, 0, scalar=[(0, slice(0, 3)), (1, ALL)], gpsimd=[(0, 3)])
         ha_held = buf("ha_held", [P, HELD * BANK], BF16, "wb_raw10", 64 - 2 * BANK_BYTES)
@@ -300,7 +300,8 @@ def tile_list_kg_max_sig_kernel(
             hb_pass(0, 0, c, c)
         quantize_wb(1, 0)
         part(1, "wb_raw10", 5 * BANK_BYTES - 64)
-        round_wb(0, 1, "g2_pair1", scalar=[(0, slice(0, 1))], gpsimd=[(0, t) for t in range(1, PACK)])
+        round_wb(0, 1, "g2_pair1", scalar=[(0, slice(0, 1))], gpsimd=[(0, 1), (0, 2)])
+        round_halved(wb_bf[0, 1][:, 3 * K_PASS :], wb_raw[0, 1][0])
         h_first = buf("h_first", [P, 6 * BANK], BF16)
         first_bank = list(range(CHUNKS))
         for c in range(CHUNKS):
@@ -314,10 +315,7 @@ def tile_list_kg_max_sig_kernel(
             if c == AHEAD - 1:
                 round_wb(1, 1, scalar=[(0, slice(0, 3))])
         last = buf("wb_last11", [P, K_PASS], BF16, "wb_bf01")
-        round_on_gpsimd(
-            last[:].rearrange("p (m e i) -> p m e i", e=RUN, i=PACK),
-            wb_raw[1, 1][0][:].rearrange("p i (m t e) -> p t m e i", t=PACK, e=RUN)[:, 3],
-        )
+        round_halved(last[:], wb_raw[1, 1][0])
         en_bf = [buf("en_bf0", [P, N * PACK], BF16, room=2 * BANK_BYTES), buf("en_bf1", [P, N * PACK], BF16, "h_last")]
         nc.scalar.copy(
             out=en_bf[0][:].rearrange("p (n u t) -> p n t u", u=2, t=PACK),

import math
from contextlib import ExitStack

import concourse.mybir as mybir

K, L, R, N, T, J = 512, 1024, 1024, 256, 2048, 1024
FLOPS = 2 * (K * R * J + L * R * J + R * N * J)

F32 = mybir.dt.float32
BF16 = mybir.dt.bfloat16
I32 = mybir.dt.int32
U32 = mybir.dt.uint32
U16 = mybir.dt.uint16
U8 = mybir.dt.uint8
FP8X4 = mybir.dt.float8_e4m3fn_x4
FP4X4 = mybir.dt.float4_e2m1fn_x4
MULT, ADD, MAX = mybir.AluOpType.mult, mybir.AluOpType.add, mybir.AluOpType.max
SIGMOID = mybir.ActivationFunctionType.Sigmoid
BYTES_OF = {F32: 4, I32: 4, U32: 4, BF16: 2, U8: 1}

P = 128
PACK = 4
RUN = 4
K_PASS = P * PACK
HALF = J // 2
CHUNK = 128
CHUNKS = J // CHUNK
BANK = CHUNK * PACK
BANK_BYTES = 2 * BANK
PARKED = 16
TAB_ROW, WA_ROW = 4, 8
AHEAD = 4
ALL = slice(None)
DIRECT = 4
HELD = 6


def tile_list_kg_max_sig_kernel(
    tc, tab_words, tab_scales, tab2_words, tab2_scales, wa_words, wa_scales, wb, en, offs, offs2, out
):
    nc = tc.nc
    with ExitStack() as ctx:
        keep = ctx.enter_context(tc.tile_pool(name="keep", bufs=1))
        psum = ctx.enter_context(tc.psum_pool(name="psum", bufs=1))
        lists = ctx.enter_context(tc.tile_pool(name="lists", bufs=1))
        place = {"end": 0}

        def buf(name, shape, dtype, on=None, shift=0, room=0):
            if on is None:
                place[name] = place["end"] + room
                place["end"] = place[name] + math.prod(shape[1:]) * BYTES_OF[dtype] + room
            else:
                place[name] = place[on] + shift
            return keep.tile(shape, dtype, name=name, align_bytes=64, offset=place[name])

        list1 = lists.tile([P, J // 16], U16, name="list1")
        list2 = lists.tile([P, J // 16], U16, name="list2")
        warm = lists.tile([P, 2], F32, name="warm")
        tab_s = buf("tab_s", [P, T], U8)
        tab2_s = buf("tab2_s", [P, T], U8)
        wa_s_raw = buf("wa_s_raw", [P, R], U8)
        tab_w = buf("tab_w", [P, T], I32)
        tab2_w = buf("tab2_w", [P, T], I32)
        wa_w_raw = buf("wa_w_raw", [P, R], I32)
        wa_w = buf("wa_w", [P, R], I32)
        wa_s = {}
        g_s = buf("g_s", [P, J], U8)
        g_w = buf("g_w", [P, J], U32)
        g2_s = [buf("g2_s%d" % a, [P, J], U8) for a in range(2)]
        wb_s = {(a, b): buf("wb_s%d%d" % (a, b), [P, K_PASS], U8) for b in range(2) for a in range(2)}
        wb_raw = {}
        for b in range(2):
            for a in range(2):
                parts = 2 if (a, b) in ((1, 0),) else 1
                names = ["wb_raw%d%d" % (a, b), "wb_right%d%d" % (a, b)]
                place["end"] += 2 * BANK_BYTES
                wb_raw[a, b] = [buf(names[h], [P, PACK, K_PASS // parts], F32) for h in range(parts)]
                place["end"] += BANK_BYTES
        en_raw = [buf("en_raw%d" % b, [P, PACK, N], F32) for b in range(2)]
        en_s = [buf("en_s%d" % b, [P, N], U8) for b in range(2)]
        h_s = [buf("h_s%d" % b, [P, J], U8) for b in range(2)]
        wb_bf, wb_w, g2_pair, g2_w, h_w, ha, hb_bank, y_bank = [{} for unused in range(8)]

        def load_scale_rows(queues, plane, first, rows):
            by_row = rows.bitcast(I32).rearrange("(q s) c -> s q c", s=4)
            for s in range(4):
                queues[s].dma_start(out=plane[first + s : P : 32, :].bitcast(I32), in_=by_row[s])

        def load_tab2_scales(queues):
            rows = tab2_scales.bitcast(I32).rearrange("a (q s) c -> s q a c", s=4)
            for s in range(4):
                queues[s].dma_start(out=tab2_s[s:P:PARKED, :].bitcast(I32), in_=rows[s])

        def as_words(packed):
            return packed[0].rearrange("p c i -> p (c i)").bitcast(I32)

        def load_wb(a, b, h=0):
            width = K_PASS // len(wb_raw[a, b])
            c0 = b * K_PASS + h * width
            rows = wb[a * K_PASS : (a + 1) * K_PASS, c0 : c0 + width]
            nc.sync.dma_start(out=wb_raw[a, b][h][:], in_=rows.rearrange("(p i) r -> p i r", i=PACK))

        def load_en(b):
            rows = en.rearrange("(b m t e) n -> b t m e n", b=2, t=PACK, e=RUN)
            for t in range(PACK):
                nc.sync.dma_start(out=en_raw[b][:, t, :], in_=rows[b, t])

        def order_wa_scales(b, t0, t1, on=None):
            ordered = buf("wa_s%d%d" % (b, t0), [P, (t1 - t0) * P], U8, on)
            runs = wa_s_raw[:, b * K_PASS : (b + 1) * K_PASS].bitcast(U32).rearrange("p (m t) -> p t m", t=PACK)
            nc.scalar.copy(out=ordered[:].bitcast(U32).rearrange("p (t m) -> p t m", t=t1 - t0), in_=runs[:, t0:t1])
            for t in range(t0, t1):
                wa_s[b, t] = ordered[WA_ROW:, (t - t0) * P : (t - t0 + 1) * P]

        def half_of(entries, h):
            return entries[:, h * HALF // 16 : (h + 1) * HALF // 16]

        def gather_tab2_scales(h):
            cols = slice(h * HALF, (h + 1) * HALF)
            nc.vector.tensor_copy(g2_s[0][:, cols], tab2_s[:].indirect(half_of(list2, h)))

        def move_parked_rows(h):
            cols = slice(h * HALF, (h + 1) * HALF)
            nc.sync.dma_start(out=g2_s[1][: P - PARKED, cols].bitcast(I32), in_=g2_s[0][PARKED:, cols].bitcast(I32))

        def gather_tab2(h, j0, count):
            first = (h * HALF + j0) // 16
            entries = list2[:, first : first + count // 16]
            nc.vector.tensor_copy(g2_pair[h][:, j0 : j0 + count], tab2_w[:].bitcast(U32).indirect(entries))

        def part(h, on, shift=0):
            g2_w[h] = buf("g2_w%d" % h, [P, 2, 2 * HALF], U8, on, shift)
            nc.vector.tensor_copy(
                out=g2_w[h][:].bitcast(U16),
                in_=g2_pair[h][:].bitcast(U16).rearrange("p (j d) -> p d j", d=2),
            )

        def round_on_gpsimd(dst, src):
            nc.gpsimd.tensor_scalar(out=dst, in0=src, scalar1=1.0, scalar2=0.0, op0=MULT, op1=ADD)

        def round_wb(a, b, on=None, scalar=(), gpsimd=(), vector=()):
            wb_bf[a, b] = buf("wb_bf%d%d" % (a, b), [P, PACK * K_PASS], BF16, on)
            parts = len(wb_raw[a, b])
            dst = wb_bf[a, b][:].rearrange("p (t h m e i) -> p h t m i e", t=PACK, h=parts, e=RUN, i=PACK)
            src = [raw[:].rearrange("p i (m t e) -> p t m i e", t=PACK, e=RUN) for raw in wb_raw[a, b]]
            for h, t in gpsimd:
                round_on_gpsimd(*[side[:, t].rearrange("p m i e -> p m e i") for side in (dst[:, h], src[h])])
            for h, slots in scalar:
                for t in range(PACK)[slots]:
                    pairs = [side[:, t].rearrange("p m i (e u) -> p m e i u", u=2) for side in (dst[:, h], src[h])]
                    nc.scalar.copy(out=pairs[0], in_=pairs[1])
            for h, slots in vector:
                nc.vector.tensor_copy(out=dst[:, h, slots], in_=src[h][:, slots])

        def round_halved(values, raw):
            dst = values.rearrange("p (s m e i) -> p s m i e", s=2, e=RUN, i=PACK)
            src = raw[:].rearrange("p i (s m t e) -> p t s m i e", s=2, t=PACK, e=RUN)[:, 3]
            round_on_gpsimd(*[side[:, 0].rearrange("p m i e -> p m e i") for side in (dst, src)])
            pairs = [side[:, 1].rearrange("p m i (e u) -> p m e i u", u=2) for side in (dst, src)]
            nc.scalar.copy(out=pairs[0], in_=pairs[1])

        def quantize(codes, scales, values):
            nc.vector.quantize_mx(out=codes.bitcast(FP8X4), scales=scales, in_=values)

        def quantize_wb(a, b, on=None, shift=0):
            wb_w[a, b] = buf("wb_w%d%d" % (a, b), [P, K_PASS], U32, on, shift)
            quantize(wb_w[a, b][:], wb_s[a, b][:], wb_bf[a, b][:])

        def h_codes(b, c0, count):
            first = max(c for half, c in h_w if half == b and c <= c0)
            return h_w[b, first][:, (c0 - first) * CHUNK : (c0 - first + count) * CHUNK]

        def quantize_h(b, c0, count, values):
            cols = slice(c0 * CHUNK, (c0 + count) * CHUNK)
            quantize(h_codes(b, c0, count), h_s[b][:, cols], values)

        def by_query(values):
            return values.rearrange("p (j t) -> p j t", t=PACK)

        def bank_by_query(bank):
            return bank[:].rearrange("p t j -> p j t")

        def chunks_of(tile, s, count=1):
            return tile[:, s * BANK : (s + count) * BANK]

        def make_ha(b, c, k, values):
            bank = psum.tile([P, PACK, CHUNK], F32, name="bank_a", tag="bank%d" % k)
            for t in range(PACK):
                cols = slice(b * K_PASS + t * P, b * K_PASS + (t + 1) * P)
                nc.tensor.matmul_mx(
                    out=bank[:, t, :],
                    lhsT=wa_w[:, cols].bitcast(FP8X4),
                    lhsT_scale=wa_s[b, t],
                    rhs=g_w[:, c * CHUNK : (c + 1) * CHUNK].bitcast(FP8X4),
                    rhs_scale=g_s[TAB_ROW:, c * CHUNK : (c + 1) * CHUNK],
                    start=True,
                    stop=True,
                )
            ha[b, c] = values
            nc.scalar.copy(out=by_query(values), in_=bank_by_query(bank))

        def hb_pass(a, b, c, k=None):
            h, j0 = divmod(c * CHUNK, HALF)
            opens = k is not None
            if opens:
                hb_bank[b, c] = psum.tile([P, PACK, CHUNK], F32, name="bank_b", tag="bank%d" % k)
            for t in range(PACK):
                nc.tensor.matmul_mx(
                    out=hb_bank[b, c][:, t, :],
                    lhsT=wb_w[a, b][:, t * P : (t + 1) * P].bitcast(FP8X4),
                    lhsT_scale=wb_s[a, b][:, t * P : (t + 1) * P],
                    rhs=g2_w[h][:, a, 2 * j0 : 2 * (j0 + CHUNK)].bitcast(FP4X4),
                    rhs_scale=g2_s[a][:, c * CHUNK : (c + 1) * CHUNK],
                    start=(opens and t == 0),
                    stop=(not opens and t == PACK - 1),
                )

        def maximum(b, c, values):
            nc.vector.tensor_tensor(
                out=by_query(values), in0=bank_by_query(hb_bank[b, c]), in1=by_query(ha[b, c]), op=MAX
            )

        def score_pass(b, c0, count, k=None):
            queries = slice(c0 * CHUNK, (c0 + count) * CHUNK)
            if b == 0:
                y_bank[c0] = psum.tile([P, N // P, count * CHUNK], F32, name="bank_y", tag="bank%d" % k)
            for m in range(N // P):
                cols = slice(m * P, (m + 1) * P)
                nc.tensor.matmul_mx(
                    out=y_bank[c0][:, m, :],
                    lhsT=en_w[b][:, cols].bitcast(FP8X4),
                    lhsT_scale=en_s[b][:, cols],
                    rhs=h_codes(b, c0, count).bitcast(FP8X4),
                    rhs_scale=h_s[b][:, queries],
                    start=(b == 0 and m == 0),
                    stop=(b == 1 and m == N // P - 1),
                )

        def finish(c0, count, values, queue):
            quantize_h(1, c0, count, values)
            score_pass(1, c0, count)
            queries = slice(c0 * CHUNK, (c0 + count) * CHUNK)
            result = buf("result%d" % c0, [P, N // P, count * CHUNK], F32)
            nc.scalar.activation(out=result[:], in_=y_bank[c0][:], func=SIGMOID)
            queue.dma_start(out=out[:, queries].rearrange("(m p) j -> p m j", p=P), in_=result[:])

        nc.gpsimd.memset(tab_s[:].bitcast(I32), 0)
        nc.vector.memset(warm[:, 0:1], 0.0)
        nc.vector.memset(wa_s_raw[:].bitcast(I32), 0)
        nc.gpsimd.memset(tab2_s[:].bitcast(I32), 0)
        nc.vector.memset(g2_s[1][:].bitcast(I32), 0)
        nc.scalar.activation(out=warm[:, 1:2], in_=warm[:, 0:1], func=SIGMOID)

        nc.sync.dma_start(list1[:], offs)
        nc.sync.dma_start(out=wa_w_raw[:], in_=as_words(wa_words))
        load_scale_rows([nc.sync] * 4, tab_s, TAB_ROW, tab_scales[0])
        nc.sync.dma_start(out=tab_w[:], in_=as_words(tab_words))
        load_scale_rows([nc.sync] * 3 + [nc.gpsimd], wa_s_raw, WA_ROW, wa_scales[0])
        load_wb(0, 0)
        nc.sync.dma_start(list2[:], offs2)
        load_tab2_scales([nc.sync] * 3 + [nc.gpsimd])
        nc.sync.dma_start(out=tab2_w[:], in_=as_words(tab2_words))
        load_wb(1, 0, 0)
        load_wb(1, 0, 1)
        nc.vector.tensor_copy(g_s[:], tab_s[:].indirect(list1[:]))
        for j0, j1 in ((0, J // 4), (J // 4, HALF), (HALF, J)):
            nc.vector.tensor_copy(g_w[:, j0:j1], tab_w[:].bitcast(U32).indirect(list1[:, j0 // 16 : j1 // 16]))
        for b in range(2):
            cols = slice(b * K_PASS, (b + 1) * K_PASS)
            nc.scalar.copy(
                out=wa_w[:, cols].bitcast(U32).rearrange("p (t m e) -> p t m e", t=PACK, e=RUN),
                in_=wa_w_raw[:, cols].bitcast(U32).rearrange("p (m t e) -> p t m e", t=PACK, e=RUN),
            )
        order_wa_scales(0, 0, PACK)
        order_wa_scales(1, 1, PACK)
        gather_tab2_scales(0)
        move_parked_rows(0)
        load_wb(0, 1)
        gather_tab2_scales(1)
        move_parked_rows(1)
        load_wb(1, 1)
        load_en(0)
        load_en(1)

        round_wb(0, 0, gpsimd=[(0, t) for t in range(PACK)])
        for c in range(CHUNKS):
            make_ha(0, c, c if c < 4 else c % 2, buf("ha0%d" % c, [P, BANK], BF16)[:])
        g2_pair[0] = buf("g2_pair0", [P, HALF], U32)
        g2_pair[1] = buf("g2_pair1", [P, HALF], U32, room=2 * BANK_BYTES)
        gather_tab2(0, 0, HALF)
        gather_tab2(1, 0, HALF)
        part(0, None)
        quantize_wb(0, 0, "tab2_w")
        order_wa_scales(1, 0, 1, "tab2_s")
        round_wb(1, 0, scalar=[(0, slice(0, 3)), (1, ALL)], gpsimd=[(0, 3)])
        ha_held = buf("ha_held", [P, HELD * BANK], BF16, "wb_raw10", 64 - 2 * BANK_BYTES)
        for c in range(HELD):
            make_ha(1, c, 2 + c, chunks_of(ha_held, c))
        for c in range(2):
            hb_pass(0, 0, c, c)
        quantize_wb(1, 0)
        part(1, "wb_raw10", 5 * BANK_BYTES - 64)
        round_wb(0, 1, "g2_pair1", scalar=[(0, slice(0, 1))], gpsimd=[(0, 1), (0, 2)])
        round_halved(wb_bf[0, 1][:, 3 * K_PASS :], wb_raw[0, 1][0])
        h_first = buf("h_first", [P, 6 * BANK], BF16)
        first_bank = list(range(CHUNKS))
        for c in range(CHUNKS):
            if c >= 2:
                hb_pass(1, 0, c, first_bank[c])
            hb_pass(1 if c < 2 else 0, 0, c)
            if c == 6:
                quantize_wb(0, 1)
                h_last = buf("h_last", [P, 2 * BANK], BF16, "wb_raw01")
            maximum(0, c, chunks_of(h_first, c) if c < 6 else chunks_of(h_last, c - 6))
            if c == AHEAD - 1:
                round_wb(1, 1, scalar=[(0, slice(0, 3))])
        last = buf("wb_last11", [P, K_PASS], BF16, "wb_bf01")
        round_halved(last[:], wb_raw[1, 1][0])
        en_bf = [buf("en_bf0", [P, N * PACK], BF16, room=2 * BANK_BYTES), buf("en_bf1", [P, N * PACK], BF16, "h_last")]
        nc.scalar.copy(
            out=en_bf[0][:].rearrange("p (n u t) -> p n t u", u=2, t=PACK),
            in_=en_raw[0][:].rearrange("p t (n u) -> p n t u", u=2),
        )
        for c in range(HELD, CHUNKS):
            make_ha(1, c, c - HELD, buf("ha1%d" % c, [P, BANK], BF16, "en_raw0", (c - 5) * BANK_BYTES)[:])
        wb_w[1, 1] = buf("wb_w11", [P, K_PASS], U32, "wb_raw01", 4 * BANK_BYTES)
        quantize(wb_w[1, 1][:, : 3 * P], wb_s[1, 1][:, : 3 * P], wb_bf[1, 1][:, : 3 * K_PASS])
        quantize(wb_w[1, 1][:, 3 * P :], wb_s[1, 1][:, 3 * P :], last[:])
        h_w[0, 0] = buf("h_w0", [P, 6 * CHUNK], U32, "wb_raw11", 4 * BANK_BYTES)
        h_w[0, 6] = buf("h_w0_last", [P, 2 * CHUNK], U32, "en_raw0")
        en_w = [buf("en_w%d" % b, [P, N], U32) for b in range(2)]
        quantize_h(0, 0, 4, chunks_of(h_first, 0, 4))
        quantize_h(0, 4, 2, chunks_of(h_first, 4, 2))
        quantize(en_w[0][:], en_s[0][:], en_bf[0][:])
        quantize_h(0, 6, 2, h_last[:])
        second_bank = [2, 3, 4, 5, 6, 7, 0, 1]
        for c in range(DIRECT):
            hb_pass(0, 1, c, second_bank[c])
        nc.scalar.copy(
            out=en_bf[1][:].rearrange("p (n u t) -> p n t u", u=2, t=PACK)[:, : N // 8],
            in_=en_raw[1][:].rearrange("p t (n u) -> p n t u", u=2)[:, : N // 8],
        )
        round_on_gpsimd(
            en_bf[1][:].rearrange("p (n t) -> p n t", t=PACK)[:, N // 4 :],
            en_raw[1][:].rearrange("p t n -> p n t")[:, N // 4 :],
        )
        h_early = buf("h_early", [P, DIRECT * BANK], BF16, "en_bf0")
        hb_late = buf("hb_late", [P, (CHUNKS - DIRECT) * BANK], BF16)
        h_late = buf("h_late", [P, (CHUNKS - DIRECT) * BANK], BF16, "en_bf1")
        h_w[1, 0] = buf("h_w1", [P, J], U32, "en_raw1")

        def late_bank(c):
            hb_pass(0, 1, c, second_bank[c])
            hb_pass(1, 1, c)
            nc.scalar.copy(out=by_query(chunks_of(hb_late, c - DIRECT)), in_=bank_by_query(hb_bank[1, c]))

        def late_maximum(c):
            h_c, hb_c = [chunks_of(tile, c - DIRECT) for tile in (h_late, hb_late)]
            nc.vector.tensor_tensor(out=h_c, in0=ha[1, c], in1=hb_c, op=MAX)

        for c in range(DIRECT):
            hb_pass(1, 1, c)
        for c in range(DIRECT):
            maximum(1, c, chunks_of(h_early, c))
        late_bank(4)
        late_bank(5)
        score_pass(0, 0, 2, second_bank[0])
        late_bank(6)
        quantize(en_w[1][:], en_s[1][:], en_bf[1][:])
        finish(0, 2, chunks_of(h_early, 0, 2), nc.sync)
        late_bank(7)
        late_maximum(4)
        score_pass(0, 2, 2, second_bank[1])
        finish(2, 2, chunks_of(h_early, 2, 2), nc.sync)
        for c in range(DIRECT, CHUNKS):
            score_pass(0, c, 1, second_bank[c - 2])
        for c in range(DIRECT, CHUNKS):
            if c + 1 < CHUNKS:
                late_maximum(c + 1)
            finish(c, 1, chunks_of(h_late, c - DIRECT), nc.sync if c + 1 < CHUNKS else nc.scalar)
